import numpy as np
import ml_dtypes


def mxq(x, axis, fmt="e4m3"):
    dtype, down = {"e4m3": (ml_dtypes.float8_e4m3fn, 7), "e5m2": (ml_dtypes.float8_e5m2, 14)}[fmt]
    v = np.moveaxis(np.asarray(x, np.float32).astype(ml_dtypes.bfloat16).astype(np.float64), axis, -1)
    blocks = v.reshape(v.shape[:-1] + (-1, 32))
    amax = np.abs(blocks).max(-1, keepdims=True)
    byte = np.maximum(np.where(amax > 0, np.frexp(amax)[1] - 1 + 127, 0) - down, 1)
    scale = np.exp2(byte - 127.0)
    codes = (blocks / scale).astype(np.float32).astype(dtype).astype(np.float64)
    return np.moveaxis((codes * scale).reshape(v.shape), -1, axis)


WIDE = False


def mx_kscale(k):
    if not WIDE:
        return np.ones(k)
    levels = np.array([24, -24, 12, -12, 0])
    if k % 512:
        return np.exp2(np.random.permutation(np.resize(levels, k // 32))).repeat(32)
    a = np.empty((k // 512, 16))
    for p in range(k // 512):
        a[p, :8] = np.random.permutation(np.resize(levels, 8))
        for g in range(8):
            far = levels[np.abs(levels - a[p, g]) >= 10]
            a[p, g + 8] = far[np.random.randint(len(far))]
    return np.exp2(a.ravel()).repeat(32)


def f64(x):
    return np.asarray(x).astype(np.float64)


def striped(idx):
    return np.tile(idx.reshape(-1, 16).T, (8, 1)).astype(np.uint16)


def unstriped(offs):
    return offs[:16].T.reshape(-1).astype(np.int64)


E2M1 = np.array([0.0, 0.5, 1.0, 1.5, 2.0, 3.0, 4.0, 6.0, -0.0, -0.5, -1.0, -1.5, -2.0, -3.0, -4.0, -6.0])


def pack_weight(w, fmt):
    k, n = w.shape
    w = f64(np.asarray(w, np.float32).astype(ml_dtypes.bfloat16)).reshape(k // 32, 32, n)
    amax = np.abs(w).max(1)
    if fmt == "e4m3":
        byte = np.frexp(amax)[1] - 1 + 127 - 7
    else:
        mant, ex = np.frexp(amax / 6.0)
        byte = np.where(mant > 0.5, ex, ex - 1) + 127
    byte = np.clip(np.where(amax > 0, byte, 1), 1, 254)
    scaled = (w * np.exp2(127.0 - byte)[:, None, :]).reshape(k, n).astype(np.float32)
    by_word = np.ascontiguousarray(scaled.reshape(k // 512, 128, 4, n).transpose(0, 1, 3, 2))
    if fmt == "e4m3":
        words = by_word.astype(ml_dtypes.float8_e4m3fn).view(np.uint8)
    else:
        c = by_word.astype(ml_dtypes.float4_e2m1fn).view(np.uint8) & 0xF
        words = (c[..., 0::2] | (c[..., 1::2] << 4)).reshape(k // 512, 128, 2 * n)
    return np.ascontiguousarray(words), np.ascontiguousarray(byte.astype(np.uint8).reshape(k // 512, 16, n))


def unpack_weight(words, scales, fmt):
    g, _, n = scales.shape
    words = np.ascontiguousarray(words).reshape(g, 128, n, -1)
    if fmt == "e4m3":
        vals = words.view(ml_dtypes.float8_e4m3fn).astype(np.float64)
    else:
        nib = np.empty((g, 128, n, 4), np.uint8)
        nib[..., 0::2] = words & 0xF
        nib[..., 1::2] = words >> 4
        vals = E2M1[nib]
    vals = vals * np.repeat(np.exp2(scales.astype(np.float64) - 127.0), 8, axis=1)[..., None]
    return vals.transpose(0, 1, 3, 2).reshape(g * 512, n)


def pack_table4(v):
    words, scales = pack_weight(v, "e2m1")
    g, t = words.shape[0] // 2, v.shape[1]
    return np.ascontiguousarray(words.reshape(g, 2, 128, t, 2).transpose(0, 2, 3, 1, 4).reshape(g, 128, t, 4)), scales


def unpack_table4(words, scales):
    g, _, t, _ = words.shape
    return unpack_weight(words.reshape(g, 128, t, 2, 2).transpose(0, 3, 1, 2, 4).reshape(2 * g, 128, 2 * t), scales, "e2m1")


def planes(y):
    n, m = y.shape
    v = y.astype(np.float32).astype(ml_dtypes.bfloat16).astype(np.float64).reshape(n // 32, 32, m)
    top = np.abs(v).max(1)
    byte = np.clip(np.where(top > 0, np.frexp(top)[1] - 1 + 127 - 7, 1), 1, 254)
    codes = (v * np.exp2(127.0 - byte)[:, None, :]).reshape(n, m).astype(np.float32).astype(ml_dtypes.float8_e4m3fn).view(np.uint8)
    words = codes.reshape(n // 512, 128, 4, m).transpose(0, 1, 3, 2)
    return np.ascontiguousarray(words), np.ascontiguousarray(byte.astype(np.uint8).reshape(n // 512, 16, m))


def sigm(f):
    return 1.0 / (1.0 + np.exp(-np.maximum(f, -700.0)))


K, L, N, T, J = 512, 1024, 512, 2048, 1024


def setup_inputs():
    n = np.random.standard_normal
    s = mx_kscale(K)[:, None]
    s2 = mx_kscale(L)[:, None]
    p_tab = pack_weight(n((K, T)) * s, "e4m3")
    p_tab2 = pack_table4(n((L, T)) * s2)
    p_zv = pack_weight(n((K, N)) / np.sqrt(K) / s, "e2m1")
    p_zt = pack_weight(n((L, N)) / np.sqrt(L) / s2, "e2m1")
    p_wt = pack_weight(n((L, N)) / np.sqrt(L) / s2, "e2m1")
    return {
        "tab_words": p_tab[0],
        "tab_scales": p_tab[1],
        "tab2_words": p_tab2[0],
        "tab2_scales": p_tab2[1],
        "zv_words": p_zv[0],
        "zv_scales": p_zv[1],
        "zt_words": p_zt[0],
        "zt_scales": p_zt[1],
        "b": (0.3 * n(N)).astype(np.float32),
        "wv": (n((K, N)) / np.sqrt(K) / s).astype(np.float32),
        "wt_words": p_wt[0],
        "wt_scales": p_wt[1],
        "wgo": np.tile(np.random.uniform(0.5, 2.0, J), (128, 1)).astype(np.float32),
        "offs": striped(np.random.permutation(T)[:J]),
        "offs2": striped(np.random.permutation(T)[:J]),
    }


def reference(tab_words, tab_scales, tab2_words, tab2_scales, zv_words, zv_scales, zt_words, zt_scales, b, wv, wt_words, wt_scales, wgo, offs, offs2):
    idx = unstriped(offs)
    idx2 = unstriped(offs2)
    tab_ = unpack_weight(tab_words, tab_scales, "e4m3")[:, idx]
    tab2_ = unpack_table4(tab2_words, tab2_scales)[:, idx2]
    zv_ = unpack_weight(zv_words, zv_scales, "e2m1")
    zt_ = unpack_weight(zt_words, zt_scales, "e2m1")
    z = zv_.T @ tab_ + zt_.T @ tab2_
    gate = sigm(z + f64(b)[:, None])
    wv_ = mxq(f64(wv), 0, "e4m3")
    wt_ = unpack_weight(wt_words, wt_scales, "e2m1")
    hv = wv_.T @ tab_
    ht = wt_.T @ tab2_
    av = np.maximum(hv, 0.0)
    at = np.maximum(ht, 0.0)
    out = np.zeros((N, T))
    out[:, idx] = f64(wgo)[0] * (at + gate * (av - at))
    return (out,) + planes(out)

@@ -1,0 +1,225 @@
+from contextlib import ExitStack
+
+import concourse.mybir as mybir
+
+K, L, N, T, J = 512, 1024, 512, 2048, 1024
+FLOPS = 2 * J * N * (2 * K + 2 * L)
+
+F32 = mybir.dt.float32
+BF16 = mybir.dt.bfloat16
+I32 = mybir.dt.int32
+U32 = mybir.dt.uint32
+U16 = mybir.dt.uint16
+U8 = mybir.dt.uint8
+FP8X4 = mybir.dt.float8_e4m3fn_x4
+FP4X4 = mybir.dt.float4_e2m1fn_x4
+ALU = mybir.AluOpType
+ACT = mybir.ActivationFunctionType
+
+P = 128
+PACK = 4
+HALF = 512
+HALVES = J // HALF
+LIST_COLS = HALF // 16
+CHUNK = 512
+CHUNKS = T // CHUNK
+ZV, ZT, WT = 0, 1, 3
+W_PASSES = 5
+
+
+def tile_list_gmu_relu_scatP_kernel(
+    tc, tab_words, tab_scales, tab2_words, tab2_scales, zv_words, zv_scales, zt_words, zt_scales,
+    b, wv, wt_words, wt_scales, wgo, offs, offs2, out_0, out_1, out_2,
+):
+    nc = tc.nc
+    with ExitStack() as ctx:
+        keep = ctx.enter_context(tc.tile_pool(name="keep", bufs=1))
+        ring = ctx.enter_context(tc.tile_pool(name="ring", bufs=3))
+        psum = ctx.enter_context(tc.psum_pool(name="psum", bufs=1))
+
+        def held(name, shape, dtype, tag=""):
+            return keep.tile(shape, dtype, name=name, tag=tag or name, align_bytes=64)
+
+        list1 = held("list1", [P, J // 16], U16)
+        list2 = held("list2", [P, J // 16], U16)
+        tab_w = held("tab_w", [P, T], I32)
+        tab_s = held("tab_s", [P, T], U8)
+        tab2_w = held("tab2_w", [P, T], I32)
+        tab2_s = held("tab2_s", [P, T], U8)
+        w_raw = held("w_raw", [P, W_PASSES, 2 * N], U8)
+        ws_raw = held("ws_raw", [P, W_PASSES, N], U8)
+        w4 = held("w4", [P, W_PASSES, 2 * N], U8)
+        ws_dealt = held("ws_dealt", [P, W_PASSES, N], U8)
+        ws = held("ws", [P, W_PASSES, N], U8)
+        wv_bf = held("wv_bf", [P, N * PACK], BF16)
+        wv_w = held("wv_w", [P, N], U32)
+        wv_s = held("wv_s", [P, N], U8)
+        bias = held("bias", [P, PACK], F32)
+        v2_s0 = held("v2_s0", [P, J], U8)
+        v2_s1 = held("v2_s1", [P, J], U8)
+        page = {0: held("page0", [P, T], F32)}
+
+        for plane in (ws_raw, tab2_s, tab_s, ws, v2_s1):
+            nc.vector.memset(plane[:].bitcast(I32), 0)
+        nc.vector.memset(page[0][:], 0.0)
+
+        for first, words in ((ZV, zv_words), (ZT, zt_words), (WT, wt_words)):
+            passes = words.shape[0]
+            nc.sync.dma_start(w_raw[:, first : first + passes, :].bitcast(I32), words.rearrange("a p n -> p a n").bitcast(I32))
+        nc.sync.dma_start(list2[:], offs2)
+        nc.sync.dma_start(list1[:], offs)
+        nc.sync.dma_start(bias[:], b.rearrange("(p t) -> p t", t=PACK))
+        nc.sync.dma_start(tab2_w[:], tab2_words[0].rearrange("p t i -> p (t i)").bitcast(I32))
+        nc.sync.dma_start(tab_w[:], tab_words[0].rearrange("p t i -> p (t i)").bitcast(I32))
+        for first, scales in ((ZV, zv_scales), (ZT, zt_scales), (WT, wt_scales)):
+            passes = scales.shape[0]
+            nc.scalar.dma_start(ws_raw[0:16, first : first + passes, :].bitcast(I32), scales.rearrange("a q n -> q a n").bitcast(I32))
+        for q in range(4):
+            nc.scalar.dma_start(tab2_s[32 * q : 32 * q + 8, :].bitcast(I32), tab2_scales[:, 4 * q : 4 * q + 4, :].bitcast(I32))
+        for q in range(4):
+            nc.scalar.dma_start(tab_s[32 * q : 32 * q + 4, :].bitcast(I32), tab_scales[0, 4 * q : 4 * q + 4, :].bitcast(I32))
+
+        nc.vector.tensor_copy(
+            w4[:].bitcast(U16).rearrange("p a (t o i) -> p o a t i", t=PACK, i=8),
+            w_raw[:].bitcast(U16).rearrange("p a (o i t) -> p o a t i", t=PACK, i=8),
+        )
+        wv_raw = held("wv_raw", [P, PACK, N], F32, tag="w_raw")
+        nc.sync.dma_start(wv_raw[:], wv.rearrange("(p i) n -> p i n", i=PACK))
+        nc.vector.tensor_copy(
+            ws_dealt[:].rearrange("p a (t o i) -> p o a t i", t=PACK, i=16),
+            ws_raw[:].rearrange("p a (o i t) -> p o a t i", t=PACK, i=16),
+        )
+        for q in range(4):
+            nc.sync.dma_start(ws[32 * q : 32 * q + 4, :, :].bitcast(I32), ws_dealt[4 * q : 4 * q + 4, :, :].bitcast(I32))
+        nc.scalar.copy(
+            wv_bf[:].rearrange("p (t m i) -> p m t i", t=PACK, i=PACK),
+            wv_raw[:].rearrange("p i (m t) -> p m t i", t=PACK),
+        )
+
+        v_w, v_s, v2_w = [], [], []
+
+        def gather_half(h):
+            cols = slice(h * LIST_COLS, (h + 1) * LIST_COLS)
+            both = held("v2_both%d" % h, [P, HALF], U32, tag="page1" if h == HALVES - 1 else "")
+            nc.vector.tensor_copy(both[:], tab2_w[:].bitcast(U32).indirect(list2[:, cols]))
+            if h == 0:
+                nc.vector.tensor_copy(v2_s0[:], tab2_s[:].indirect(list2[:]))
+                nc.sync.dma_start(v2_s1[0 : P - 4, :].bitcast(I32), v2_s0[4:P, :].bitcast(I32))
+            words = held("v_w%d" % h, [P, HALF], U32)
+            nc.vector.tensor_copy(words[:], tab_w[:].bitcast(U32).indirect(list1[:, cols]))
+            parted = held("v2_w%d" % h, [P, 2, 2 * HALF], U8)
+            nc.vector.tensor_copy(
+                parted[:].bitcast(U16).rearrange("p d (o i) -> p o d i", i=8),
+                both[:].bitcast(U16).rearrange("p (o i d) -> p o d i", d=2, i=8),
+            )
+            scales = held("v_s%d" % h, [P, HALF], U8)
+            nc.vector.tensor_copy(scales[:], tab_s[:].indirect(list1[:, cols]))
+            v_w.append(words)
+            v_s.append(scales)
+            v2_w.append(parted)
+
+        gather_half(0)
+        wgo_sb = held("wgo_sb", [P, J], F32, tag="tab2_s")
+        nc.sync.dma_start(wgo_sb[:], wgo)
+        nc.vector.quantize_mx(out=wv_w[:].bitcast(FP8X4), scales=wv_s[:], in_=wv_bf[:])
+        gather_half(1)
+
+        def w4_pass(a, t):
+            return dict(
+                lhsT=w4[:, a, 2 * P * t : 2 * P * (t + 1)].bitcast(FP4X4),
+                lhsT_scale=ws[:, a, P * t : P * (t + 1)],
+            )
+
+        def v_pass(h):
+            return dict(rhs=v_w[h][:].bitcast(FP8X4), rhs_scale=v_s[h][:])
+
+        def v2_pass(h, d):
+            plane = (v2_s0, v2_s1)[d]
+            return dict(rhs=v2_w[h][:, d, :].bitcast(FP4X4), rhs_scale=plane[:, h * HALF : (h + 1) * HALF])
+
+        def mm(out, left, right, start, stop):
+            nc.tensor.matmul_mx(out=out, lhsT=left["lhsT"], lhsT_scale=left["lhsT_scale"], rhs=right["rhs"], rhs_scale=right["rhs_scale"], start=start, stop=stop)
+
+        units = [(t, h) for t in range(PACK) for h in range(HALVES)]
+        gate, rest, summed, shares = {}, {}, {}, {}
+
+        def gates(u):
+            t, h = units[u]
+            z = psum.tile([P, HALF], F32, name="z", bufs=2)
+            mm(z[:], w4_pass(ZT, t), v2_pass(h, 0), True, False)
+            mm(z[:], w4_pass(ZV, t), v_pass(h), False, False)
+            mm(z[:], w4_pass(ZT + 1, t), v2_pass(h, 1), False, True)
+            if h == 0:
+                shares[t] = held("shares%d" % t, [P, 2 * J], F32, tag="page%d" % (t + 2))
+            gate[u] = shares[t][:, 2 * h * HALF : (2 * h + 1) * HALF]
+            rest[u] = shares[t][:, (2 * h + 1) * HALF : (2 * h + 2) * HALF]
+            nc.scalar.activation(gate[u], z[:], ACT.Sigmoid, bias=bias[:, t : t + 1])
+            nc.scalar.activation(rest[u], gate[u], ACT.Copy, bias=1.0, scale=-1.0)
+
+        def branches(u):
+            t, h = units[u]
+            hv = psum.tile([P, HALF], F32, name="hv", bufs=3)
+            left = dict(lhsT=wv_w[:, P * t : P * (t + 1)].bitcast(FP8X4), lhsT_scale=wv_s[:, P * t : P * (t + 1)])
+            mm(hv[:], left, v_pass(h), True, True)
+            ht = psum.tile([P, HALF], F32, name="ht", bufs=3)
+            mm(ht[:], w4_pass(WT, t), v2_pass(h, 0), True, False)
+            mm(ht[:], w4_pass(WT + 1, t), v2_pass(h, 1), False, True)
+            return hv, ht
+
+        def mix(u, hv, ht):
+            part_v = ring.tile([P, HALF], F32, name="part_v")
+            nc.vector.scalar_tensor_tensor(part_v[:], hv[:], 0.0, gate[u], ALU.max, ALU.mult)
+            part_t = ring.tile([P, HALF], F32, name="part_t")
+            nc.vector.scalar_tensor_tensor(part_t[:], ht[:], 0.0, rest[u], ALU.max, ALU.mult)
+            summed[u] = ring.tile([P, HALF], F32, name="summed")
+            nc.gpsimd.tensor_tensor(summed[u][:], part_v[:], part_t[:], ALU.add)
+
+        pairs = [held("pairs%d" % c, [P, 2, CHUNK, 2], BF16) for c in range(CHUNKS)]
+        out_rows = out_0.rearrange("(p t) c -> t p c", t=PACK)
+
+        def scatter(u):
+            t, h = units[u]
+            cols = slice(h * LIST_COLS, (h + 1) * LIST_COLS)
+            nc.vector.tensor_tensor(page[t][:].indirect(list1[:, cols]), summed[u][:], wgo_sb[:, h * HALF : (h + 1) * HALF], ALU.mult)
+            if h == HALVES - 1:
+                nc.sync.dma_start(out_rows[t], page[t][:])
+                for c in range(CHUNKS):
+                    nc.scalar.copy(pairs[c][:, t // 2, :, t % 2], page[t][:, c * CHUNK : (c + 1) * CHUNK])
+
+        def clear_page(t):
+            page[t] = held("page%d" % t, [P, T], F32)
+            nc.gpsimd.memset(page[t][:], 0.0)
+
+        clear_page(1)
+        banks = {}
+        for u in range(2):
+            gates(u)
+            banks[u] = branches(u)
+        for u in range(2, len(units)):
+            gates(u)
+        for u in range(len(units) + 1):
+            if u < len(units):
+                if u not in banks:
+                    banks[u] = branches(u)
+                mix(u, *banks[u])
+                t, h = units[u]
+                if h == HALVES - 1 and t + 2 < PACK:
+                    clear_page(t + 2)
+            if u >= 1:
+                scatter(u - 1)
+
+        y_s = held("y_s", [P, T], U8)
+        out_words = out_1[0].rearrange("p c i -> p (c i)").bitcast(I32)
+        for c in range(CHUNKS):
+            grouped = held("grouped%d" % c, [P, CHUNK * PACK], BF16)
+            src = pairs[c][:].rearrange("p u c e -> p u (c e)").bitcast(F32).rearrange("p u c -> p c u")
+            dst = grouped[:].bitcast(F32).rearrange("p (c u) -> p c u", u=2)
+            if c == CHUNKS - 1:
+                nc.scalar.copy(dst, src)
+            else:
+                nc.vector.tensor_copy(dst, src)
+            y_w = held("y_w%d" % c, [P, CHUNK], I32)
+            nc.vector.quantize_mx(out=y_w[:].bitcast(FP8X4), scales=y_s[:, c * CHUNK : (c + 1) * CHUNK], in_=grouped[:])
+            nc.sync.dma_start(out_words[:, c * CHUNK : (c + 1) * CHUNK], y_w[:])
+        for q in range(4):
+            nc.scalar.dma_start(out_2[0, 4 * q : 4 * q + 4, :].bitcast(I32), y_s[32 * q : 32 * q + 4, :].bitcast(I32))

@@ -25,6 +25,8 @@ CHUNK = 512
 CHUNKS = T // CHUNK
 ZV, ZT, WT = 0, 1, 3
 W_PASSES = 5
+VECTOR_CHUNKS = 2
+LAG = 2
 
 
 def tile_list_gmu_relu_scatP_kernel(
@@ -172,9 +174,10 @@ def tile_list_gmu_relu_scatP_kernel(
             part_t = ring.tile([P, HALF], F32, name="part_t")
             nc.vector.scalar_tensor_tensor(part_t[:], ht[:], 0.0, rest[u], ALU.max, ALU.mult)
             summed[u] = ring.tile([P, HALF], F32, name="summed")
-            nc.gpsimd.tensor_tensor(summed[u][:], part_v[:], part_t[:], ALU.add)
+            adder = nc.vector if u == len(units) - 1 else nc.gpsimd
+            adder.tensor_tensor(summed[u][:], part_v[:], part_t[:], ALU.add)
 
-        pairs = [held("pairs%d" % c, [P, 2, CHUNK, 2], BF16) for c in range(CHUNKS)]
+        grouped = [held("grouped%d" % c, [P, CHUNK, PACK], BF16) for c in range(CHUNKS)]
         out_rows = out_0.rearrange("(p t) c -> t p c", t=PACK)
 
         def scatter(u):
@@ -184,7 +187,13 @@ def tile_list_gmu_relu_scatP_kernel(
             if h == HALVES - 1:
                 nc.sync.dma_start(out_rows[t], page[t][:])
                 for c in range(CHUNKS):
-                    nc.scalar.copy(pairs[c][:, t // 2, :, t % 2], page[t][:, c * CHUNK : (c + 1) * CHUNK])
+                    rows = page[t][:, c * CHUNK : (c + 1) * CHUNK]
+                    if c < VECTOR_CHUNKS and t == PACK - 2:
+                        nc.scalar.copy(grouped[c][:, :, t : t + 2], rows.unsqueeze(2).to_broadcast([P, CHUNK, 2]))
+                    elif c < VECTOR_CHUNKS and t == PACK - 1:
+                        nc.vector.tensor_copy(grouped[c][:, :, t], rows)
+                    else:
+                        nc.scalar.copy(grouped[c][:, :, t], rows)
 
         def clear_page(t):
             page[t] = held("page%d" % t, [P, T], F32)
@@ -197,7 +206,7 @@ def tile_list_gmu_relu_scatP_kernel(
             banks[u] = branches(u)
         for u in range(2, len(units)):
             gates(u)
-        for u in range(len(units) + 1):
+        for u in range(len(units) + LAG):
             if u < len(units):
                 if u not in banks:
                     banks[u] = branches(u)
@@ -205,21 +214,14 @@ def tile_list_gmu_relu_scatP_kernel(
                 t, h = units[u]
                 if h == HALVES - 1 and t + 2 < PACK:
                     clear_page(t + 2)
-            if u >= 1:
-                scatter(u - 1)
+            if u >= LAG:
+                scatter(u - LAG)
 
         y_s = held("y_s", [P, T], U8)
         out_words = out_1[0].rearrange("p c i -> p (c i)").bitcast(I32)
         for c in range(CHUNKS):
-            grouped = held("grouped%d" % c, [P, CHUNK * PACK], BF16)
-            src = pairs[c][:].rearrange("p u c e -> p u (c e)").bitcast(F32).rearrange("p u c -> p c u")
-            dst = grouped[:].bitcast(F32).rearrange("p (c u) -> p c u", u=2)
-            if c == CHUNKS - 1:
-                nc.scalar.copy(dst, src)
-            else:
-                nc.vector.tensor_copy(dst, src)
             y_w = held("y_w%d" % c, [P, CHUNK], I32)
-            nc.vector.quantize_mx(out=y_w[:].bitcast(FP8X4), scales=y_s[:, c * CHUNK : (c + 1) * CHUNK], in_=grouped[:])
+            nc.vector.quantize_mx(out=y_w[:].bitcast(FP8X4), scales=y_s[:, c * CHUNK : (c + 1) * CHUNK], in_=grouped[c][:].rearrange("p c i -> p (c i)"))
             nc.sync.dma_start(out_words[:, c * CHUNK : (c + 1) * CHUNK], y_w[:])
         for q in range(4):
             nc.scalar.dma_start(out_2[0, 4 * q : 4 * q + 4, :].bitcast(I32), y_s[32 * q : 32 * q + 4, :].bitcast(I32))

@@ -44,7 +44,7 @@ def tile_list_gmu_relu_scatP_kernel(
 
         list1 = held("list1", [P, J // 16], U16)
         list2 = held("list2", [P, J // 16], U16)
-        tab_w = held("tab_w", [P, T], I32)
+        tab_w = held("tab_w", [P, T], I32, tag="page1")
         tab_s = held("tab_s", [P, T], U8)
         tab2_w = held("tab2_w", [P, T], I32)
         tab2_s = held("tab2_s", [P, T], U8)
@@ -102,12 +102,12 @@ def tile_list_gmu_relu_scatP_kernel(
 
         def gather_half(h):
             cols = slice(h * LIST_COLS, (h + 1) * LIST_COLS)
-            both = held("v2_both%d" % h, [P, HALF], U32, tag="page1" if h == HALVES - 1 else "")
+            both = held("v2_both%d" % h, [P, HALF], U32)
             nc.vector.tensor_copy(both[:], tab2_w[:].bitcast(U32).indirect(list2[:, cols]))
             if h == 0:
                 nc.vector.tensor_copy(v2_s0[:], tab2_s[:].indirect(list2[:]))
                 nc.sync.dma_start(v2_s1[0 : P - 4, :].bitcast(I32), v2_s0[4:P, :].bitcast(I32))
-            words = held("v_w%d" % h, [P, HALF], U32)
+            words = held("v_w%d" % h, [P, HALF], U32, tag="wv_bf" if h == HALVES - 1 else "")
             nc.vector.tensor_copy(words[:], tab_w[:].bitcast(U32).indirect(list1[:, cols]))
             parted = held("v2_w%d" % h, [P, 2, 2 * HALF], U8)
             nc.vector.tensor_copy(
@@ -169,13 +169,15 @@ def tile_list_gmu_relu_scatP_kernel(
             return hv, ht
 
         def mix(u, hv, ht):
-            part_v = ring.tile([P, HALF], F32, name="part_v")
+            part_v = ring.tile([P, HALF], F32, name="part_v", bufs=2)
             nc.vector.scalar_tensor_tensor(part_v[:], hv[:], 0.0, gate[u], ALU.max, ALU.mult)
-            part_t = ring.tile([P, HALF], F32, name="part_t")
+            part_t = ring.tile([P, HALF], F32, name="part_t", bufs=2)
             nc.vector.scalar_tensor_tensor(part_t[:], ht[:], 0.0, rest[u], ALU.max, ALU.mult)
             summed[u] = ring.tile([P, HALF], F32, name="summed")
-            adder = nc.vector if u == len(units) - 1 else nc.gpsimd
-            adder.tensor_tensor(summed[u][:], part_v[:], part_t[:], ALU.add)
+            h = units[u][1]
+            both = ring.tile([P, HALF], F32, name="both")
+            nc.gpsimd.tensor_tensor(both[:], part_v[:], part_t[:], ALU.add)
+            nc.gpsimd.tensor_tensor(summed[u][:], both[:], wgo_sb[:, h * HALF : (h + 1) * HALF], ALU.mult)
 
         grouped = [held("grouped%d" % c, [P, CHUNK, PACK], BF16) for c in range(CHUNKS)]
         out_rows = out_0.rearrange("(p t) c -> t p c", t=PACK)
@@ -183,9 +185,12 @@ def tile_list_gmu_relu_scatP_kernel(
         def scatter(u):
             t, h = units[u]
             cols = slice(h * LIST_COLS, (h + 1) * LIST_COLS)
-            nc.vector.tensor_tensor(page[t][:].indirect(list1[:, cols]), summed[u][:], wgo_sb[:, h * HALF : (h + 1) * HALF], ALU.mult)
+            nc.vector.tensor_copy(page[t][:].indirect(list1[:, cols]), summed[u][:])
             if h == HALVES - 1:
                 nc.sync.dma_start(out_rows[t], page[t][:])
+
+        def round_page(t):
+            if True:
                 for c in range(CHUNKS):
                     rows = page[t][:, c * CHUNK : (c + 1) * CHUNK]
                     if c < VECTOR_CHUNKS and t == PACK - 2:
@@ -200,22 +205,17 @@ def tile_list_gmu_relu_scatP_kernel(
             nc.gpsimd.memset(page[t][:], 0.0)
 
         clear_page(1)
-        banks = {}
-        for u in range(2):
-            gates(u)
-            banks[u] = branches(u)
-        for u in range(2, len(units)):
-            gates(u)
         for u in range(len(units) + LAG):
             if u < len(units):
-                if u not in banks:
-                    banks[u] = branches(u)
-                mix(u, *banks[u])
+                gates(u)
+                mix(u, *branches(u))
                 t, h = units[u]
                 if h == HALVES - 1 and t + 2 < PACK:
                     clear_page(t + 2)
             if u >= LAG:
                 scatter(u - LAG)
+        for t in range(PACK):
+            round_page(t)
 
         y_s = held("y_s", [P, T], U8)
         out_words = out_1[0].rearrange("p c i -> p (c i)").bitcast(I32)

@@ -21,8 +21,9 @@ PACK = 4
 HALF = 512
 HALVES = J // HALF
 LIST_COLS = HALF // 16
-CHUNK = 512
-CHUNKS = T // CHUNK
+CHUNK_WIDTHS = (512, 512, 512, 256, 256)
+CHUNKS = len(CHUNK_WIDTHS)
+CHUNK_COLS = [slice(sum(CHUNK_WIDTHS[:c]), sum(CHUNK_WIDTHS[: c + 1])) for c in range(CHUNKS)]
 ZV, ZT, WT = 0, 1, 3
 W_PASSES = 5
 VECTOR_CHUNKS = 2
@@ -44,174 +45,196 @@ def tile_list_gmu_relu_scatP_kernel(
 
         list1 = held("list1", [P, J // 16], U16)
         list2 = held("list2", [P, J // 16], U16)
-        tab_w = held("tab_w", [P, T], I32, tag="page1")
         tab_s = held("tab_s", [P, T], U8)
         tab2_w = held("tab2_w", [P, T], I32)
         tab2_s = held("tab2_s", [P, T], U8)
         w_raw = held("w_raw", [P, W_PASSES, 2 * N], U8)
-        ws_raw = held("ws_raw", [P, W_PASSES, N], U8)
-        w4 = held("w4", [P, W_PASSES, 2 * N], U8)
-        ws_dealt = held("ws_dealt", [P, W_PASSES, N], U8)
-        ws = held("ws", [P, W_PASSES, N], U8)
-        wv_bf = held("wv_bf", [P, N * PACK], BF16)
-        wv_w = held("wv_w", [P, N], U32)
+        ws_raw = held("ws_raw", [P, 3, N], U8)
+        ws = held("ws", [P, 2, 3, N], U8)
+        wv_bf = held("wv_bf", [P, N * PACK], BF16, tag="page2")
+        wv_raw = held("wv_raw", [P, PACK, N], F32)
         wv_s = held("wv_s", [P, N], U8)
         bias = held("bias", [P, PACK], F32)
-        v2_s0 = held("v2_s0", [P, J], U8)
-        v2_s1 = held("v2_s1", [P, J], U8)
-        page = {0: held("page0", [P, T], F32)}
+        v2_s_rows = held("v2_s_rows", [P, J], U8)
+        v2_s = held("v2_s", [P, 2, J], U8)
+        page = {t: held("page%d" % t, [P, T], F32) for t in range(2)}
 
-        for plane in (ws_raw, tab2_s, tab_s, ws, v2_s1):
+        for plane in (tab2_s, ws_raw, tab_s, v2_s, ws):
             nc.vector.memset(plane[:].bitcast(I32), 0)
-        nc.vector.memset(page[0][:], 0.0)
+        for t in range(2):
+            nc.vector.memset(page[t][:], 0.0)
 
+        nc.sync.dma_start(list2[:], offs2)
+        nc.sync.dma_start(tab2_w[:], tab2_words[0].rearrange("p t i -> p (t i)").bitcast(I32))
+        nc.sync.dma_start(list1[:], offs)
+        nc.sync.dma_start(bias[:], b.rearrange("(p t) -> p t", t=PACK))
+        nc.sync.dma_start(wv_raw[:], wv.rearrange("(p i) n -> p i n", i=PACK))
         for first, words in ((ZV, zv_words), (ZT, zt_words), (WT, wt_words)):
             passes = words.shape[0]
             nc.sync.dma_start(w_raw[:, first : first + passes, :].bitcast(I32), words.rearrange("a p n -> p a n").bitcast(I32))
-        nc.sync.dma_start(list2[:], offs2)
-        nc.sync.dma_start(list1[:], offs)
-        nc.sync.dma_start(bias[:], b.rearrange("(p t) -> p t", t=PACK))
-        nc.sync.dma_start(tab2_w[:], tab2_words[0].rearrange("p t i -> p (t i)").bitcast(I32))
-        nc.sync.dma_start(tab_w[:], tab_words[0].rearrange("p t i -> p (t i)").bitcast(I32))
-        for first, scales in ((ZV, zv_scales), (ZT, zt_scales), (WT, wt_scales)):
-            passes = scales.shape[0]
-            nc.scalar.dma_start(ws_raw[0:16, first : first + passes, :].bitcast(I32), scales.rearrange("a q n -> q a n").bitcast(I32))
-        for q in range(4):
-            nc.scalar.dma_start(tab2_s[32 * q : 32 * q + 8, :].bitcast(I32), tab2_scales[:, 4 * q : 4 * q + 4, :].bitcast(I32))
+        nc.scalar.dma_start(tab2_s[0:32, :].bitcast(I32), tab2_scales.rearrange("a q t -> q a t").bitcast(I32))
+        nc.scalar.dma_start(ws_raw[0:32, 0, :].bitcast(I32), zt_scales.rearrange("a q n -> q a n").bitcast(I32))
+        nc.scalar.dma_start(ws_raw[0:32, 1, :].bitcast(I32), wt_scales.rearrange("a q n -> q a n").bitcast(I32))
+        nc.scalar.dma_start(ws_raw[0:32:2, 2, :].bitcast(I32), zv_scales[0].bitcast(I32))
         for q in range(4):
             nc.scalar.dma_start(tab_s[32 * q : 32 * q + 4, :].bitcast(I32), tab_scales[0, 4 * q : 4 * q + 4, :].bitcast(I32))
 
-        nc.vector.tensor_copy(
-            w4[:].bitcast(U16).rearrange("p a (t o i) -> p o a t i", t=PACK, i=8),
-            w_raw[:].bitcast(U16).rearrange("p a (o i t) -> p o a t i", t=PACK, i=8),
-        )
-        wv_raw = held("wv_raw", [P, PACK, N], F32, tag="w_raw")
-        nc.sync.dma_start(wv_raw[:], wv.rearrange("(p i) n -> p i n", i=PACK))
-        nc.vector.tensor_copy(
-            ws_dealt[:].rearrange("p a (t o i) -> p o a t i", t=PACK, i=16),
-            ws_raw[:].rearrange("p a (o i t) -> p o a t i", t=PACK, i=16),
-        )
-        for q in range(4):
-            nc.sync.dma_start(ws[32 * q : 32 * q + 4, :, :].bitcast(I32), ws_dealt[4 * q : 4 * q + 4, :, :].bitcast(I32))
-        nc.scalar.copy(
-            wv_bf[:].rearrange("p (t m i) -> p m t i", t=PACK, i=PACK),
-            wv_raw[:].rearrange("p i (m t) -> p m t i", t=PACK),
-        )
+        def list_cols(h):
+            return slice(h * LIST_COLS, (h + 1) * LIST_COLS)
 
-        v_w, v_s, v2_w = [], [], []
-
-        def gather_half(h):
-            cols = slice(h * LIST_COLS, (h + 1) * LIST_COLS)
+        v2_w = []
+        for h in range(HALVES):
             both = held("v2_both%d" % h, [P, HALF], U32)
-            nc.vector.tensor_copy(both[:], tab2_w[:].bitcast(U32).indirect(list2[:, cols]))
-            if h == 0:
-                nc.vector.tensor_copy(v2_s0[:], tab2_s[:].indirect(list2[:]))
-                nc.sync.dma_start(v2_s1[0 : P - 4, :].bitcast(I32), v2_s0[4:P, :].bitcast(I32))
-            words = held("v_w%d" % h, [P, HALF], U32, tag="wv_bf" if h == HALVES - 1 else "")
-            nc.vector.tensor_copy(words[:], tab_w[:].bitcast(U32).indirect(list1[:, cols]))
+            nc.vector.tensor_copy(both[:], tab2_w[:].bitcast(U32).indirect(list2[:, list_cols(h)]))
             parted = held("v2_w%d" % h, [P, 2, 2 * HALF], U8)
             nc.vector.tensor_copy(
                 parted[:].bitcast(U16).rearrange("p d (o i) -> p o d i", i=8),
                 both[:].bitcast(U16).rearrange("p (o i d) -> p o d i", d=2, i=8),
             )
-            scales = held("v_s%d" % h, [P, HALF], U8)
-            nc.vector.tensor_copy(scales[:], tab_s[:].indirect(list1[:, cols]))
+            v2_w.append(parted)
+        tab_w = held("tab_w", [P, T], I32, tag="v2_both0")
+        nc.sync.dma_start(tab_w[:], tab_words[0].rearrange("p t i -> p (t i)").bitcast(I32))
+
+        nc.vector.tensor_copy(v2_s_rows[:], tab2_s[:].indirect(list2[:]))
+        for q in range(4):
+            nc.sync.dma_start(v2_s[32 * q : 32 * q + 4, :, :].bitcast(I32), v2_s_rows[8 * q : 8 * q + 8, :].bitcast(I32))
+
+        ws_dealt = held("ws_dealt", [P, 3, N], U8, tag="tab2_s")
+        nc.vector.tensor_copy(
+            ws_dealt[:].rearrange("p a (t o i) -> p o a t i", t=PACK, i=16),
+            ws_raw[:].rearrange("p a (o i t) -> p o a t i", t=PACK, i=16),
+        )
+        for q in range(4):
+            nc.sync.dma_start(
+                ws[32 * q : 32 * q + 4, :, :, :].rearrange("p d a n -> p d (a n)").bitcast(I32),
+                ws_dealt[8 * q : 8 * q + 8, :, :].rearrange("p a n -> p (a n)").bitcast(I32),
+            )
+        wgo_sb = held("wgo_sb", [P, J], F32, tag="v2_s_rows")
+        nc.sync.dma_start(wgo_sb[:], wgo)
+        w4 = held("w4", [P, W_PASSES, 2 * N], U8, tag="ws_raw")
+        nc.vector.tensor_copy(
+            w4[:].bitcast(U16).rearrange("p a (t o i) -> p o a t i", t=PACK, i=8),
+            w_raw[:].bitcast(U16).rearrange("p a (o i t) -> p o a t i", t=PACK, i=8),
+        )
+        nc.scalar.copy(
+            wv_bf[:].rearrange("p (t m i) -> p m t i", t=PACK, i=PACK),
+            wv_raw[:].rearrange("p i (m t) -> p m t i", t=PACK),
+        )
+        wv_w = held("wv_w", [P, N], U32, tag="w_raw")
+        nc.vector.quantize_mx(out=wv_w[:].bitcast(FP8X4), scales=wv_s[:], in_=wv_bf[:])
+        page[2] = held("page2", [P, T], F32)
+        nc.gpsimd.memset(page[2][:], 0.0)
+
+        v_w, v_s = [], []
+        for h in range(HALVES):
+            words = held("v_w%d" % h, [P, HALF], U32)
+            nc.vector.tensor_copy(words[:], tab_w[:].bitcast(U32).indirect(list1[:, list_cols(h)]))
+            scales = held("v_s%d" % h, [P, HALF], U8, tag="tab2_s" if h == 1 else "")
+            nc.vector.tensor_copy(scales[:], tab_s[:].indirect(list1[:, list_cols(h)]))
             v_w.append(words)
             v_s.append(scales)
-            v2_w.append(parted)
 
-        gather_half(0)
-        wgo_sb = held("wgo_sb", [P, J], F32, tag="tab2_s")
-        nc.sync.dma_start(wgo_sb[:], wgo)
-        nc.vector.quantize_mx(out=wv_w[:].bitcast(FP8X4), scales=wv_s[:], in_=wv_bf[:])
-        gather_half(1)
+        page[3] = held("page3", [P, T], F32, tag="v2_both0")
+        nc.gpsimd.memset(page[3][:], 0.0)
+        plane_of = {ZV: (0, 2), ZT: (0, 0), ZT + 1: (1, 0), WT: (0, 1), WT + 1: (1, 1)}
 
         def w4_pass(a, t):
             return dict(
                 lhsT=w4[:, a, 2 * P * t : 2 * P * (t + 1)].bitcast(FP4X4),
-                lhsT_scale=ws[:, a, P * t : P * (t + 1)],
+                lhsT_scale=ws[:, plane_of[a][0], plane_of[a][1], P * t : P * (t + 1)],
             )
 
         def v_pass(h):
             return dict(rhs=v_w[h][:].bitcast(FP8X4), rhs_scale=v_s[h][:])
 
         def v2_pass(h, d):
-            plane = (v2_s0, v2_s1)[d]
-            return dict(rhs=v2_w[h][:, d, :].bitcast(FP4X4), rhs_scale=plane[:, h * HALF : (h + 1) * HALF])
+            return dict(rhs=v2_w[h][:, d, :].bitcast(FP4X4), rhs_scale=v2_s[:, d, h * HALF : (h + 1) * HALF])
 
         def mm(out, left, right, start, stop):
             nc.tensor.matmul_mx(out=out, lhsT=left["lhsT"], lhsT_scale=left["lhsT_scale"], rhs=right["rhs"], rhs_scale=right["rhs_scale"], start=start, stop=stop)
 
         units = [(t, h) for t in range(PACK) for h in range(HALVES)]
-        gate, rest, summed, shares = {}, {}, {}, {}
+        summed = {}
+        last = len(units) - 1
 
-        def gates(u):
+        def mix(u):
             t, h = units[u]
-            z = psum.tile([P, HALF], F32, name="z", bufs=2)
-            mm(z[:], w4_pass(ZT, t), v2_pass(h, 0), True, False)
-            mm(z[:], w4_pass(ZV, t), v_pass(h), False, False)
-            mm(z[:], w4_pass(ZT + 1, t), v2_pass(h, 1), False, True)
-            if h == 0:
-                shares[t] = held("shares%d" % t, [P, 2 * J], F32, tag="page%d" % (t + 2))
-            gate[u] = shares[t][:, 2 * h * HALF : (2 * h + 1) * HALF]
-            rest[u] = shares[t][:, (2 * h + 1) * HALF : (2 * h + 2) * HALF]
-            nc.scalar.activation(gate[u], z[:], ACT.Sigmoid, bias=bias[:, t : t + 1])
-            nc.scalar.activation(rest[u], gate[u], ACT.Copy, bias=1.0, scale=-1.0)
-
-        def branches(u):
-            t, h = units[u]
-            hv = psum.tile([P, HALF], F32, name="hv", bufs=3)
-            left = dict(lhsT=wv_w[:, P * t : P * (t + 1)].bitcast(FP8X4), lhsT_scale=wv_s[:, P * t : P * (t + 1)])
-            mm(hv[:], left, v_pass(h), True, True)
-            ht = psum.tile([P, HALF], F32, name="ht", bufs=3)
-            mm(ht[:], w4_pass(WT, t), v2_pass(h, 0), True, False)
-            mm(ht[:], w4_pass(WT + 1, t), v2_pass(h, 1), False, True)
-            return hv, ht
-
-        def mix(u, hv, ht):
-            part_v = ring.tile([P, HALF], F32, name="part_v", bufs=2)
-            nc.vector.scalar_tensor_tensor(part_v[:], hv[:], 0.0, gate[u], ALU.max, ALU.mult)
-            part_t = ring.tile([P, HALF], F32, name="part_t", bufs=2)
-            nc.vector.scalar_tensor_tensor(part_t[:], ht[:], 0.0, rest[u], ALU.max, ALU.mult)
-            summed[u] = ring.tile([P, HALF], F32, name="summed")
-            h = units[u][1]
+            gate = held("gate%d" % u, [P, HALF], F32)
+            other = held("other%d" % u, [P, HALF], F32)
+            slot = 2 if u == 0 else u % 2
+            part_v = held("part_v%d" % slot, [P, HALF], F32)
+            part_t = held("part_t%d" % slot, [P, HALF], F32)
             both = ring.tile([P, HALF], F32, name="both")
-            nc.gpsimd.tensor_tensor(both[:], part_v[:], part_t[:], ALU.add)
-            nc.gpsimd.tensor_tensor(summed[u][:], both[:], wgo_sb[:, h * HALF : (h + 1) * HALF], ALU.mult)
 
-        grouped = [held("grouped%d" % c, [P, CHUNK, PACK], BF16) for c in range(CHUNKS)]
+            def gate_of(tag):
+                z = psum.tile([P, HALF], F32, name=tag, bufs=2)
+                mm(z[:], w4_pass(ZT, t), v2_pass(h, 0), True, False)
+                mm(z[:], w4_pass(ZT + 1, t), v2_pass(h, 1), False, False)
+                mm(z[:], w4_pass(ZV, t), v_pass(h), False, True)
+                nc.scalar.activation(gate[:], z[:], ACT.Sigmoid, bias=bias[:, t : t + 1])
+                return z
+
+            def text_sum(tag):
+                ht = psum.tile([P, HALF], F32, name=tag, bufs=2)
+                mm(ht[:], w4_pass(WT, t), v2_pass(h, 0), True, False)
+                mm(ht[:], w4_pass(WT + 1, t), v2_pass(h, 1), False, True)
+                return ht
+
+            def picture_sum(hv):
+                left = dict(lhsT=wv_w[:, P * t : P * (t + 1)].bitcast(FP8X4), lhsT_scale=wv_s[:, P * t : P * (t + 1)])
+                mm(hv[:], left, v_pass(h), True, True)
+                return hv
+
+            if h == 0:
+                z = gate_of("z_hv")
+                ht = text_sum("ht")
+                hv = picture_sum(z)
+                nc.scalar.activation(other[:], gate[:], ACT.Copy, bias=1.0, scale=-1.0)
+                nc.vector.scalar_tensor_tensor(part_v[:], hv[:], 0.0, gate[:], ALU.max, ALU.mult)
+                nc.vector.scalar_tensor_tensor(part_t[:], ht[:], 0.0, other[:], ALU.max, ALU.mult)
+                adder = nc.vector if u == 0 else nc.gpsimd
+                adder.tensor_tensor(both[:], part_v[:], part_t[:], ALU.add)
+            else:
+                ht = text_sum("brief")
+                nc.scalar.activation(other[:], ht[:], ACT.Relu)
+                hv = picture_sum(psum.tile([P, HALF], F32, name="hv", bufs=2))
+                gate_of("brief")
+                nc.vector.scalar_tensor_tensor(part_v[:], hv[:], 0.0, other[:], ALU.max, ALU.subtract)
+                nc.gpsimd.tensor_tensor(part_t[:], part_v[:], gate[:], ALU.mult)
+                nc.gpsimd.tensor_tensor(both[:], part_t[:], other[:], ALU.add)
+            if u == last:
+                summed[u] = both
+            else:
+                summed[u] = ring.tile([P, HALF], F32, name="summed")
+                nc.gpsimd.tensor_tensor(summed[u][:], both[:], wgo_sb[:, h * HALF : (h + 1) * HALF], ALU.mult)
+
+        grouped = [held("grouped%d" % c, [P, CHUNK_WIDTHS[c], PACK], BF16) for c in range(CHUNKS)]
         out_rows = out_0.rearrange("(p t) c -> t p c", t=PACK)
 
         def scatter(u):
             t, h = units[u]
             cols = slice(h * LIST_COLS, (h + 1) * LIST_COLS)
-            nc.vector.tensor_copy(page[t][:].indirect(list1[:, cols]), summed[u][:])
+            if u == last:
+                nc.vector.tensor_tensor(page[t][:].indirect(list1[:, cols]), summed[u][:], wgo_sb[:, h * HALF : (h + 1) * HALF], ALU.mult)
+            else:
+                nc.vector.tensor_copy(page[t][:].indirect(list1[:, cols]), summed[u][:])
             if h == HALVES - 1:
                 nc.sync.dma_start(out_rows[t], page[t][:])
 
         def round_page(t):
             if True:
                 for c in range(CHUNKS):
-                    rows = page[t][:, c * CHUNK : (c + 1) * CHUNK]
+                    rows = page[t][:, CHUNK_COLS[c]]
                     if c < VECTOR_CHUNKS and t == PACK - 2:
-                        nc.scalar.copy(grouped[c][:, :, t : t + 2], rows.unsqueeze(2).to_broadcast([P, CHUNK, 2]))
+                        nc.scalar.copy(grouped[c][:, :, t : t + 2], rows.unsqueeze(2).to_broadcast([P, CHUNK_WIDTHS[c], 2]))
                     elif c < VECTOR_CHUNKS and t == PACK - 1:
                         nc.vector.tensor_copy(grouped[c][:, :, t], rows)
                     else:
                         nc.scalar.copy(grouped[c][:, :, t], rows)
 
-        def clear_page(t):
-            page[t] = held("page%d" % t, [P, T], F32)
-            nc.gpsimd.memset(page[t][:], 0.0)
-
-        clear_page(1)
         for u in range(len(units) + LAG):
             if u < len(units):
-                gates(u)
-                mix(u, *branches(u))
-                t, h = units[u]
-                if h == HALVES - 1 and t + 2 < PACK:
-                    clear_page(t + 2)
+                mix(u)
             if u >= LAG:
                 scatter(u - LAG)
         for t in range(PACK):
@@ -220,8 +243,8 @@ def tile_list_gmu_relu_scatP_kernel(
         y_s = held("y_s", [P, T], U8)
         out_words = out_1[0].rearrange("p c i -> p (c i)").bitcast(I32)
         for c in range(CHUNKS):
-            y_w = held("y_w%d" % c, [P, CHUNK], I32)
-            nc.vector.quantize_mx(out=y_w[:].bitcast(FP8X4), scales=y_s[:, c * CHUNK : (c + 1) * CHUNK], in_=grouped[c][:].rearrange("p c i -> p (c i)"))
-            nc.sync.dma_start(out_words[:, c * CHUNK : (c + 1) * CHUNK], y_w[:])
+            y_w = held("y_w%d" % c, [P, CHUNK_WIDTHS[c]], I32)
+            nc.vector.quantize_mx(out=y_w[:].bitcast(FP8X4), scales=y_s[:, CHUNK_COLS[c]], in_=grouped[c][:].rearrange("p c i -> p (c i)"))
+            nc.sync.dma_start(out_words[:, CHUNK_COLS[c]], y_w[:])
         for q in range(4):
             nc.scalar.dma_start(out_2[0, 4 * q : 4 * q + 4, :].bitcast(I32), y_s[32 * q : 32 * q + 4, :].bitcast(I32))

@@ -27,7 +27,13 @@ CHUNK_COLS = [slice(sum(CHUNK_WIDTHS[:c]), sum(CHUNK_WIDTHS[: c + 1])) for c in 
 ZV, ZT, WT = 0, 1, 3
 W_PASSES = 5
 VECTOR_CHUNKS = 2
-LAG = 2
+BANKS = {"scalar": 4, "vector": 4}
+ROADS = "WTTTXXXE"
+AFTER = {3: 0}
+PAGE_BYTES = 4 * T
+WORD_BYTES = 4 * HALF
+RAW_AT = PAGE_BYTES
+CAST_AT = RAW_AT + 8192
 
 
 def tile_list_gmu_relu_scatP_kernel(
@@ -37,208 +43,285 @@ def tile_list_gmu_relu_scatP_kernel(
     nc = tc.nc
     with ExitStack() as ctx:
         keep = ctx.enter_context(tc.tile_pool(name="keep", bufs=1))
-        ring = ctx.enter_context(tc.tile_pool(name="ring", bufs=3))
+        placed = ctx.enter_context(tc.tile_pool(name="placed", bufs=1))
+        ring = ctx.enter_context(tc.tile_pool(name="ring", bufs=1))
         psum = ctx.enter_context(tc.psum_pool(name="psum", bufs=1))
 
         def held(name, shape, dtype, tag=""):
             return keep.tile(shape, dtype, name=name, tag=tag or name, align_bytes=64)
 
+        def at_byte(name, shape, dtype, offset):
+            return placed.tile(shape, dtype, name=name, tag=name, align_bytes=64, offset=offset)
+
         list1 = held("list1", [P, J // 16], U16)
         list2 = held("list2", [P, J // 16], U16)
         tab_s = held("tab_s", [P, T], U8)
+        tab2_s = held("tab2_s", [P, T], U8, tag="tab_w")
         tab2_w = held("tab2_w", [P, T], I32)
-        tab2_s = held("tab2_s", [P, T], U8)
-        w_raw = held("w_raw", [P, W_PASSES, 2 * N], U8)
         ws_raw = held("ws_raw", [P, 3, N], U8)
-        ws = held("ws", [P, 2, 3, N], U8)
-        wv_bf = held("wv_bf", [P, N * PACK], BF16, tag="page2")
+        w_raw = at_byte("w_raw", [P, W_PASSES, 2 * N], U8, RAW_AT)
         wv_raw = held("wv_raw", [P, PACK, N], F32)
-        wv_s = held("wv_s", [P, N], U8)
+        wv_bf = at_byte("wv_bf", [P, N * PACK], BF16, CAST_AT)
         bias = held("bias", [P, PACK], F32)
-        v2_s_rows = held("v2_s_rows", [P, J], U8)
-        v2_s = held("v2_s", [P, 2, J], U8)
-        page = {t: held("page%d" % t, [P, T], F32) for t in range(2)}
+        page = {0: held("page0", [P, T], F32)}
 
-        for plane in (tab2_s, ws_raw, tab_s, v2_s, ws):
-            nc.vector.memset(plane[:].bitcast(I32), 0)
-        for t in range(2):
-            nc.vector.memset(page[t][:], 0.0)
+        nc.vector.memset(ws_raw[:].bitcast(I32), 0)
+        nc.vector.memset(tab_s[:].bitcast(I32), 0)
+        nc.vector.memset(tab2_s[32:64, :].bitcast(I32), 0)
+        nc.vector.memset(tab2_s[64:128, :].bitcast(I32), 0)
+        nc.vector.memset(page[0][:], 0.0)
 
         nc.sync.dma_start(list2[:], offs2)
+        nc.sync.dma_start(tab2_s[0:32, :].bitcast(I32), tab2_scales.rearrange("a q t -> q a t").bitcast(I32))
         nc.sync.dma_start(tab2_w[:], tab2_words[0].rearrange("p t i -> p (t i)").bitcast(I32))
         nc.sync.dma_start(list1[:], offs)
-        nc.sync.dma_start(bias[:], b.rearrange("(p t) -> p t", t=PACK))
         nc.sync.dma_start(wv_raw[:], wv.rearrange("(p i) n -> p i n", i=PACK))
-        for first, words in ((ZV, zv_words), (ZT, zt_words), (WT, wt_words)):
-            passes = words.shape[0]
-            nc.sync.dma_start(w_raw[:, first : first + passes, :].bitcast(I32), words.rearrange("a p n -> p a n").bitcast(I32))
-        nc.scalar.dma_start(tab2_s[0:32, :].bitcast(I32), tab2_scales.rearrange("a q t -> q a t").bitcast(I32))
+        nc.sync.dma_start(bias[:], b.rearrange("(p t) -> p t", t=PACK))
         nc.scalar.dma_start(ws_raw[0:32, 0, :].bitcast(I32), zt_scales.rearrange("a q n -> q a n").bitcast(I32))
         nc.scalar.dma_start(ws_raw[0:32, 1, :].bitcast(I32), wt_scales.rearrange("a q n -> q a n").bitcast(I32))
         nc.scalar.dma_start(ws_raw[0:32:2, 2, :].bitcast(I32), zv_scales[0].bitcast(I32))
+        for first, words in ((ZT, zt_words), (WT, wt_words), (ZV, zv_words)):
+            passes = words.shape[0]
+            nc.scalar.dma_start(w_raw[:, first : first + passes, :].bitcast(I32), words.rearrange("a p n -> p a n").bitcast(I32))
         for q in range(4):
             nc.scalar.dma_start(tab_s[32 * q : 32 * q + 4, :].bitcast(I32), tab_scales[0, 4 * q : 4 * q + 4, :].bitcast(I32))
+
+        warm = held("warm", [P, 8], F32)
+        nc.scalar.activation(warm[:, 0:1], page[0][:, 0:1], ACT.Sigmoid)
 
         def list_cols(h):
             return slice(h * LIST_COLS, (h + 1) * LIST_COLS)
 
-        v2_w = []
-        for h in range(HALVES):
-            both = held("v2_both%d" % h, [P, HALF], U32)
-            nc.vector.tensor_copy(both[:], tab2_w[:].bitcast(U32).indirect(list2[:, list_cols(h)]))
-            parted = held("v2_w%d" % h, [P, 2, 2 * HALF], U8)
-            nc.vector.tensor_copy(
-                parted[:].bitcast(U16).rearrange("p d (o i) -> p o d i", i=8),
-                both[:].bitcast(U16).rearrange("p (o i d) -> p o d i", d=2, i=8),
-            )
-            v2_w.append(parted)
-        tab_w = held("tab_w", [P, T], I32, tag="v2_both0")
-        nc.sync.dma_start(tab_w[:], tab_words[0].rearrange("p t i -> p (t i)").bitcast(I32))
+        def half_cols(h):
+            return slice(h * HALF, (h + 1) * HALF)
 
+        v2_s_rows = held("v2_s_rows", [P, J], U8)
         nc.vector.tensor_copy(v2_s_rows[:], tab2_s[:].indirect(list2[:]))
-        for q in range(4):
-            nc.sync.dma_start(v2_s[32 * q : 32 * q + 4, :, :].bitcast(I32), v2_s_rows[8 * q : 8 * q + 8, :].bitcast(I32))
-
-        ws_dealt = held("ws_dealt", [P, 3, N], U8, tag="tab2_s")
+        tab_w = held("tab_w", [P, T], I32)
+        nc.sync.dma_start(tab_w[:], tab_words[0].rearrange("p t i -> p (t i)").bitcast(I32))
+        rows = held("rows", [P, J + 3 * N], U8, tag="wgo_sb")
         nc.vector.tensor_copy(
-            ws_dealt[:].rearrange("p a (t o i) -> p o a t i", t=PACK, i=16),
+            rows[:, J:].rearrange("p (a t o i) -> p o a t i", a=3, t=PACK, i=16),
             ws_raw[:].rearrange("p a (o i t) -> p o a t i", t=PACK, i=16),
         )
+        nc.vector.tensor_copy(rows[:, :J].bitcast(I32), v2_s_rows[:].bitcast(I32))
+        planes = held("planes", [P, 2, J + 3 * N], U8)
         for q in range(4):
-            nc.sync.dma_start(
-                ws[32 * q : 32 * q + 4, :, :, :].rearrange("p d a n -> p d (a n)").bitcast(I32),
-                ws_dealt[8 * q : 8 * q + 8, :, :].rearrange("p a n -> p (a n)").bitcast(I32),
-            )
-        wgo_sb = held("wgo_sb", [P, J], F32, tag="v2_s_rows")
+            nc.scalar.dma_start(planes[32 * q : 32 * q + 4, :, :].bitcast(I32), rows[8 * q : 8 * q + 8, :].bitcast(I32))
+        wgo_sb = held("wgo_sb", [P, J], F32)
         nc.sync.dma_start(wgo_sb[:], wgo)
-        w4 = held("w4", [P, W_PASSES, 2 * N], U8, tag="ws_raw")
+
+        both, v2_w, v_w, v_s = {}, {}, {}, {}
+
+        def text_words(h):
+            both[h] = held("both%d" % h, [P, HALF], U32, tag="wv_raw" if h == 1 else "")
+            nc.vector.tensor_copy(both[h][:], tab2_w[:].bitcast(U32).indirect(list2[:, list_cols(h)]))
+
+        def part_words(h):
+            v2_w[h] = held("v2_w%d" % h, [P, 2, 2 * HALF], U8)
+            nc.vector.tensor_copy(
+                v2_w[h][:].bitcast(U16).rearrange("p d (o i) -> p o d i", i=8),
+                both[h][:].bitcast(U16).rearrange("p (o i d) -> p o d i", d=2, i=8),
+            )
+
+        def picture_words(h, offset):
+            v_w[h] = at_byte("v_w%d" % h, [P, HALF], U32, offset)
+            nc.vector.tensor_copy(v_w[h][:], tab_w[:].bitcast(U32).indirect(list1[:, list_cols(h)]))
+
+        def picture_scales(h, offset):
+            v_s[h] = at_byte("v_s%d" % h, [P, HALF], U8, offset)
+            nc.vector.tensor_copy(v_s[h][:], tab_s[:].indirect(list1[:, list_cols(h)]))
+
+        w4 = held("w4", [P, W_PASSES, 2 * N], U8)
         nc.vector.tensor_copy(
             w4[:].bitcast(U16).rearrange("p a (t o i) -> p o a t i", t=PACK, i=8),
             w_raw[:].bitcast(U16).rearrange("p a (o i t) -> p o a t i", t=PACK, i=8),
         )
+        page[1] = at_byte("page1", [P, T], F32, RAW_AT + 64 - PAGE_BYTES)
+        nc.gpsimd.memset(page[1][:], 0.0)
+        text_words(0)
+        picture_scales(0, RAW_AT + 1024)
+        part_words(0)
         nc.scalar.copy(
             wv_bf[:].rearrange("p (t m i) -> p m t i", t=PACK, i=PACK),
             wv_raw[:].rearrange("p i (m t) -> p m t i", t=PACK),
         )
-        wv_w = held("wv_w", [P, N], U32, tag="w_raw")
+        text_words(1)
+        wv_w = held("wv_w", [P, N], U32)
+        wv_s = held("wv_s", [P, N], U8)
         nc.vector.quantize_mx(out=wv_w[:].bitcast(FP8X4), scales=wv_s[:], in_=wv_bf[:])
-        page[2] = held("page2", [P, T], F32)
+        part_words(1)
+        page[2] = at_byte("page2", [P, T], F32, CAST_AT + 4096 - 64)
         nc.gpsimd.memset(page[2][:], 0.0)
+        page[3] = page[0]
+        picture_words(0, CAST_AT + 64 - WORD_BYTES)
+        picture_scales(1, CAST_AT + 64)
+        picture_words(1, CAST_AT + 1024)
 
-        v_w, v_s = [], []
-        for h in range(HALVES):
-            words = held("v_w%d" % h, [P, HALF], U32)
-            nc.vector.tensor_copy(words[:], tab_w[:].bitcast(U32).indirect(list1[:, list_cols(h)]))
-            scales = held("v_s%d" % h, [P, HALF], U8, tag="tab2_s" if h == 1 else "")
-            nc.vector.tensor_copy(scales[:], tab_s[:].indirect(list1[:, list_cols(h)]))
-            v_w.append(words)
-            v_s.append(scales)
-
-        page[3] = held("page3", [P, T], F32, tag="v2_both0")
-        nc.gpsimd.memset(page[3][:], 0.0)
         plane_of = {ZV: (0, 2), ZT: (0, 0), ZT + 1: (1, 0), WT: (0, 1), WT + 1: (1, 1)}
 
         def w4_pass(a, t):
-            return dict(
-                lhsT=w4[:, a, 2 * P * t : 2 * P * (t + 1)].bitcast(FP4X4),
-                lhsT_scale=ws[:, plane_of[a][0], plane_of[a][1], P * t : P * (t + 1)],
-            )
+            first = J + plane_of[a][1] * N + P * t
+            return w4[:, a, 2 * P * t : 2 * P * (t + 1)].bitcast(FP4X4), planes[:, plane_of[a][0], first : first + P]
+
+        def wv_pass(t):
+            return wv_w[:, P * t : P * (t + 1)].bitcast(FP8X4), wv_s[:, P * t : P * (t + 1)]
 
         def v_pass(h):
-            return dict(rhs=v_w[h][:].bitcast(FP8X4), rhs_scale=v_s[h][:])
+            return v_w[h][:].bitcast(FP8X4), v_s[h][:]
 
         def v2_pass(h, d):
-            return dict(rhs=v2_w[h][:, d, :].bitcast(FP4X4), rhs_scale=v2_s[:, d, h * HALF : (h + 1) * HALF])
+            return v2_w[h][:, d, :].bitcast(FP4X4), planes[:, d, half_cols(h)]
 
         def mm(out, left, right, start, stop):
-            nc.tensor.matmul_mx(out=out, lhsT=left["lhsT"], lhsT_scale=left["lhsT_scale"], rhs=right["rhs"], rhs_scale=right["rhs_scale"], start=start, stop=stop)
+            nc.tensor.matmul_mx(out=out[:], lhsT=left[0], lhsT_scale=left[1], rhs=right[0], rhs_scale=right[1], start=start, stop=stop)
 
-        units = [(t, h) for t in range(PACK) for h in range(HALVES)]
-        summed = {}
-        last = len(units) - 1
+        units = [(2 * g + e, h) for g in range(PACK // 2) for h in range(HALVES) for e in range(2)]
+        taken = {"scalar": 0, "vector": 0}
 
-        def mix(u):
+        def bank(reader):
+            n = taken[reader] % BANKS[reader]
+            taken[reader] = taken[reader] + 1
+            return psum.tile([P, HALF], F32, name="bank", tag="%s_bank%d" % (reader, n))
+
+        def unit_tile(name, u):
+            return held("%s%d" % (name, u), [P, HALF], F32)
+
+        gate, text, picture, result = {}, {}, {}, {}
+
+        banks, rest = {}, {}
+
+        def vector_steps(u):
+            tag = "picture%d" % AFTER.get(u, u)
+            if ROADS[u] == "T":
+                products = held("products%d" % u, [P, 2, HALF], F32, tag=tag)
+                picture[u], text[u] = products[:, 0, :], products[:, 1, :]
+                nc.vector.scalar_tensor_tensor(picture[u][:], banks["hv", u][:], 0.0, gate[u][:], ALU.max, ALU.mult)
+                nc.vector.scalar_tensor_tensor(text[u][:], banks["ht", u][:], 0.0, rest[u][:], ALU.max, ALU.mult)
+            else:
+                picture[u] = held("picture%d" % u, [P, HALF], F32, tag=tag)
+                nc.vector.scalar_tensor_tensor(picture[u][:], banks["hv", u][:], 0.0, text[u][:], ALU.max, ALU.subtract)
+
+        def text_sum(u):
             t, h = units[u]
-            gate = held("gate%d" % u, [P, HALF], F32)
-            other = held("other%d" % u, [P, HALF], F32)
-            slot = 2 if u == 0 else u % 2
-            part_v = held("part_v%d" % slot, [P, HALF], F32)
-            part_t = held("part_t%d" % slot, [P, HALF], F32)
-            both = ring.tile([P, HALF], F32, name="both")
+            ht = bank("vector" if ROADS[u] == "T" else "scalar")
+            banks["ht", u] = ht
+            mm(ht, w4_pass(WT, t), v2_pass(h, 0), True, False)
+            mm(ht, w4_pass(WT + 1, t), v2_pass(h, 1), False, True)
+            if ROADS[u] != "T":
+                text[u] = unit_tile("text", u)
+                nc.scalar.activation(text[u][:], ht[:], ACT.Relu)
 
-            def gate_of(tag):
-                z = psum.tile([P, HALF], F32, name=tag, bufs=2)
-                mm(z[:], w4_pass(ZT, t), v2_pass(h, 0), True, False)
-                mm(z[:], w4_pass(ZT + 1, t), v2_pass(h, 1), False, False)
-                mm(z[:], w4_pass(ZV, t), v_pass(h), False, True)
-                nc.scalar.activation(gate[:], z[:], ACT.Sigmoid, bias=bias[:, t : t + 1])
-                return z
+        def picture_sum(u):
+            t, h = units[u]
+            hv = bank("scalar" if ROADS[u] == "W" else "vector")
+            banks["hv", u] = hv
+            mm(hv, wv_pass(t), v_pass(h), True, True)
+            if ROADS[u] == "W":
+                picture[u] = unit_tile("picture", u)
+                nc.scalar.activation(picture[u][:], hv[:], ACT.Relu)
+            elif ROADS[u] != "T" and u not in AFTER:
+                vector_steps(u)
 
-            def text_sum(tag):
-                ht = psum.tile([P, HALF], F32, name=tag, bufs=2)
-                mm(ht[:], w4_pass(WT, t), v2_pass(h, 0), True, False)
-                mm(ht[:], w4_pass(WT + 1, t), v2_pass(h, 1), False, True)
-                return ht
+        def gate_sum(u):
+            t, h = units[u]
+            z = bank("scalar")
+            gate[u] = unit_tile("gate", u)
+            mm(z, w4_pass(ZT, t), v2_pass(h, 0), True, False)
+            mm(z, w4_pass(ZT + 1, t), v2_pass(h, 1), False, False)
+            mm(z, w4_pass(ZV, t), v_pass(h), False, True)
+            nc.scalar.activation(gate[u][:], z[:], ACT.Sigmoid, bias=bias[:, t : t + 1])
+            if ROADS[u] == "T":
+                rest[u] = unit_tile("rest", u)
+                nc.scalar.activation(rest[u][:], gate[u][:], ACT.Copy, bias=1.0, scale=-1.0)
+                if u not in AFTER:
+                    vector_steps(u)
 
-            def picture_sum(hv):
-                left = dict(lhsT=wv_w[:, P * t : P * (t + 1)].bitcast(FP8X4), lhsT_scale=wv_s[:, P * t : P * (t + 1)])
-                mm(hv[:], left, v_pass(h), True, True)
-                return hv
+        part = {}
 
-            if h == 0:
-                z = gate_of("z_hv")
-                ht = text_sum("ht")
-                hv = picture_sum(z)
-                nc.scalar.activation(other[:], gate[:], ACT.Copy, bias=1.0, scale=-1.0)
-                nc.vector.scalar_tensor_tensor(part_v[:], hv[:], 0.0, gate[:], ALU.max, ALU.mult)
-                nc.vector.scalar_tensor_tensor(part_t[:], ht[:], 0.0, other[:], ALU.max, ALU.mult)
-                adder = nc.vector if u == 0 else nc.gpsimd
-                adder.tensor_tensor(both[:], part_v[:], part_t[:], ALU.add)
+        def gate_step(u):
+            part[u] = ring.tile([P, HALF], F32, name="part")
+            if ROADS[u] == "W":
+                nc.gpsimd.tensor_tensor(picture[u][:], picture[u][:], text[u][:], ALU.subtract)
+            if ROADS[u] != "T":
+                nc.gpsimd.tensor_tensor(part[u][:], picture[u][:], gate[u][:], ALU.mult)
+
+        def add_step(u):
+            first = picture[u] if ROADS[u] == "T" else part[u]
+            nc.gpsimd.tensor_tensor(part[u][:], first[:], text[u][:], ALU.add)
+
+        def weigh_step(u):
+            t, h = units[u]
+            if ROADS[u] == "E":
+                result[u] = part[u]
             else:
-                ht = text_sum("brief")
-                nc.scalar.activation(other[:], ht[:], ACT.Relu)
-                hv = picture_sum(psum.tile([P, HALF], F32, name="hv", bufs=2))
-                gate_of("brief")
-                nc.vector.scalar_tensor_tensor(part_v[:], hv[:], 0.0, other[:], ALU.max, ALU.subtract)
-                nc.gpsimd.tensor_tensor(part_t[:], part_v[:], gate[:], ALU.mult)
-                nc.gpsimd.tensor_tensor(both[:], part_t[:], other[:], ALU.add)
-            if u == last:
-                summed[u] = both
-            else:
-                summed[u] = ring.tile([P, HALF], F32, name="summed")
-                nc.gpsimd.tensor_tensor(summed[u][:], both[:], wgo_sb[:, h * HALF : (h + 1) * HALF], ALU.mult)
+                result[u] = picture[u]
+                nc.gpsimd.tensor_tensor(result[u][:], part[u][:], wgo_sb[:, half_cols(h)], ALU.mult)
 
-        grouped = [held("grouped%d" % c, [P, CHUNK_WIDTHS[c], PACK], BF16) for c in range(CHUNKS)]
         out_rows = out_0.rearrange("(p t) c -> t p c", t=PACK)
 
-        def scatter(u):
+        def place(u):
             t, h = units[u]
-            cols = slice(h * LIST_COLS, (h + 1) * LIST_COLS)
-            if u == last:
-                nc.vector.tensor_tensor(page[t][:].indirect(list1[:, cols]), summed[u][:], wgo_sb[:, h * HALF : (h + 1) * HALF], ALU.mult)
+            window = page[t][:].indirect(list1[:, list_cols(h)])
+            if ROADS[u] in "FE":
+                nc.vector.tensor_tensor(window, result[u][:], wgo_sb[:, half_cols(h)], ALU.mult)
             else:
-                nc.vector.tensor_copy(page[t][:].indirect(list1[:, cols]), summed[u][:])
+                nc.vector.tensor_copy(window, result[u][:])
             if h == HALVES - 1:
                 nc.sync.dma_start(out_rows[t], page[t][:])
 
-        def round_page(t):
-            if True:
-                for c in range(CHUNKS):
-                    rows = page[t][:, CHUNK_COLS[c]]
-                    if c < VECTOR_CHUNKS and t == PACK - 2:
-                        nc.scalar.copy(grouped[c][:, :, t : t + 2], rows.unsqueeze(2).to_broadcast([P, CHUNK_WIDTHS[c], 2]))
-                    elif c < VECTOR_CHUNKS and t == PACK - 1:
-                        nc.vector.tensor_copy(grouped[c][:, :, t], rows)
-                    else:
-                        nc.scalar.copy(grouped[c][:, :, t], rows)
+        pairs = {}
 
-        for u in range(len(units) + LAG):
-            if u < len(units):
-                mix(u)
-            if u >= LAG:
-                scatter(u - LAG)
-        for t in range(PACK):
-            round_page(t)
+        def round_page(t):
+            for c in range(CHUNKS):
+                rows = page[t][:, CHUNK_COLS[c]]
+                words = pairs[c][:, t // 2, :, :]
+                if c < VECTOR_CHUNKS and t == PACK - 2:
+                    nc.scalar.copy(words, rows.unsqueeze(2).to_broadcast([P, CHUNK_WIDTHS[c], 2]))
+                elif c < VECTOR_CHUNKS and t == PACK - 1:
+                    nc.vector.tensor_copy(words[:, :, t % 2], rows)
+                else:
+                    nc.scalar.copy(words[:, :, t % 2], rows)
+
+        for u in (0, 4, 5):
+            text_sum(u)
+        picture_sum(0)
+        gate_sum(0)
+        picture_sum(4)
+        picture_sum(5)
+        text_sum(1)
+        picture_sum(1)
+        gate_sum(1)
+        for u in (6, 7):
+            text_sum(u)
+            picture_sum(u)
+        for u in (2, 3):
+            text_sum(u)
+            picture_sum(u)
+            gate_sum(u)
+        for u in (4, 5, 6, 7):
+            gate_sum(u)
+        for c, operand in enumerate(("w4", "planes", "v2_w1", "v2_w0", "wv_w")):
+            pairs[c] = held("pairs%d" % c, [P, 2, CHUNK_WIDTHS[c], 2], BF16, tag=operand)
+        for u, (t, h) in enumerate(units):
+            gate_step(u)
+            add_step(u)
+            weigh_step(u)
+            place(u)
+            for later, first in AFTER.items():
+                if first == u:
+                    vector_steps(later)
+            if h == HALVES - 1:
+                round_page(t)
+        grouped = [held("grouped%d" % c, [P, CHUNK_WIDTHS[c], PACK], BF16) for c in range(CHUNKS)]
+        for c in range(CHUNKS):
+            word = I32 if c < VECTOR_CHUNKS else U32
+            woven = grouped[c][:].rearrange("p c i -> p (c i)").bitcast(word).rearrange("p (c a) -> p c a", a=2)
+            parts = pairs[c][:].rearrange("p a c i -> p a (c i)").bitcast(word).rearrange("p a c -> p c a")
+            if c < VECTOR_CHUNKS:
+                nc.vector.tensor_copy(woven, parts)
+            else:
+                nc.scalar.copy(woven, parts)
 
         y_s = held("y_s", [P, T], U8)
         out_words = out_1[0].rearrange("p c i -> p (c i)").bitcast(I32)

@@ -1,6 +1,7 @@
 from contextlib import ExitStack
 
 import concourse.mybir as mybir
+from concourse.masks import make_identity
 
 K, L, N, T, J = 512, 1024, 512, 2048, 1024
 FLOPS = 2 * J * N * (2 * K + 2 * L)
@@ -20,20 +21,19 @@ P = 128
 PACK = 4
 HALF = 512
 HALVES = J // HALF
+BLOCKS = HALF // P
 LIST_COLS = HALF // 16
-CHUNK_WIDTHS = (512, 512, 512, 256, 256)
-CHUNKS = len(CHUNK_WIDTHS)
-CHUNK_COLS = [slice(sum(CHUNK_WIDTHS[:c]), sum(CHUNK_WIDTHS[: c + 1])) for c in range(CHUNKS)]
-ZV, ZT, WT = 0, 1, 3
-W_PASSES = 5
+CHUNK = 512
+CHUNKS = T // CHUNK
+PIECES = ((0, 0, 512), (1, 0, 512), (2, 0, 512), (3, 0, 256), (3, 256, 256))
 VECTOR_CHUNKS = 2
-BANKS = {"scalar": 4, "vector": 4}
-ROADS = "WTTTXXXE"
-AFTER = {3: 0}
+MX_BANKS = 6
+UNITS = ((0, 0), (1, 0), (0, 1), (2, 0), (1, 1), (2, 1), (3, 0), (3, 1))
 PAGE_BYTES = 4 * T
-WORD_BYTES = 4 * HALF
-RAW_AT = PAGE_BYTES
-CAST_AT = RAW_AT + 8192
+ROWS_AT = PAGE_BYTES
+BOTH_AT = ROWS_AT + 1024 + PAGE_BYTES
+CAST_AT = BOTH_AT + 2048 + 2048
+LAST_AT = CAST_AT + 4096 + PAGE_BYTES + 4096
 
 
 def tile_list_gmu_relu_scatP_kernel(
@@ -44,7 +44,7 @@ def tile_list_gmu_relu_scatP_kernel(
     with ExitStack() as ctx:
         keep = ctx.enter_context(tc.tile_pool(name="keep", bufs=1))
         placed = ctx.enter_context(tc.tile_pool(name="placed", bufs=1))
-        ring = ctx.enter_context(tc.tile_pool(name="ring", bufs=1))
+        ring = ctx.enter_context(tc.tile_pool(name="ring", bufs=3))
         psum = ctx.enter_context(tc.psum_pool(name="psum", bufs=1))
 
         def held(name, shape, dtype, tag=""):
@@ -53,41 +53,56 @@ def tile_list_gmu_relu_scatP_kernel(
         def at_byte(name, shape, dtype, offset):
             return placed.tile(shape, dtype, name=name, tag=name, align_bytes=64, offset=offset)
 
+        def bank(tag):
+            return psum.tile([P, HALF], F32, name="bank", tag=tag)
+
         list1 = held("list1", [P, J // 16], U16)
         list2 = held("list2", [P, J // 16], U16)
         tab_s = held("tab_s", [P, T], U8)
-        tab2_s = held("tab2_s", [P, T], U8, tag="tab_w")
+        tab2_s = held("tab2_s", [P, T], U8)
         tab2_w = held("tab2_w", [P, T], I32)
-        ws_raw = held("ws_raw", [P, 3, N], U8)
-        w_raw = at_byte("w_raw", [P, W_PASSES, 2 * N], U8, RAW_AT)
+        ws_raw = held("ws_raw", [P, 3 * N], U8)
+        raw = {"zt": held("zt_raw", [P, 2, 2 * N], U8), "wt": held("wt_raw", [P, 2, 2 * N], U8), "zv": held("zv_raw", [P, 1, 2 * N], U8)}
         wv_raw = held("wv_raw", [P, PACK, N], F32)
         wv_bf = at_byte("wv_bf", [P, N * PACK], BF16, CAST_AT)
         bias = held("bias", [P, PACK], F32)
+        w_rows = held("w_rows", [P, P], F32)
+        ident = held("ident", [P, P], F32)
         page = {0: held("page0", [P, T], F32)}
+        warm = held("warm", [P, 8], F32)
 
-        nc.vector.memset(ws_raw[:].bitcast(I32), 0)
+        nc.vector.memset(ws_raw[:, 2 * N :].bitcast(I32), 0)
         nc.vector.memset(tab_s[:].bitcast(I32), 0)
-        nc.vector.memset(tab2_s[32:64, :].bitcast(I32), 0)
-        nc.vector.memset(tab2_s[64:128, :].bitcast(I32), 0)
-        nc.vector.memset(page[0][:], 0.0)
+        for rows32 in (slice(32, 64), slice(64, 128)):
+            nc.gpsimd.memset(tab2_s[rows32, :].bitcast(I32), 0)
+            nc.gpsimd.memset(ws_raw[rows32, : 2 * N].bitcast(I32), 0)
+        nc.vector.memset(warm[:], 0.0)
+        nc.gpsimd.memset(page[0][:], 0.0)
+        nc.gpsimd.memset(w_rows[:], 0.0)
 
         nc.sync.dma_start(list2[:], offs2)
         nc.sync.dma_start(tab2_s[0:32, :].bitcast(I32), tab2_scales.rearrange("a q t -> q a t").bitcast(I32))
-        nc.sync.dma_start(tab2_w[:], tab2_words[0].rearrange("p t i -> p (t i)").bitcast(I32))
+        nc.scalar.dma_start(ws_raw[0:32, 0:N].bitcast(I32), zt_scales.rearrange("a q n -> q a n").bitcast(I32))
+        nc.scalar.dma_start(ws_raw[0:32, N : 2 * N].bitcast(I32), wt_scales.rearrange("a q n -> q a n").bitcast(I32))
+        nc.scalar.dma_start(ws_raw[0:32:2, 2 * N :].bitcast(I32), zv_scales[0].bitcast(I32))
         nc.sync.dma_start(list1[:], offs)
-        nc.sync.dma_start(wv_raw[:], wv.rearrange("(p i) n -> p i n", i=PACK))
-        nc.sync.dma_start(bias[:], b.rearrange("(p t) -> p t", t=PACK))
-        nc.scalar.dma_start(ws_raw[0:32, 0, :].bitcast(I32), zt_scales.rearrange("a q n -> q a n").bitcast(I32))
-        nc.scalar.dma_start(ws_raw[0:32, 1, :].bitcast(I32), wt_scales.rearrange("a q n -> q a n").bitcast(I32))
-        nc.scalar.dma_start(ws_raw[0:32:2, 2, :].bitcast(I32), zv_scales[0].bitcast(I32))
-        for first, words in ((ZT, zt_words), (WT, wt_words), (ZV, zv_words)):
-            passes = words.shape[0]
-            nc.scalar.dma_start(w_raw[:, first : first + passes, :].bitcast(I32), words.rearrange("a p n -> p a n").bitcast(I32))
+        words_in = {"zt": zt_words, "wt": wt_words, "zv": zv_words}
+
+        def load_words(name):
+            nc.sync.dma_start(raw[name][:].bitcast(I32), words_in[name].rearrange("a p n -> p a n").bitcast(I32))
+
+        load_words("zv")
+        nc.sync.dma_start(tab2_w[:], tab2_words[0].rearrange("p t i -> p (t i)").bitcast(I32))
+        load_words("wt")
         for q in range(4):
             nc.scalar.dma_start(tab_s[32 * q : 32 * q + 4, :].bitcast(I32), tab_scales[0, 4 * q : 4 * q + 4, :].bitcast(I32))
+        load_words("zt")
+        nc.sync.dma_start(wv_raw[:], wv.rearrange("(p i) n -> p i n", i=PACK))
+        nc.sync.dma_start(w_rows[0 : J // P, :], wgo[0].rearrange("(c p) -> c p", p=P))
+        nc.sync.dma_start(bias[:], b.rearrange("(p t) -> p t", t=PACK))
+        make_identity(nc, ident[:])
 
-        warm = held("warm", [P, 8], F32)
-        nc.scalar.activation(warm[:, 0:1], page[0][:, 0:1], ACT.Sigmoid)
+        nc.scalar.activation(warm[:, 0:1], warm[:, 1:2], ACT.Sigmoid)
 
         def list_cols(h):
             return slice(h * LIST_COLS, (h + 1) * LIST_COLS)
@@ -95,30 +110,58 @@ def tile_list_gmu_relu_scatP_kernel(
         def half_cols(h):
             return slice(h * HALF, (h + 1) * HALF)
 
-        v2_s_rows = held("v2_s_rows", [P, J], U8)
+        def block(k):
+            return slice(k * P, (k + 1) * P)
+
+        v2_s_rows = at_byte("v2_s_rows", [P, J], U8, ROWS_AT)
         nc.vector.tensor_copy(v2_s_rows[:], tab2_s[:].indirect(list2[:]))
-        tab_w = held("tab_w", [P, T], I32)
-        nc.sync.dma_start(tab_w[:], tab_words[0].rearrange("p t i -> p (t i)").bitcast(I32))
-        rows = held("rows", [P, J + 3 * N], U8, tag="wgo_sb")
+        rows = held("rows", [P, J + 3 * N], U8, tag="tab2_s")
         nc.vector.tensor_copy(
             rows[:, J:].rearrange("p (a t o i) -> p o a t i", a=3, t=PACK, i=16),
-            ws_raw[:].rearrange("p a (o i t) -> p o a t i", t=PACK, i=16),
+            ws_raw[:].rearrange("p (a o i t) -> p o a t i", a=3, t=PACK, i=16),
         )
         nc.vector.tensor_copy(rows[:, :J].bitcast(I32), v2_s_rows[:].bitcast(I32))
         planes = held("planes", [P, 2, J + 3 * N], U8)
         for q in range(4):
-            nc.scalar.dma_start(planes[32 * q : 32 * q + 4, :, :].bitcast(I32), rows[8 * q : 8 * q + 8, :].bitcast(I32))
-        wgo_sb = held("wgo_sb", [P, J], F32)
-        nc.sync.dma_start(wgo_sb[:], wgo)
+            nc.sync.dma_start(planes[32 * q : 32 * q + 4, :, :].bitcast(I32), rows[8 * q : 8 * q + 8, :].bitcast(I32))
+
+        tab_w = at_byte("tab_w", [P, T], I32, ROWS_AT + 1024 - 64)
+        nc.sync.dma_start(tab_w[:], tab_words[0].rearrange("p t i -> p (t i)").bitcast(I32))
+
+        dealt = {}
+
+        def deal(name):
+            dealt[name] = held(name + "_dealt", [P, raw[name].shape[1], 2 * N], U8)
+            nc.scalar.copy(
+                dealt[name][:].bitcast(U16).rearrange("p a (t o i) -> p o a t i", t=PACK, i=8),
+                raw[name][:].bitcast(U16).rearrange("p a (o i t) -> p o a t i", t=PACK, i=8),
+            )
+
+        deal("wt")
+        deal("zt")
+        nc.scalar.copy(
+            wv_bf[:].rearrange("p (t m i) -> p m t i", t=PACK, i=PACK),
+            wv_raw[:].rearrange("p i (m t) -> p m t i", t=PACK),
+        )
+
+        deal("zv")
+
+        w_bank = bank("mx0")
+        nc.tensor.transpose(w_bank[:, 0:P], w_rows[:], ident[:])
+        w_cols = held("w_cols", [P, J // P], F32)
+        nc.scalar.copy(w_cols[:], w_bank[:, 0 : J // P])
+        w_wide = bank("back")
+        for k in range(BLOCKS):
+            nc.tensor.transpose(w_wide[:, block(k)], w_cols[:, k : k + 1].to_broadcast([P, P]), ident[:])
 
         both, v2_w, v_w, v_s = {}, {}, {}, {}
 
-        def text_words(h):
-            both[h] = held("both%d" % h, [P, HALF], U32, tag="wv_raw" if h == 1 else "")
+        def text_words(h, offset):
+            both[h] = at_byte("both%d" % h, [P, HALF], U32, offset)
             nc.vector.tensor_copy(both[h][:], tab2_w[:].bitcast(U32).indirect(list2[:, list_cols(h)]))
 
-        def part_words(h):
-            v2_w[h] = held("v2_w%d" % h, [P, 2, 2 * HALF], U8)
+        def part_words(h, tile):
+            v2_w[h] = tile
             nc.vector.tensor_copy(
                 v2_w[h][:].bitcast(U16).rearrange("p d (o i) -> p o d i", i=8),
                 both[h][:].bitcast(U16).rearrange("p (o i d) -> p o d i", d=2, i=8),
@@ -132,40 +175,30 @@ def tile_list_gmu_relu_scatP_kernel(
             v_s[h] = at_byte("v_s%d" % h, [P, HALF], U8, offset)
             nc.vector.tensor_copy(v_s[h][:], tab_s[:].indirect(list1[:, list_cols(h)]))
 
-        w4 = held("w4", [P, W_PASSES, 2 * N], U8)
-        nc.vector.tensor_copy(
-            w4[:].bitcast(U16).rearrange("p a (t o i) -> p o a t i", t=PACK, i=8),
-            w_raw[:].bitcast(U16).rearrange("p a (o i t) -> p o a t i", t=PACK, i=8),
-        )
-        page[1] = at_byte("page1", [P, T], F32, RAW_AT + 64 - PAGE_BYTES)
+        page[1] = at_byte("page1", [P, T], F32, ROWS_AT + 64 - PAGE_BYTES)
         nc.gpsimd.memset(page[1][:], 0.0)
-        text_words(0)
-        picture_scales(0, RAW_AT + 1024)
-        part_words(0)
-        nc.scalar.copy(
-            wv_bf[:].rearrange("p (t m i) -> p m t i", t=PACK, i=PACK),
-            wv_raw[:].rearrange("p i (m t) -> p m t i", t=PACK),
-        )
-        text_words(1)
+        picture_scales(0, ROWS_AT + 64)
+        text_words(0, BOTH_AT)
+        part_words(0, held("v2_w0", [P, 2, 2 * HALF], U8))
+        picture_scales(1, BOTH_AT + 64)
         wv_w = held("wv_w", [P, N], U32)
         wv_s = held("wv_s", [P, N], U8)
         nc.vector.quantize_mx(out=wv_w[:].bitcast(FP8X4), scales=wv_s[:], in_=wv_bf[:])
-        part_words(1)
         page[2] = at_byte("page2", [P, T], F32, CAST_AT + 4096 - 64)
         nc.gpsimd.memset(page[2][:], 0.0)
-        page[3] = page[0]
-        picture_words(0, CAST_AT + 64 - WORD_BYTES)
-        picture_scales(1, CAST_AT + 64)
-        picture_words(1, CAST_AT + 1024)
+        picture_words(0, CAST_AT + 64 - 2048)
+        picture_words(1, CAST_AT + 64)
+        text_words(1, ROWS_AT + 1024)
+        part_words(1, held("v2_w1", [P, 2, 2 * HALF], U8))
 
-        plane_of = {ZV: (0, 2), ZT: (0, 0), ZT + 1: (1, 0), WT: (0, 1), WT + 1: (1, 1)}
+        scale_run = {"zt": 0, "wt": 1, "zv": 2}
 
-        def w4_pass(a, t):
-            first = J + plane_of[a][1] * N + P * t
-            return w4[:, a, 2 * P * t : 2 * P * (t + 1)].bitcast(FP4X4), planes[:, plane_of[a][0], first : first + P]
+        def w4_pass(name, a, t):
+            first = J + scale_run[name] * N + P * t
+            return dealt[name][:, a, 2 * P * t : 2 * P * (t + 1)].bitcast(FP4X4), planes[:, a, first : first + P]
 
         def wv_pass(t):
-            return wv_w[:, P * t : P * (t + 1)].bitcast(FP8X4), wv_s[:, P * t : P * (t + 1)]
+            return wv_w[:, block(t)].bitcast(FP8X4), wv_s[:, block(t)]
 
         def v_pass(h):
             return v_w[h][:].bitcast(FP8X4), v_s[h][:]
@@ -176,158 +209,149 @@ def tile_list_gmu_relu_scatP_kernel(
         def mm(out, left, right, start, stop):
             nc.tensor.matmul_mx(out=out[:], lhsT=left[0], lhsT_scale=left[1], rhs=right[0], rhs_scale=right[1], start=start, stop=stop)
 
-        units = [(2 * g + e, h) for g in range(PACK // 2) for h in range(HALVES) for e in range(2)]
-        taken = {"scalar": 0, "vector": 0}
+        taken = [0]
 
-        def bank(reader):
-            n = taken[reader] % BANKS[reader]
-            taken[reader] = taken[reader] + 1
-            return psum.tile([P, HALF], F32, name="bank", tag="%s_bank%d" % (reader, n))
+        def mx_bank():
+            taken[0] = taken[0] + 1
+            return bank("mx%d" % (taken[0] % MX_BANKS))
 
-        def unit_tile(name, u):
-            return held("%s%d" % (name, u), [P, HALF], F32)
-
-        gate, text, picture, result = {}, {}, {}, {}
-
-        banks, rest = {}, {}
-
-        def vector_steps(u):
-            tag = "picture%d" % AFTER.get(u, u)
-            if ROADS[u] == "T":
-                products = held("products%d" % u, [P, 2, HALF], F32, tag=tag)
-                picture[u], text[u] = products[:, 0, :], products[:, 1, :]
-                nc.vector.scalar_tensor_tensor(picture[u][:], banks["hv", u][:], 0.0, gate[u][:], ALU.max, ALU.mult)
-                nc.vector.scalar_tensor_tensor(text[u][:], banks["ht", u][:], 0.0, rest[u][:], ALU.max, ALU.mult)
-            else:
-                picture[u] = held("picture%d" % u, [P, HALF], F32, tag=tag)
-                nc.vector.scalar_tensor_tensor(picture[u][:], banks["hv", u][:], 0.0, text[u][:], ALU.max, ALU.subtract)
-
-        def text_sum(u):
-            t, h = units[u]
-            ht = bank("vector" if ROADS[u] == "T" else "scalar")
-            banks["ht", u] = ht
-            mm(ht, w4_pass(WT, t), v2_pass(h, 0), True, False)
-            mm(ht, w4_pass(WT + 1, t), v2_pass(h, 1), False, True)
-            if ROADS[u] != "T":
-                text[u] = unit_tile("text", u)
-                nc.scalar.activation(text[u][:], ht[:], ACT.Relu)
-
-        def picture_sum(u):
-            t, h = units[u]
-            hv = bank("scalar" if ROADS[u] == "W" else "vector")
-            banks["hv", u] = hv
-            mm(hv, wv_pass(t), v_pass(h), True, True)
-            if ROADS[u] == "W":
-                picture[u] = unit_tile("picture", u)
-                nc.scalar.activation(picture[u][:], hv[:], ACT.Relu)
-            elif ROADS[u] != "T" and u not in AFTER:
-                vector_steps(u)
-
-        def gate_sum(u):
-            t, h = units[u]
-            z = bank("scalar")
-            gate[u] = unit_tile("gate", u)
-            mm(z, w4_pass(ZT, t), v2_pass(h, 0), True, False)
-            mm(z, w4_pass(ZT + 1, t), v2_pass(h, 1), False, False)
-            mm(z, w4_pass(ZV, t), v_pass(h), False, True)
-            nc.scalar.activation(gate[u][:], z[:], ACT.Sigmoid, bias=bias[:, t : t + 1])
-            if ROADS[u] == "T":
-                rest[u] = unit_tile("rest", u)
-                nc.scalar.activation(rest[u][:], gate[u][:], ACT.Copy, bias=1.0, scale=-1.0)
-                if u not in AFTER:
-                    vector_steps(u)
-
-        part = {}
-
-        def gate_step(u):
-            part[u] = ring.tile([P, HALF], F32, name="part")
-            if ROADS[u] == "W":
-                nc.gpsimd.tensor_tensor(picture[u][:], picture[u][:], text[u][:], ALU.subtract)
-            if ROADS[u] != "T":
-                nc.gpsimd.tensor_tensor(part[u][:], picture[u][:], gate[u][:], ALU.mult)
-
-        def add_step(u):
-            first = picture[u] if ROADS[u] == "T" else part[u]
-            nc.gpsimd.tensor_tensor(part[u][:], first[:], text[u][:], ALU.add)
-
-        def weigh_step(u):
-            t, h = units[u]
-            if ROADS[u] == "E":
-                result[u] = part[u]
-            else:
-                result[u] = picture[u]
-                nc.gpsimd.tensor_tensor(result[u][:], part[u][:], wgo_sb[:, half_cols(h)], ALU.mult)
-
+        last = len(UNITS) - 1
         out_rows = out_0.rearrange("(p t) c -> t p c", t=PACK)
 
+        def unit_tile(name, u):
+            if u == last and name in ("gate", "picture"):
+                return at_byte(name, [P, HALF], F32, LAST_AT + (0 if name == "gate" else 2048 + 8192))
+            return held("%s%d" % (name, u), [P, HALF], F32)
+
+        text, gate, picture, gated, weighed, result = {}, {}, {}, {}, {}, {}
+
+        def text_sum(u):
+            t, h = UNITS[u]
+            text[u] = unit_tile("text", u)
+            ht = mx_bank()
+            mm(ht, w4_pass("wt", 0, t), v2_pass(h, 0), True, False)
+            mm(ht, w4_pass("wt", 1, t), v2_pass(h, 1), False, True)
+            nc.scalar.activation(text[u][:], ht[:], ACT.Relu)
+
+        def picture_sum(u, hv):
+            t, h = UNITS[u]
+            picture[u] = unit_tile("picture", u)
+            mm(hv, wv_pass(t), v_pass(h), True, True)
+
+        def gate_sum(u):
+            t, h = UNITS[u]
+            gate[u] = unit_tile("gate", u)
+            z = mx_bank()
+            mm(z, w4_pass("zt", 0, t), v2_pass(h, 0), True, False)
+            mm(z, w4_pass("zt", 1, t), v2_pass(h, 1), False, False)
+            mm(z, w4_pass("zv", 0, t), v_pass(h), False, True)
+            nc.scalar.activation(gate[u][:], z[:], ACT.Sigmoid, bias=bias[:, t : t + 1])
+
         def place(u):
-            t, h = units[u]
-            window = page[t][:].indirect(list1[:, list_cols(h)])
-            if ROADS[u] in "FE":
-                nc.vector.tensor_tensor(window, result[u][:], wgo_sb[:, half_cols(h)], ALU.mult)
-            else:
-                nc.vector.tensor_copy(window, result[u][:])
+            t, h = UNITS[u]
+            nc.vector.tensor_copy(page[t][:].indirect(list1[:, list_cols(h)]), result[u][:])
             if h == HALVES - 1:
                 nc.sync.dma_start(out_rows[t], page[t][:])
 
-        pairs = {}
+        def first_unit():
+            hv = bank("turned")
+            picture_sum(0, hv)
+            gate_sum(0)
+            result[0] = unit_tile("result", 0)
+            parts = (slice(0, HALF // 2), slice(HALF // 2, HALF))
+            for c in parts:
+                nc.vector.scalar_tensor_tensor(picture[0][:, c], hv[:, c], 0.0, text[0][:, c], ALU.max, ALU.subtract)
+            for c in parts:
+                nc.vector.tensor_tensor(picture[0][:, c], picture[0][:, c], gate[0][:, c], ALU.mult)
+            for c in parts:
+                nc.vector.tensor_tensor(picture[0][:, c], picture[0][:, c], text[0][:, c], ALU.add)
+            for c in parts:
+                nc.vector.tensor_tensor(result[0][:, c], picture[0][:, c], w_wide[:, c], ALU.mult)
+            place(0)
 
-        def round_page(t):
-            for c in range(CHUNKS):
-                rows = page[t][:, CHUNK_COLS[c]]
-                words = pairs[c][:, t // 2, :, :]
-                if c < VECTOR_CHUNKS and t == PACK - 2:
-                    nc.scalar.copy(words, rows.unsqueeze(2).to_broadcast([P, CHUNK_WIDTHS[c], 2]))
-                elif c < VECTOR_CHUNKS and t == PACK - 1:
-                    nc.vector.tensor_copy(words[:, :, t % 2], rows)
-                else:
-                    nc.scalar.copy(words[:, :, t % 2], rows)
+        def mix(u):
+            hv = mx_bank()
+            picture_sum(u, hv)
+            nc.scalar.activation(picture[u][:], hv[:], ACT.Relu)
+            nc.gpsimd.tensor_tensor(picture[u][:], picture[u][:], text[u][:], ALU.subtract)
+            gate_sum(u)
+            gated[u] = ring.tile([P, HALF], F32, name="gated")
+            nc.gpsimd.tensor_tensor(gated[u][:], picture[u][:], gate[u][:], ALU.mult)
 
-        for u in (0, 4, 5):
-            text_sum(u)
-        picture_sum(0)
-        gate_sum(0)
-        picture_sum(4)
-        picture_sum(5)
-        text_sum(1)
-        picture_sum(1)
-        gate_sum(1)
-        for u in (6, 7):
-            text_sum(u)
-            picture_sum(u)
-        for u in (2, 3):
-            text_sum(u)
-            picture_sum(u)
-            gate_sum(u)
-        for u in (4, 5, 6, 7):
-            gate_sum(u)
-        for c, operand in enumerate(("w4", "planes", "v2_w1", "v2_w0", "wv_w")):
-            pairs[c] = held("pairs%d" % c, [P, 2, CHUNK_WIDTHS[c], 2], BF16, tag=operand)
-        for u, (t, h) in enumerate(units):
-            gate_step(u)
-            add_step(u)
-            weigh_step(u)
+        def weigh(u):
+            t, h = UNITS[u]
+            turned = bank("turned")
+            for k in range(BLOCKS):
+                nc.tensor.matmul(turned[:, block(k)], gated[u][:, block(k)], ident[:], start=True, stop=False, is_transpose=True)
+                nc.tensor.matmul(turned[:, block(k)], text[u][:, block(k)], ident[:], start=False, stop=True, is_transpose=True)
+            if u == last:
+                weighed[u] = [pairs[k][:, 2 * CHUNK : 2 * CHUNK + 2 * P].bitcast(F32) for k in range(BLOCKS)]
+            else:
+                whole = ring.tile([P, HALF], F32, name="weighed")
+                weighed[u] = [whole[:, block(k)] for k in range(BLOCKS)]
+            for k in range(BLOCKS):
+                col = h * BLOCKS + k
+                nc.scalar.activation(weighed[u][k], turned[:, block(k)], ACT.Copy, scale=w_cols[:, col : col + 1])
+
+        def turn_back(u):
+            back = bank("back")
+            for k in range(BLOCKS):
+                nc.tensor.transpose(back[:, block(k)], weighed[u][k], ident[:])
+            result[u] = unit_tile("result", u)
+            nc.scalar.copy(result[u][:], back[:])
             place(u)
-            for later, first in AFTER.items():
-                if first == u:
-                    vector_steps(later)
-            if h == HALVES - 1:
-                round_page(t)
-        grouped = [held("grouped%d" % c, [P, CHUNK_WIDTHS[c], PACK], BF16) for c in range(CHUNKS)]
-        for c in range(CHUNKS):
+
+        pair_at = (LAST_AT + 64 - 4096, LAST_AT + 2048 - 64, LAST_AT + 2048 + 8192 + 64 - 4096, LAST_AT + 4096 + 8192 - 64)
+        pairs = []
+        text_sum(1)
+        text_sum(0)
+        for u in range(1, last + 3):
+            if u <= last:
+                mix(u)
+            if u == 1:
+                first_unit()
+                page[3] = held("page3", [P, T], F32, tag="picture0")
+            if u == last:
+                pairs.extend(at_byte("pairs%d" % c, [P, 4 * CHUNK], BF16, pair_at[c]) for c in range(CHUNKS))
+            if u < last:
+                text_sum(u + 1)
+            if u >= 3:
+                turn_back(u - 2)
+            if 2 <= u <= last + 1:
+                weigh(u - 1)
+            if 2 <= u < 2 + CHUNKS:
+                nc.gpsimd.memset(page[3][:, (u - 2) * CHUNK : (u - 1) * CHUNK], 0.0)
+
+        for t in range(PACK):
+            for c in range(CHUNKS):
+                rows_f32 = page[t][:, c * CHUNK : (c + 1) * CHUNK]
+                words = pairs[c][:, t // 2 * 2 * CHUNK : (t // 2 + 1) * 2 * CHUNK].rearrange("p (c i) -> p c i", i=2)
+                if t < 2:
+                    nc.gpsimd.tensor_scalar(words[:, :, t], rows_f32, 1.0, -0.0, ALU.mult, ALU.add)
+                elif c < VECTOR_CHUNKS and t == PACK - 2:
+                    nc.scalar.copy(words, rows_f32.unsqueeze(2).to_broadcast([P, CHUNK, 2]))
+                elif c < VECTOR_CHUNKS:
+                    nc.vector.tensor_copy(words[:, :, 1], rows_f32)
+                else:
+                    nc.scalar.copy(words[:, :, t % 2], rows_f32)
+
+        y_s = held("y_s", [P, T], U8)
+        out_words = out_1[0].rearrange("p c i -> p (c i)").bitcast(I32)
+        spare = ("tab2_w", "wv_raw", "tab2_s", "zt_raw", "wt_raw")
+        grouped = []
+        for n, (c, first, width) in enumerate(PIECES):
+            grouped.append(held("grouped%d" % n, [P, width, PACK], BF16, tag=spare[n]))
             word = I32 if c < VECTOR_CHUNKS else U32
-            woven = grouped[c][:].rearrange("p c i -> p (c i)").bitcast(word).rearrange("p (c a) -> p c a", a=2)
-            parts = pairs[c][:].rearrange("p a c i -> p a (c i)").bitcast(word).rearrange("p a c -> p c a")
+            woven = grouped[n][:].rearrange("p c i -> p (c i)").bitcast(word).rearrange("p (c a) -> p c a", a=2)
+            parts = pairs[c][:].bitcast(word).rearrange("p (a c) -> p c a", a=2)[:, first : first + width, :]
             if c < VECTOR_CHUNKS:
                 nc.vector.tensor_copy(woven, parts)
             else:
                 nc.scalar.copy(woven, parts)
-
-        y_s = held("y_s", [P, T], U8)
-        out_words = out_1[0].rearrange("p c i -> p (c i)").bitcast(I32)
-        for c in range(CHUNKS):
-            y_w = held("y_w%d" % c, [P, CHUNK_WIDTHS[c]], I32)
-            nc.vector.quantize_mx(out=y_w[:].bitcast(FP8X4), scales=y_s[:, CHUNK_COLS[c]], in_=grouped[c][:].rearrange("p c i -> p (c i)"))
-            nc.sync.dma_start(out_words[:, CHUNK_COLS[c]], y_w[:])
+        for n, (c, first, width) in enumerate(PIECES):
+            cols = slice(c * CHUNK + first, c * CHUNK + first + width)
+            y_w = held("y_w%d" % n, [P, width], I32)
+            nc.vector.quantize_mx(out=y_w[:].bitcast(FP8X4), scales=y_s[:, cols], in_=grouped[n][:].rearrange("p c i -> p (c i)"))
+            nc.sync.dma_start(out_words[:, cols], y_w[:])
         for q in range(4):
             nc.scalar.dma_start(out_2[0, 4 * q : 4 * q + 4, :].bitcast(I32), y_s[32 * q : 32 * q + 4, :].bitcast(I32))

@@ -94,8 +94,8 @@ def tile_list_gmu_relu_scatP_kernel(
         load_words("zv")
         nc.sync.dma_start(tab2_w[:], tab2_words[0].rearrange("p t i -> p (t i)").bitcast(I32))
         load_words("wt")
-        for q in range(4):
-            nc.scalar.dma_start(tab_s[32 * q : 32 * q + 4, :].bitcast(I32), tab_scales[0, 4 * q : 4 * q + 4, :].bitcast(I32))
+        for r in range(4):
+            nc.scalar.dma_start(tab_s[r:P:32, :].bitcast(I32), tab_scales[0, r:16:4, :].bitcast(I32))
         load_words("zt")
         nc.sync.dma_start(wv_raw[:], wv.rearrange("(p i) n -> p i n", i=PACK))
         nc.sync.dma_start(w_rows[0 : J // P, :], wgo[0].rearrange("(c p) -> c p", p=P))
@@ -123,7 +123,8 @@ def tile_list_gmu_relu_scatP_kernel(
         nc.vector.tensor_copy(rows[:, :J].bitcast(I32), v2_s_rows[:].bitcast(I32))
         planes = held("planes", [P, 2, J + 3 * N], U8)
         for q in range(4):
-            nc.sync.dma_start(planes[32 * q : 32 * q + 4, :, :].bitcast(I32), rows[8 * q : 8 * q + 8, :].bitcast(I32))
+            queue = nc.sync if q < 2 else nc.scalar
+            queue.dma_start(planes[32 * q : 32 * q + 4, :, :].bitcast(I32), rows[8 * q : 8 * q + 8, :].bitcast(I32))
 
         tab_w = at_byte("tab_w", [P, T], I32, ROWS_AT + 1024 - 64)
         nc.sync.dma_start(tab_w[:], tab_words[0].rearrange("p t i -> p (t i)").bitcast(I32))
@@ -353,5 +354,5 @@ def tile_list_gmu_relu_scatP_kernel(
             y_w = held("y_w%d" % n, [P, width], I32)
             nc.vector.quantize_mx(out=y_w[:].bitcast(FP8X4), scales=y_s[:, cols], in_=grouped[n][:].rearrange("p c i -> p (c i)"))
             nc.sync.dma_start(out_words[:, cols], y_w[:])
-        for q in range(4):
-            nc.scalar.dma_start(out_2[0, 4 * q : 4 * q + 4, :].bitcast(I32), y_s[32 * q : 32 * q + 4, :].bitcast(I32))
+        for r in range(4):
+            nc.scalar.dma_start(out_2[0, r:16:4, :].bitcast(I32), y_s[r:P:32, :].bitcast(I32))

@@ -31,8 +31,8 @@ MX_BANKS = 6
 UNITS = ((0, 0), (1, 0), (0, 1), (2, 0), (1, 1), (2, 1), (3, 0), (3, 1))
 PAGE_BYTES = 4 * T
 ROWS_AT = PAGE_BYTES
-BOTH_AT = ROWS_AT + 1024 + PAGE_BYTES
-CAST_AT = BOTH_AT + 2048 + 2048
+BOTH_AT = ROWS_AT + 1024 + 2 * PAGE_BYTES
+CAST_AT = BOTH_AT + 3072 + 4096
 LAST_AT = CAST_AT + 4096 + PAGE_BYTES + 4096
 
 
@@ -168,8 +168,8 @@ def tile_list_gmu_relu_scatP_kernel(
                 both[h][:].bitcast(U16).rearrange("p (o i d) -> p o d i", d=2, i=8),
             )
 
-        def picture_words(h, offset):
-            v_w[h] = at_byte("v_w%d" % h, [P, HALF], U32, offset)
+        def picture_words(h, tile):
+            v_w[h] = tile[:, half_cols(h)]
             nc.vector.tensor_copy(v_w[h][:], tab_w[:].bitcast(U32).indirect(list1[:, list_cols(h)]))
 
         def picture_scales(h, offset):
@@ -181,16 +181,19 @@ def tile_list_gmu_relu_scatP_kernel(
         picture_scales(0, ROWS_AT + 64)
         text_words(0, BOTH_AT)
         part_words(0, held("v2_w0", [P, 2, 2 * HALF], U8))
+        page[3] = at_byte("page3", [P, T], F32, BOTH_AT + 64 - PAGE_BYTES)
+        nc.gpsimd.memset(page[3][:], 0.0)
         picture_scales(1, BOTH_AT + 64)
+        text_words(1, BOTH_AT + 1024)
         wv_w = held("wv_w", [P, N], U32)
         wv_s = held("wv_s", [P, N], U8)
         nc.vector.quantize_mx(out=wv_w[:].bitcast(FP8X4), scales=wv_s[:], in_=wv_bf[:])
         page[2] = at_byte("page2", [P, T], F32, CAST_AT + 4096 - 64)
         nc.gpsimd.memset(page[2][:], 0.0)
-        picture_words(0, CAST_AT + 64 - 2048)
-        picture_words(1, CAST_AT + 64)
-        text_words(1, ROWS_AT + 1024)
-        part_words(1, held("v2_w1", [P, 2, 2 * HALF], U8))
+        picked = at_byte("picked", [P, J], U32, CAST_AT + 64 - 4096)
+        picture_words(0, picked)
+        picture_words(1, picked)
+        part_words(1, at_byte("v2_w1", [P, 2, 2 * HALF], U8, CAST_AT + 64))
 
         scale_run = {"zt": 0, "wt": 1, "zv": 2}
 
@@ -311,7 +314,6 @@ def tile_list_gmu_relu_scatP_kernel(
                 mix(u)
             if u == 1:
                 first_unit()
-                page[3] = held("page3", [P, T], F32, tag="picture0")
             if u == last:
                 pairs.extend(at_byte("pairs%d" % c, [P, 4 * CHUNK], BF16, pair_at[c]) for c in range(CHUNKS))
             if u < last:
@@ -320,18 +322,17 @@ def tile_list_gmu_relu_scatP_kernel(
                 turn_back(u - 2)
             if 2 <= u <= last + 1:
                 weigh(u - 1)
-            if 2 <= u < 2 + CHUNKS:
-                nc.gpsimd.memset(page[3][:, (u - 2) * CHUNK : (u - 1) * CHUNK], 0.0)
 
         for t in range(PACK):
             for c in range(CHUNKS):
                 rows_f32 = page[t][:, c * CHUNK : (c + 1) * CHUNK]
                 words = pairs[c][:, t // 2 * 2 * CHUNK : (t // 2 + 1) * 2 * CHUNK].rearrange("p (c i) -> p c i", i=2)
-                if t < 2:
-                    nc.gpsimd.tensor_scalar(words[:, :, t], rows_f32, 1.0, -0.0, ALU.mult, ALU.add)
+                twice = rows_f32.unsqueeze(2).to_broadcast([P, CHUNK, 2])
+                if t == 0:
+                    nc.gpsimd.tensor_scalar(words, twice, 1.0, -0.0, ALU.mult, ALU.add)
                 elif c < VECTOR_CHUNKS and t == PACK - 2:
-                    nc.scalar.copy(words, rows_f32.unsqueeze(2).to_broadcast([P, CHUNK, 2]))
-                elif c < VECTOR_CHUNKS:
+                    nc.scalar.copy(words, twice)
+                elif c < VECTOR_CHUNKS and t == PACK - 1:
                     nc.vector.tensor_copy(words[:, :, 1], rows_f32)
                 else:
                     nc.scalar.copy(words[:, :, t % 2], rows_f32)

@@ -28,7 +28,8 @@ CHUNKS = T // CHUNK
 PIECES = ((0, 0, 512), (1, 0, 512), (2, 0, 512), (3, 0, 256), (3, 256, 256))
 VECTOR_CHUNKS = 2
 MX_BANKS = 6
-UNITS = ((0, 0), (1, 0), (0, 1), (2, 0), (1, 1), (2, 1), (3, 0), (3, 1))
+UNITS = ((0, 0), (1, 0), (2, 0), (0, 1), (1, 1), (2, 1), (3, 0), (3, 1))
+VECTOR_UNITS = 2
 PAGE_BYTES = 4 * T
 ROWS_AT = PAGE_BYTES
 BOTH_AT = ROWS_AT + 1024 + 2 * PAGE_BYTES
@@ -257,37 +258,41 @@ def tile_list_gmu_relu_scatP_kernel(
             if h == HALVES - 1:
                 nc.sync.dma_start(out_rows[t], page[t][:])
 
-        def first_unit():
-            hv = bank("turned")
-            picture_sum(0, hv)
-            gate_sum(0)
-            result[0] = unit_tile("result", 0)
+        def vector_unit(u, hv):
+            picture_sum(u, hv)
+            gate_sum(u)
+            result[u] = unit_tile("result", u)
             parts = (slice(0, HALF // 2), slice(HALF // 2, HALF))
             for c in parts:
-                nc.vector.scalar_tensor_tensor(picture[0][:, c], hv[:, c], 0.0, text[0][:, c], ALU.max, ALU.subtract)
+                nc.vector.scalar_tensor_tensor(picture[u][:, c], hv[:, c], 0.0, text[u][:, c], ALU.max, ALU.subtract)
             for c in parts:
-                nc.vector.tensor_tensor(picture[0][:, c], picture[0][:, c], gate[0][:, c], ALU.mult)
+                nc.vector.tensor_tensor(picture[u][:, c], picture[u][:, c], gate[u][:, c], ALU.mult)
             for c in parts:
-                nc.vector.tensor_tensor(picture[0][:, c], picture[0][:, c], text[0][:, c], ALU.add)
+                nc.vector.tensor_tensor(picture[u][:, c], picture[u][:, c], text[u][:, c], ALU.add)
             for c in parts:
-                nc.vector.tensor_tensor(result[0][:, c], picture[0][:, c], w_wide[:, c], ALU.mult)
-            place(0)
+                nc.vector.tensor_tensor(result[u][:, c], picture[u][:, c], w_wide[:, c], ALU.mult)
 
-        def mix(u):
+        def difference(u):
             hv = mx_bank()
             picture_sum(u, hv)
             nc.scalar.activation(picture[u][:], hv[:], ACT.Relu)
             nc.gpsimd.tensor_tensor(picture[u][:], picture[u][:], text[u][:], ALU.subtract)
+
+        def product(u):
             gate_sum(u)
             gated[u] = ring.tile([P, HALF], F32, name="gated")
             nc.gpsimd.tensor_tensor(gated[u][:], picture[u][:], gate[u][:], ALU.mult)
 
+        turned, back = {}, {}
+
+        def turn(u):
+            turned[u] = bank("turned")
+            for k in range(BLOCKS):
+                nc.tensor.matmul(turned[u][:, block(k)], gated[u][:, block(k)], ident[:], start=True, stop=False, is_transpose=True)
+                nc.tensor.matmul(turned[u][:, block(k)], text[u][:, block(k)], ident[:], start=False, stop=True, is_transpose=True)
+
         def weigh(u):
             t, h = UNITS[u]
-            turned = bank("turned")
-            for k in range(BLOCKS):
-                nc.tensor.matmul(turned[:, block(k)], gated[u][:, block(k)], ident[:], start=True, stop=False, is_transpose=True)
-                nc.tensor.matmul(turned[:, block(k)], text[u][:, block(k)], ident[:], start=False, stop=True, is_transpose=True)
             if u == last:
                 weighed[u] = [pairs[k][:, 2 * CHUNK : 2 * CHUNK + 2 * P].bitcast(F32) for k in range(BLOCKS)]
             else:
@@ -295,33 +300,41 @@ def tile_list_gmu_relu_scatP_kernel(
                 weighed[u] = [whole[:, block(k)] for k in range(BLOCKS)]
             for k in range(BLOCKS):
                 col = h * BLOCKS + k
-                nc.scalar.activation(weighed[u][k], turned[:, block(k)], ACT.Copy, scale=w_cols[:, col : col + 1])
-
-        def turn_back(u):
-            back = bank("back")
+                nc.scalar.activation(weighed[u][k], turned[u][:, block(k)], ACT.Copy, scale=w_cols[:, col : col + 1])
+            back[u] = bank("back")
             for k in range(BLOCKS):
-                nc.tensor.transpose(back[:, block(k)], weighed[u][k], ident[:])
+                nc.tensor.transpose(back[u][:, block(k)], weighed[u][k], ident[:])
+
+        def hand_over(u):
             result[u] = unit_tile("result", u)
-            nc.scalar.copy(result[u][:], back[:])
+            nc.scalar.copy(result[u][:], back[u][:])
             place(u)
 
         pair_at = (LAST_AT + 64 - 4096, LAST_AT + 2048 - 64, LAST_AT + 2048 + 8192 + 64 - 4096, LAST_AT + 4096 + 8192 - 64)
         pairs = []
-        text_sum(1)
-        text_sum(0)
-        for u in range(1, last + 3):
-            if u <= last:
-                mix(u)
-            if u == 1:
-                first_unit()
+        first = VECTOR_UNITS
+        for u in (first, 0, 1):
+            text_sum(u)
+        difference(first)
+        vector_unit(0, bank("turned"))
+        product(first)
+        vector_unit(1, mx_bank())
+        place(0)
+        place(1)
+        for u in range(first, last + 3):
+            if u - 2 >= first:
+                weigh(u - 2)
+            if first < u <= last:
+                difference(u)
+                product(u)
             if u == last:
                 pairs.extend(at_byte("pairs%d" % c, [P, 4 * CHUNK], BF16, pair_at[c]) for c in range(CHUNKS))
             if u < last:
                 text_sum(u + 1)
-            if u >= 3:
-                turn_back(u - 2)
-            if 2 <= u <= last + 1:
-                weigh(u - 1)
+            if u - 2 >= first:
+                hand_over(u - 2)
+            if first <= u - 1 <= last:
+                turn(u - 1)
 
         for t in range(PACK):
             for c in range(CHUNKS):
@@ -330,6 +343,8 @@ def tile_list_gmu_relu_scatP_kernel(
                 twice = rows_f32.unsqueeze(2).to_broadcast([P, CHUNK, 2])
                 if t == 0:
                     nc.gpsimd.tensor_scalar(words, twice, 1.0, -0.0, ALU.mult, ALU.add)
+                elif t == 1 and c >= VECTOR_CHUNKS:
+                    nc.gpsimd.tensor_scalar(words[:, :, 1], rows_f32, 1.0, -0.0, ALU.mult, ALU.add)
                 elif c < VECTOR_CHUNKS and t == PACK - 2:
                     nc.scalar.copy(words, twice)
                 elif c < VECTOR_CHUNKS and t == PACK - 1:

@@ -30,11 +30,13 @@ VECTOR_CHUNKS = 2
 MX_BANKS = 6
 UNITS = ((0, 0), (1, 0), (2, 0), (0, 1), (1, 1), (2, 1), (3, 0), (3, 1))
 VECTOR_UNITS = 2
+ROUNDING_ORDER = (2, 3, 0, 1)
 PAGE_BYTES = 4 * T
 ROWS_AT = PAGE_BYTES
 BOTH_AT = ROWS_AT + 1024 + 2 * PAGE_BYTES
-CAST_AT = BOTH_AT + 3072 + 4096
-LAST_AT = CAST_AT + 4096 + PAGE_BYTES + 4096
+LAST_AT = BOTH_AT + 4096 + PAGE_BYTES + 4096
+WV_AT = ROWS_AT + 1024 - 64
+SCALES_AT = LAST_AT + 16384 + 2560
 
 
 def tile_list_gmu_relu_scatP_kernel(
@@ -60,12 +62,11 @@ def tile_list_gmu_relu_scatP_kernel(
         list1 = held("list1", [P, J // 16], U16)
         list2 = held("list2", [P, J // 16], U16)
         tab_s = held("tab_s", [P, T], U8)
-        tab2_s = held("tab2_s", [P, T], U8)
+        tab2_s = at_byte("tab2_s", [P, T], U8, SCALES_AT)
         tab2_w = held("tab2_w", [P, T], I32)
+        tab_w = held("tab_w", [P, T], I32)
         ws_raw = held("ws_raw", [P, 3 * N], U8)
         raw = {"zt": held("zt_raw", [P, 2, 2 * N], U8), "wt": held("wt_raw", [P, 2, 2 * N], U8), "zv": held("zv_raw", [P, 1, 2 * N], U8)}
-        wv_raw = held("wv_raw", [P, PACK, N], F32)
-        wv_bf = at_byte("wv_bf", [P, N * PACK], BF16, CAST_AT)
         bias = held("bias", [P, PACK], F32)
         w_rows = held("w_rows", [P, P], F32)
         ident = held("ident", [P, P], F32)
@@ -78,30 +79,30 @@ def tile_list_gmu_relu_scatP_kernel(
             nc.gpsimd.memset(tab2_s[rows32, :].bitcast(I32), 0)
             nc.gpsimd.memset(ws_raw[rows32, : 2 * N].bitcast(I32), 0)
         nc.vector.memset(warm[:], 0.0)
+        nc.vector.memset(w_rows[:], 0.0)
+        make_identity(nc, ident[:])
         nc.gpsimd.memset(page[0][:], 0.0)
-        nc.gpsimd.memset(w_rows[:], 0.0)
 
         nc.sync.dma_start(list2[:], offs2)
         nc.sync.dma_start(tab2_s[0:32, :].bitcast(I32), tab2_scales.rearrange("a q t -> q a t").bitcast(I32))
         nc.scalar.dma_start(ws_raw[0:32, 0:N].bitcast(I32), zt_scales.rearrange("a q n -> q a n").bitcast(I32))
         nc.scalar.dma_start(ws_raw[0:32, N : 2 * N].bitcast(I32), wt_scales.rearrange("a q n -> q a n").bitcast(I32))
         nc.scalar.dma_start(ws_raw[0:32:2, 2 * N :].bitcast(I32), zv_scales[0].bitcast(I32))
+        nc.scalar.dma_start(w_rows[0 : J // P, :], wgo[0].rearrange("(c p) -> c p", p=P))
         nc.sync.dma_start(list1[:], offs)
         words_in = {"zt": zt_words, "wt": wt_words, "zv": zv_words}
 
         def load_words(name):
             nc.sync.dma_start(raw[name][:].bitcast(I32), words_in[name].rearrange("a p n -> p a n").bitcast(I32))
 
-        load_words("zv")
         nc.sync.dma_start(tab2_w[:], tab2_words[0].rearrange("p t i -> p (t i)").bitcast(I32))
+        nc.sync.dma_start(tab_w[:], tab_words[0].rearrange("p t i -> p (t i)").bitcast(I32))
         load_words("wt")
         for r in range(4):
             nc.scalar.dma_start(tab_s[r:P:32, :].bitcast(I32), tab_scales[0, r:16:4, :].bitcast(I32))
         load_words("zt")
-        nc.sync.dma_start(wv_raw[:], wv.rearrange("(p i) n -> p i n", i=PACK))
-        nc.sync.dma_start(w_rows[0 : J // P, :], wgo[0].rearrange("(c p) -> c p", p=P))
+        load_words("zv")
         nc.sync.dma_start(bias[:], b.rearrange("(p t) -> p t", t=PACK))
-        make_identity(nc, ident[:])
 
         nc.scalar.activation(warm[:, 0:1], warm[:, 1:2], ACT.Sigmoid)
 
@@ -116,19 +117,26 @@ def tile_list_gmu_relu_scatP_kernel(
 
         v2_s_rows = at_byte("v2_s_rows", [P, J], U8, ROWS_AT)
         nc.vector.tensor_copy(v2_s_rows[:], tab2_s[:].indirect(list2[:]))
-        rows = held("rows", [P, J + 3 * N], U8, tag="tab2_s")
+        rows = at_byte("rows", [P, J + 3 * N], U8, SCALES_AT + 64 - (J + 3 * N))
         nc.vector.tensor_copy(
             rows[:, J:].rearrange("p (a t o i) -> p o a t i", a=3, t=PACK, i=16),
             ws_raw[:].rearrange("p (a o i t) -> p o a t i", a=3, t=PACK, i=16),
         )
         nc.vector.tensor_copy(rows[:, :J].bitcast(I32), v2_s_rows[:].bitcast(I32))
         planes = held("planes", [P, 2, J + 3 * N], U8)
-        for q in range(4):
-            queue = nc.sync if q < 2 else nc.scalar
-            queue.dma_start(planes[32 * q : 32 * q + 4, :, :].bitcast(I32), rows[8 * q : 8 * q + 8, :].bitcast(I32))
+        for q in (0, 2, 1, 3):
+            nc.sync.dma_start(planes[32 * q : 32 * q + 4, :, :].bitcast(I32), rows[8 * q : 8 * q + 8, :].bitcast(I32))
 
-        tab_w = at_byte("tab_w", [P, T], I32, ROWS_AT + 1024 - 64)
-        nc.sync.dma_start(tab_w[:], tab_words[0].rearrange("p t i -> p (t i)").bitcast(I32))
+        wv_raw = at_byte("wv_raw", [P, PACK, N], F32, WV_AT)
+        nc.sync.dma_start(wv_raw[:], wv.rearrange("(p i) n -> p i n", i=PACK))
+
+        w_bank = bank("mx0")
+        nc.tensor.transpose(w_bank[:, 0:P], w_rows[:], ident[:])
+        w_cols = held("w_cols", [P, J // P], F32)
+        nc.scalar.copy(w_cols[:], w_bank[:, 0 : J // P])
+        w_wide = bank("back")
+        for k in range(BLOCKS):
+            nc.tensor.transpose(w_wide[:, block(k)], w_cols[:, k : k + 1].to_broadcast([P, P]), ident[:])
 
         dealt = {}
 
@@ -141,60 +149,40 @@ def tile_list_gmu_relu_scatP_kernel(
 
         deal("wt")
         deal("zt")
-        nc.scalar.copy(
-            wv_bf[:].rearrange("p (t m i) -> p m t i", t=PACK, i=PACK),
-            wv_raw[:].rearrange("p i (m t) -> p m t i", t=PACK),
-        )
-
         deal("zv")
-
-        w_bank = bank("mx0")
-        nc.tensor.transpose(w_bank[:, 0:P], w_rows[:], ident[:])
-        w_cols = held("w_cols", [P, J // P], F32)
-        nc.scalar.copy(w_cols[:], w_bank[:, 0 : J // P])
-        w_wide = bank("back")
-        for k in range(BLOCKS):
-            nc.tensor.transpose(w_wide[:, block(k)], w_cols[:, k : k + 1].to_broadcast([P, P]), ident[:])
-
-        both, v2_w, v_w, v_s = {}, {}, {}, {}
-
-        def text_words(h, offset):
-            both[h] = at_byte("both%d" % h, [P, HALF], U32, offset)
-            nc.vector.tensor_copy(both[h][:], tab2_w[:].bitcast(U32).indirect(list2[:, list_cols(h)]))
-
-        def part_words(h, tile):
-            v2_w[h] = tile
-            nc.vector.tensor_copy(
-                v2_w[h][:].bitcast(U16).rearrange("p d (o i) -> p o d i", i=8),
-                both[h][:].bitcast(U16).rearrange("p (o i d) -> p o d i", d=2, i=8),
-            )
-
-        def picture_words(h, tile):
-            v_w[h] = tile[:, half_cols(h)]
-            nc.vector.tensor_copy(v_w[h][:], tab_w[:].bitcast(U32).indirect(list1[:, list_cols(h)]))
-
-        def picture_scales(h, offset):
-            v_s[h] = at_byte("v_s%d" % h, [P, HALF], U8, offset)
-            nc.vector.tensor_copy(v_s[h][:], tab_s[:].indirect(list1[:, list_cols(h)]))
 
         page[1] = at_byte("page1", [P, T], F32, ROWS_AT + 64 - PAGE_BYTES)
         nc.gpsimd.memset(page[1][:], 0.0)
-        picture_scales(0, ROWS_AT + 64)
-        text_words(0, BOTH_AT)
-        part_words(0, held("v2_w0", [P, 2, 2 * HALF], U8))
+        both = at_byte("both", [P, J], U32, BOTH_AT)
+        nc.vector.tensor_copy(both[:], tab2_w[:].bitcast(U32).indirect(list2[:]))
+        v2_w, v_w = {}, {}
+        for h in range(HALVES):
+            v2_w[h] = held("v2_w%d" % h, [P, 2, 2 * HALF], U8)
+            nc.vector.tensor_copy(
+                v2_w[h][:].bitcast(U16).rearrange("p d (o i) -> p o d i", i=8),
+                both[:, half_cols(h)].bitcast(U16).rearrange("p (o i d) -> p o d i", d=2, i=8),
+            )
         page[3] = at_byte("page3", [P, T], F32, BOTH_AT + 64 - PAGE_BYTES)
         nc.gpsimd.memset(page[3][:], 0.0)
-        picture_scales(1, BOTH_AT + 64)
-        text_words(1, BOTH_AT + 1024)
-        wv_w = held("wv_w", [P, N], U32)
-        wv_s = held("wv_s", [P, N], U8)
-        nc.vector.quantize_mx(out=wv_w[:].bitcast(FP8X4), scales=wv_s[:], in_=wv_bf[:])
-        page[2] = at_byte("page2", [P, T], F32, CAST_AT + 4096 - 64)
+        page[2] = at_byte("page2", [P, T], F32, BOTH_AT + 4096 - 64)
         nc.gpsimd.memset(page[2][:], 0.0)
-        picked = at_byte("picked", [P, J], U32, CAST_AT + 64 - 4096)
-        picture_words(0, picked)
-        picture_words(1, picked)
-        part_words(1, at_byte("v2_w1", [P, 2, 2 * HALF], U8, CAST_AT + 64))
+        v_s = at_byte("v_s", [P, J], U8, BOTH_AT + 64)
+        nc.vector.tensor_copy(v_s[:], tab_s[:].indirect(list1[:]))
+        for h in range(HALVES):
+            v_w[h] = held("v_w%d" % h, [P, HALF], U32)
+            nc.vector.tensor_copy(v_w[h][:], tab_w[:].bitcast(U32).indirect(list1[:, list_cols(h)]))
+
+        wv_w, wv_s = {}, {}
+
+        def quantise_wv(g):
+            rounded = held("wv_bf%d" % g, [P, 2 * P * PACK], BF16)
+            nc.scalar.copy(
+                rounded[:].rearrange("p (t m i) -> p m t i", t=2, i=PACK),
+                wv_raw[:].rearrange("p i (m t) -> p m t i", t=PACK)[:, :, 2 * g : 2 * g + 2, :],
+            )
+            wv_w[g] = held("wv_w%d" % g, [P, 2 * P], U32)
+            wv_s[g] = held("wv_s%d" % g, [P, 2 * P], U8)
+            nc.vector.quantize_mx(out=wv_w[g][:].bitcast(FP8X4), scales=wv_s[g][:], in_=rounded[:])
 
         scale_run = {"zt": 0, "wt": 1, "zv": 2}
 
@@ -203,10 +191,10 @@ def tile_list_gmu_relu_scatP_kernel(
             return dealt[name][:, a, 2 * P * t : 2 * P * (t + 1)].bitcast(FP4X4), planes[:, a, first : first + P]
 
         def wv_pass(t):
-            return wv_w[:, block(t)].bitcast(FP8X4), wv_s[:, block(t)]
+            return wv_w[t // 2][:, block(t % 2)].bitcast(FP8X4), wv_s[t // 2][:, block(t % 2)]
 
         def v_pass(h):
-            return v_w[h][:].bitcast(FP8X4), v_s[h][:]
+            return v_w[h][:].bitcast(FP8X4), v_s[:, half_cols(h)]
 
         def v2_pass(h, d):
             return v2_w[h][:, d, :].bitcast(FP4X4), planes[:, d, half_cols(h)]
@@ -226,6 +214,10 @@ def tile_list_gmu_relu_scatP_kernel(
         def unit_tile(name, u):
             if u == last and name in ("gate", "picture"):
                 return at_byte(name, [P, HALF], F32, LAST_AT + (0 if name == "gate" else 2048 + 8192))
+            if u == VECTOR_UNITS and name == "text":
+                return at_byte("text%d" % u, [P, HALF], F32, WV_AT + 64 + 2048 * u)
+            if u < VECTOR_UNITS and name == "gate":
+                return at_byte("gate%d" % u, [P, HALF], F32, WV_AT + 64 + 2048 * u)
             return held("%s%d" % (name, u), [P, HALF], F32)
 
         text, gate, picture, gated, weighed, result = {}, {}, {}, {}, {}, {}
@@ -243,14 +235,21 @@ def tile_list_gmu_relu_scatP_kernel(
             picture[u] = unit_tile("picture", u)
             mm(hv, wv_pass(t), v_pass(h), True, True)
 
+        z = {}
+
+        def open_gate(u):
+            t, h = UNITS[u]
+            z[u] = mx_bank()
+            mm(z[u], w4_pass("zt", 0, t), v2_pass(h, 0), True, False)
+            mm(z[u], w4_pass("zt", 1, t), v2_pass(h, 1), False, False)
+
         def gate_sum(u):
             t, h = UNITS[u]
+            if u not in z:
+                open_gate(u)
             gate[u] = unit_tile("gate", u)
-            z = mx_bank()
-            mm(z, w4_pass("zt", 0, t), v2_pass(h, 0), True, False)
-            mm(z, w4_pass("zt", 1, t), v2_pass(h, 1), False, False)
-            mm(z, w4_pass("zv", 0, t), v_pass(h), False, True)
-            nc.scalar.activation(gate[u][:], z[:], ACT.Sigmoid, bias=bias[:, t : t + 1])
+            mm(z[u], w4_pass("zv", 0, t), v_pass(h), False, True)
+            nc.scalar.activation(gate[u][:], z[u][:], ACT.Sigmoid, bias=bias[:, t : t + 1])
 
         def place(u):
             t, h = UNITS[u]
@@ -258,19 +257,18 @@ def tile_list_gmu_relu_scatP_kernel(
             if h == HALVES - 1:
                 nc.sync.dma_start(out_rows[t], page[t][:])
 
-        def vector_unit(u, hv):
-            picture_sum(u, hv)
-            gate_sum(u)
-            result[u] = unit_tile("result", u)
-            parts = (slice(0, HALF // 2), slice(HALF // 2, HALF))
-            for c in parts:
-                nc.vector.scalar_tensor_tensor(picture[u][:, c], hv[:, c], 0.0, text[u][:, c], ALU.max, ALU.subtract)
-            for c in parts:
-                nc.vector.tensor_tensor(picture[u][:, c], picture[u][:, c], gate[u][:, c], ALU.mult)
-            for c in parts:
-                nc.vector.tensor_tensor(picture[u][:, c], picture[u][:, c], text[u][:, c], ALU.add)
-            for c in parts:
-                nc.vector.tensor_tensor(result[u][:, c], picture[u][:, c], w_wide[:, c], ALU.mult)
+        def vector_units(hv):
+            for u in hv:
+                nc.vector.scalar_tensor_tensor(picture[u][:], hv[u][:], 0.0, text[u][:], ALU.max, ALU.subtract)
+            for u in hv:
+                nc.vector.tensor_tensor(picture[u][:], picture[u][:], gate[u][:], ALU.mult)
+            for u in hv:
+                nc.vector.tensor_tensor(picture[u][:], picture[u][:], text[u][:], ALU.add)
+            for u in hv:
+                result[u] = unit_tile("result", u)
+                nc.vector.tensor_tensor(result[u][:], picture[u][:], w_wide[:], ALU.mult)
+            for u in hv:
+                place(u)
 
         def difference(u):
             hv = mx_bank()
@@ -313,14 +311,23 @@ def tile_list_gmu_relu_scatP_kernel(
         pair_at = (LAST_AT + 64 - 4096, LAST_AT + 2048 - 64, LAST_AT + 2048 + 8192 + 64 - 4096, LAST_AT + 4096 + 8192 - 64)
         pairs = []
         first = VECTOR_UNITS
-        for u in (first, 0, 1):
-            text_sum(u)
+        quantise_wv(0)
+        quantise_wv(1)
+        text_sum(0)
+        text_sum(1)
+        open_gate(0)
+        open_gate(1)
+        for u in range(first):
+            gate_sum(u)
+        text_sum(first)
+        open_gate(first)
+        hv_banks = {0: bank("turned"), 1: mx_bank()}
+        for u in hv_banks:
+            picture_sum(u, hv_banks[u])
+        vector_units(hv_banks)
         difference(first)
-        vector_unit(0, bank("turned"))
         product(first)
-        vector_unit(1, mx_bank())
-        place(0)
-        place(1)
+        text_sum(first + 1)
         for u in range(first, last + 3):
             if u - 2 >= first:
                 weigh(u - 2)
@@ -329,32 +336,38 @@ def tile_list_gmu_relu_scatP_kernel(
                 product(u)
             if u == last:
                 pairs.extend(at_byte("pairs%d" % c, [P, 4 * CHUNK], BF16, pair_at[c]) for c in range(CHUNKS))
-            if u < last:
-                text_sum(u + 1)
+            if u + 2 <= last:
+                text_sum(u + 2)
             if u - 2 >= first:
                 hand_over(u - 2)
             if first <= u - 1 <= last:
                 turn(u - 1)
 
-        for t in range(PACK):
+        def round_page(t, c):
+            rows_f32 = page[t][:, c * CHUNK : (c + 1) * CHUNK]
+            words = pairs[c][:, t // 2 * 2 * CHUNK : (t // 2 + 1) * 2 * CHUNK].rearrange("p (c i) -> p c i", i=2)
+            twice = rows_f32.unsqueeze(2).to_broadcast([P, CHUNK, 2])
+            if t == 0:
+                nc.gpsimd.tensor_scalar(words, twice, 1.0, -0.0, ALU.mult, ALU.add)
+            elif t == 1 and c >= VECTOR_CHUNKS:
+                nc.gpsimd.tensor_scalar(words[:, :, 1], rows_f32, 1.0, -0.0, ALU.mult, ALU.add)
+            elif c < VECTOR_CHUNKS and t == PACK - 2:
+                nc.scalar.copy(words, twice)
+            elif c < VECTOR_CHUNKS and t == PACK - 1:
+                nc.vector.tensor_copy(words[:, :, 1], rows_f32)
+            else:
+                nc.scalar.copy(words[:, :, t % 2], rows_f32)
+
+        for c in ROUNDING_ORDER:
+            round_page(0, c)
+            round_page(1, c)
+        for t in (2, 3):
             for c in range(CHUNKS):
-                rows_f32 = page[t][:, c * CHUNK : (c + 1) * CHUNK]
-                words = pairs[c][:, t // 2 * 2 * CHUNK : (t // 2 + 1) * 2 * CHUNK].rearrange("p (c i) -> p c i", i=2)
-                twice = rows_f32.unsqueeze(2).to_broadcast([P, CHUNK, 2])
-                if t == 0:
-                    nc.gpsimd.tensor_scalar(words, twice, 1.0, -0.0, ALU.mult, ALU.add)
-                elif t == 1 and c >= VECTOR_CHUNKS:
-                    nc.gpsimd.tensor_scalar(words[:, :, 1], rows_f32, 1.0, -0.0, ALU.mult, ALU.add)
-                elif c < VECTOR_CHUNKS and t == PACK - 2:
-                    nc.scalar.copy(words, twice)
-                elif c < VECTOR_CHUNKS and t == PACK - 1:
-                    nc.vector.tensor_copy(words[:, :, 1], rows_f32)
-                else:
-                    nc.scalar.copy(words[:, :, t % 2], rows_f32)
+                round_page(t, c)
 
         y_s = held("y_s", [P, T], U8)
         out_words = out_1[0].rearrange("p c i -> p (c i)").bitcast(I32)
-        spare = ("tab2_w", "wv_raw", "tab2_s", "zt_raw", "wt_raw")
+        spare = ("tab2_w", "text0", "text1", "zt_raw", "wt_raw")
         grouped = []
         for n, (c, first, width) in enumerate(PIECES):
             grouped.append(held("grouped%d" % n, [P, width, PACK], BF16, tag=spare[n]))

@@ -21,22 +21,38 @@ P = 128
 PACK = 4
 HALF = 512
 HALVES = J // HALF
-BLOCKS = HALF // P
-LIST_COLS = HALF // 16
 CHUNK = 512
 CHUNKS = T // CHUNK
-PIECES = ((0, 0, 512), (1, 0, 512), (2, 0, 512), (3, 0, 256), (3, 256, 256))
 VECTOR_CHUNKS = 2
-MX_BANKS = 6
-UNITS = ((0, 0), (1, 0), (2, 0), (0, 1), (1, 1), (2, 1), (3, 0), (3, 1))
-VECTOR_UNITS = 2
-ROUNDING_ORDER = (2, 3, 0, 1)
-PAGE_BYTES = 4 * T
-ROWS_AT = PAGE_BYTES
-BOTH_AT = ROWS_AT + 1024 + 2 * PAGE_BYTES
-LAST_AT = BOTH_AT + 4096 + PAGE_BYTES + 4096
-WV_AT = ROWS_AT + 1024 - 64
-SCALES_AT = LAST_AT + 16384 + 2560
+PIECES = ((0, 0, 512), (1, 0, 512), (2, 0, 512), (3, 0, 256), (3, 256, 256))
+UNITS = tuple((t, h * HALF, HALF) for t, h in ((0, 0), (1, 0), (2, 0), (0, 1), (1, 1), (3, 0), (2, 1), (3, 1)))
+SWAPPED = {("gate", 3): ("turned", 0), ("turned", 2): ("gate", 1), ("picture", 3): ("back", 0), ("back", 2): ("picture", 1)}
+LAP = 64
+PAGE = 4 * T
+ROW = 4 * HALF
+PAIR = 8 * CHUNK
+PAGE0_AT = 0
+WS_AT = PAGE0_AT + PAGE - LAP
+PAGE1_AT = WS_AT + 3 * N
+V2ROWS_AT = PAGE1_AT + PAGE - LAP
+WV_AT = V2ROWS_AT + J - LAP
+BOTH_AT = WV_AT + PAGE
+VS0_AT = BOTH_AT + HALF
+PAGE2_AT = BOTH_AT + 2 * ROW - LAP
+SHARE_AT = PAGE2_AT + PAGE
+ROUND0_AT = SHARE_AT + ROW - LAP
+ROUND1_AT = ROUND0_AT + ROW // 2
+ROUND2_AT = ROUND1_AT + ROW // 2
+VS1_AT = ROUND2_AT + LAP
+VW1_AT = ROUND2_AT + ROW - LAP
+PAGE3_AT = VW1_AT + ROW
+TEXT0_AT = PAGE3_AT + PAGE - LAP
+PAIR0_AT = TEXT0_AT + ROW
+GATE_AT = PAIR0_AT + PAIR - LAP
+PAIR1_AT = GATE_AT + ROW - LAP
+PAIR2_AT = PAIR1_AT + PAIR
+WEIGHED_AT = PAIR2_AT + PAIR - LAP
+PAIR3_AT = WEIGHED_AT + ROW - LAP
 
 
 def tile_list_gmu_relu_scatP_kernel(
@@ -56,58 +72,57 @@ def tile_list_gmu_relu_scatP_kernel(
         def at_byte(name, shape, dtype, offset):
             return placed.tile(shape, dtype, name=name, tag=name, align_bytes=64, offset=offset)
 
-        def bank(tag):
-            return psum.tile([P, HALF], F32, name="bank", tag=tag)
+        def bank(role, u):
+            role, n = SWAPPED.get((role, u), (role, u % 2))
+            return psum.tile([P, HALF], F32, name="bank", tag="%s%d" % (role, n))
 
         list1 = held("list1", [P, J // 16], U16)
         list2 = held("list2", [P, J // 16], U16)
         tab_s = held("tab_s", [P, T], U8)
-        tab2_s = at_byte("tab2_s", [P, T], U8, SCALES_AT)
+        tab2_s = held("tab2_s", [P, T], U8)
         tab2_w = held("tab2_w", [P, T], I32)
         tab_w = held("tab_w", [P, T], I32)
-        ws_raw = held("ws_raw", [P, 3 * N], U8)
-        raw = {"zt": held("zt_raw", [P, 2, 2 * N], U8), "wt": held("wt_raw", [P, 2, 2 * N], U8), "zv": held("zv_raw", [P, 1, 2 * N], U8)}
+        ws_raw = at_byte("ws_raw", [P, 3 * N], U8, WS_AT)
+        raw = {name: held(name + "_raw", [P, passes, 2 * N], U8) for name, passes in (("wt", 2), ("zt", 2), ("zv", 1))}
         bias = held("bias", [P, PACK], F32)
         w_rows = held("w_rows", [P, P], F32)
         ident = held("ident", [P, P], F32)
-        page = {0: held("page0", [P, T], F32)}
         warm = held("warm", [P, 8], F32)
 
+        nc.vector.memset(warm[:], 0.0)
         nc.vector.memset(ws_raw[:, 2 * N :].bitcast(I32), 0)
+        for rows32 in (slice(32, 64), slice(64, 128)):
+            nc.vector.memset(ws_raw[rows32, : 2 * N].bitcast(I32), 0)
         nc.vector.memset(tab_s[:].bitcast(I32), 0)
+        nc.vector.memset(w_rows[:], 0.0)
         for rows32 in (slice(32, 64), slice(64, 128)):
             nc.gpsimd.memset(tab2_s[rows32, :].bitcast(I32), 0)
-            nc.gpsimd.memset(ws_raw[rows32, : 2 * N].bitcast(I32), 0)
-        nc.vector.memset(warm[:], 0.0)
-        nc.vector.memset(w_rows[:], 0.0)
-        make_identity(nc, ident[:])
-        nc.gpsimd.memset(page[0][:], 0.0)
 
-        nc.sync.dma_start(list2[:], offs2)
-        nc.sync.dma_start(tab2_s[0:32, :].bitcast(I32), tab2_scales.rearrange("a q t -> q a t").bitcast(I32))
-        nc.scalar.dma_start(ws_raw[0:32, 0:N].bitcast(I32), zt_scales.rearrange("a q n -> q a n").bitcast(I32))
-        nc.scalar.dma_start(ws_raw[0:32, N : 2 * N].bitcast(I32), wt_scales.rearrange("a q n -> q a n").bitcast(I32))
-        nc.scalar.dma_start(ws_raw[0:32:2, 2 * N :].bitcast(I32), zv_scales[0].bitcast(I32))
-        nc.scalar.dma_start(w_rows[0 : J // P, :], wgo[0].rearrange("(c p) -> c p", p=P))
-        nc.sync.dma_start(list1[:], offs)
         words_in = {"zt": zt_words, "wt": wt_words, "zv": zv_words}
 
         def load_words(name):
             nc.sync.dma_start(raw[name][:].bitcast(I32), words_in[name].rearrange("a p n -> p a n").bitcast(I32))
 
+        make_identity(nc, ident[:])
+        nc.sync.dma_start(list2[:], offs2)
+        nc.sync.dma_start(tab2_s[0:32, :].bitcast(I32), tab2_scales.rearrange("a q t -> q a t").bitcast(I32))
+        nc.scalar.dma_start(ws_raw[0:32, 0:N].bitcast(I32), zt_scales.rearrange("a q n -> q a n").bitcast(I32))
+        nc.scalar.dma_start(ws_raw[0:32, N : 2 * N].bitcast(I32), wt_scales.rearrange("a q n -> q a n").bitcast(I32))
+        nc.scalar.dma_start(ws_raw[0:32:2, 2 * N :].bitcast(I32), zv_scales[0].bitcast(I32))
         nc.sync.dma_start(tab2_w[:], tab2_words[0].rearrange("p t i -> p (t i)").bitcast(I32))
-        nc.sync.dma_start(tab_w[:], tab_words[0].rearrange("p t i -> p (t i)").bitcast(I32))
         load_words("wt")
+        load_words("zt")
+        nc.sync.dma_start(list1[:], offs)
         for r in range(4):
             nc.scalar.dma_start(tab_s[r:P:32, :].bitcast(I32), tab_scales[0, r:16:4, :].bitcast(I32))
-        load_words("zt")
+        nc.sync.dma_start(tab_w[:], tab_words[0].rearrange("p t i -> p (t i)").bitcast(I32))
         load_words("zv")
-        nc.sync.dma_start(bias[:], b.rearrange("(p t) -> p t", t=PACK))
+        nc.scalar.dma_start(w_rows[0 : J // P, :], wgo[0].rearrange("(c p) -> c p", p=P))
 
         nc.scalar.activation(warm[:, 0:1], warm[:, 1:2], ACT.Sigmoid)
 
-        def list_cols(h):
-            return slice(h * LIST_COLS, (h + 1) * LIST_COLS)
+        def entries(first, count):
+            return slice(first // 16, (first + count) // 16)
 
         def half_cols(h):
             return slice(h * HALF, (h + 1) * HALF)
@@ -115,259 +130,249 @@ def tile_list_gmu_relu_scatP_kernel(
         def block(k):
             return slice(k * P, (k + 1) * P)
 
-        v2_s_rows = at_byte("v2_s_rows", [P, J], U8, ROWS_AT)
-        nc.vector.tensor_copy(v2_s_rows[:], tab2_s[:].indirect(list2[:]))
-        rows = at_byte("rows", [P, J + 3 * N], U8, SCALES_AT + 64 - (J + 3 * N))
-        nc.vector.tensor_copy(
-            rows[:, J:].rearrange("p (a t o i) -> p o a t i", a=3, t=PACK, i=16),
-            ws_raw[:].rearrange("p (a o i t) -> p o a t i", a=3, t=PACK, i=16),
-        )
-        nc.vector.tensor_copy(rows[:, :J].bitcast(I32), v2_s_rows[:].bitcast(I32))
-        planes = held("planes", [P, 2, J + 3 * N], U8)
-        for q in (0, 2, 1, 3):
-            nc.sync.dma_start(planes[32 * q : 32 * q + 4, :, :].bitcast(I32), rows[8 * q : 8 * q + 8, :].bitcast(I32))
+        page = {}
 
+        def clear_page(t, offset, pieces):
+            page[t] = at_byte("page%d" % t, [P, T], F32, offset)
+            for c in range(pieces):
+                nc.gpsimd.memset(page[t][:, c * T // pieces : (c + 1) * T // pieces], 0.0)
+
+        rows, planes = {}, {}
+        width = HALF + 3 * 2 * P
+
+        def deal_scales(g):
+            rows[g] = held("rows%d" % g, [P, width], U8)
+            nc.vector.tensor_copy(
+                rows[g][:, HALF:].rearrange("p (a t o i) -> p o a t i", a=3, t=2, i=16),
+                ws_raw[:].rearrange("p (a o i t) -> p o a t i", a=3, t=PACK, i=16)[:, :, :, 2 * g : 2 * g + 2, :],
+            )
+
+        def join_rows(g):
+            nc.vector.tensor_copy(rows[g][:, :HALF].bitcast(I32), v2_rows[:, half_cols(g)].bitcast(I32))
+
+        def move_rows(g):
+            planes[g] = held("planes%d" % g, [P, 2, width], U8)
+            for q in (0, 2, 1, 3):
+                nc.sync.dma_start(planes[g][32 * q : 32 * q + 4, :, :].bitcast(I32), rows[g][8 * q : 8 * q + 8, :].bitcast(I32))
+
+        deal_scales(0)
+        deal_scales(1)
+        clear_page(0, PAGE0_AT, 1)
+        v2_rows = at_byte("v2_rows", [P, J], U8, V2ROWS_AT)
+        nc.vector.tensor_copy(v2_rows[:], tab2_s[:].indirect(list2[:]))
+        join_rows(0)
+        join_rows(1)
+        move_rows(0)
+        nc.scalar.dma_start(bias[:], b.rearrange("(p t) -> p t", t=PACK))
         wv_raw = at_byte("wv_raw", [P, PACK, N], F32, WV_AT)
         nc.sync.dma_start(wv_raw[:], wv.rearrange("(p i) n -> p i n", i=PACK))
-
-        w_bank = bank("mx0")
-        nc.tensor.transpose(w_bank[:, 0:P], w_rows[:], ident[:])
-        w_cols = held("w_cols", [P, J // P], F32)
-        nc.scalar.copy(w_cols[:], w_bank[:, 0 : J // P])
-        w_wide = bank("back")
-        for k in range(BLOCKS):
-            nc.tensor.transpose(w_wide[:, block(k)], w_cols[:, k : k + 1].to_broadcast([P, P]), ident[:])
+        move_rows(1)
+        clear_page(1, PAGE1_AT, 1)
 
         dealt = {}
 
         def deal(name):
-            dealt[name] = held(name + "_dealt", [P, raw[name].shape[1], 2 * N], U8)
-            nc.scalar.copy(
-                dealt[name][:].bitcast(U16).rearrange("p a (t o i) -> p o a t i", t=PACK, i=8),
-                raw[name][:].bitcast(U16).rearrange("p a (o i t) -> p o a t i", t=PACK, i=8),
-            )
+            passes = raw[name].shape[1]
+            dealt[name] = held(name + "_dealt", [P, passes, 2 * N], U8)
+            for a in range(passes):
+                nc.scalar.copy(
+                    dealt[name][:, a, :].bitcast(U16).rearrange("p (t o i) -> p o t i", t=PACK, i=8),
+                    raw[name][:, a, :].bitcast(U16).rearrange("p (o i t) -> p o t i", t=PACK, i=8),
+                )
 
         deal("wt")
         deal("zt")
+        w_bank = bank("picture", 1)
+        nc.tensor.transpose(w_bank[:, 0:P], w_rows[:], ident[:])
+        w_cols = held("w_cols", [P, J // P], F32)
+        nc.scalar.copy(w_cols[:], w_bank[:, 0 : J // P])
         deal("zv")
 
-        page[1] = at_byte("page1", [P, T], F32, ROWS_AT + 64 - PAGE_BYTES)
-        nc.gpsimd.memset(page[1][:], 0.0)
+        v2_w, v_w, v_s, wv_w, wv_s = {}, {}, {}, {}, {}
         both = at_byte("both", [P, J], U32, BOTH_AT)
         nc.vector.tensor_copy(both[:], tab2_w[:].bitcast(U32).indirect(list2[:]))
-        v2_w, v_w = {}, {}
-        for h in range(HALVES):
+
+        def part_text(h):
             v2_w[h] = held("v2_w%d" % h, [P, 2, 2 * HALF], U8)
             nc.vector.tensor_copy(
                 v2_w[h][:].bitcast(U16).rearrange("p d (o i) -> p o d i", i=8),
                 both[:, half_cols(h)].bitcast(U16).rearrange("p (o i d) -> p o d i", d=2, i=8),
             )
-        page[3] = at_byte("page3", [P, T], F32, BOTH_AT + 64 - PAGE_BYTES)
-        nc.gpsimd.memset(page[3][:], 0.0)
-        page[2] = at_byte("page2", [P, T], F32, BOTH_AT + 4096 - 64)
-        nc.gpsimd.memset(page[2][:], 0.0)
-        v_s = at_byte("v_s", [P, J], U8, BOTH_AT + 64)
-        nc.vector.tensor_copy(v_s[:], tab_s[:].indirect(list1[:]))
-        for h in range(HALVES):
-            v_w[h] = held("v_w%d" % h, [P, HALF], U32)
-            nc.vector.tensor_copy(v_w[h][:], tab_w[:].bitcast(U32).indirect(list1[:, list_cols(h)]))
 
-        wv_w, wv_s = {}, {}
+        def gather_picture_scales(h):
+            v_s[h] = at_byte("v_s%d" % h, [P, HALF], U8, (VS0_AT, VS1_AT)[h])
+            nc.vector.tensor_copy(v_s[h][:], tab_s[:].indirect(list1[:, entries(h * HALF, HALF)]))
 
-        def quantise_wv(g):
-            rounded = held("wv_bf%d" % g, [P, 2 * P * PACK], BF16)
-            nc.scalar.copy(
-                rounded[:].rearrange("p (t m i) -> p m t i", t=2, i=PACK),
-                wv_raw[:].rearrange("p i (m t) -> p m t i", t=PACK)[:, :, 2 * g : 2 * g + 2, :],
+        def gather_picture(h):
+            v_w[h] = at_byte("v_w1", [P, HALF], U32, VW1_AT) if h else held("v_w0", [P, HALF], U32)
+            nc.vector.tensor_copy(v_w[h][:], tab_w[:].bitcast(U32).indirect(list1[:, entries(h * HALF, HALF)]))
+
+        rounded = {}
+
+        def round_wv(t, count, offset):
+            rounded[t] = at_byte("wv_bf%d" % t, [P, count * P * PACK], BF16, offset)
+            nc.vector.tensor_copy(
+                rounded[t][:].rearrange("p (t m i) -> p m t i", t=count, i=PACK),
+                wv_raw[:].rearrange("p i (m t) -> p m t i", t=PACK)[:, :, t : t + count, :],
             )
-            wv_w[g] = held("wv_w%d" % g, [P, 2 * P], U32)
-            wv_s[g] = held("wv_s%d" % g, [P, 2 * P], U8)
-            nc.vector.quantize_mx(out=wv_w[g][:].bitcast(FP8X4), scales=wv_s[g][:], in_=rounded[:])
+
+        def quantise_wv(t, count):
+            words = held("wv_w%d" % t, [P, count * P], U32)
+            scales = held("wv_s%d" % t, [P, count * P], U8)
+            nc.vector.quantize_mx(out=words[:].bitcast(FP8X4), scales=scales[:], in_=rounded[t][:])
+            for n in range(count):
+                wv_w[t + n], wv_s[t + n] = words[:, block(n)], scales[:, block(n)]
+
+        part_text(0)
+        part_text(1)
+        clear_page(2, PAGE2_AT, 1)
+        gather_picture_scales(0)
+        gather_picture(0)
+        round_wv(0, 1, ROUND0_AT)
+        round_wv(1, 1, ROUND1_AT)
+        quantise_wv(0, 1)
+        quantise_wv(1, 1)
+        round_wv(2, 2, ROUND2_AT)
+        quantise_wv(2, 2)
 
         scale_run = {"zt": 0, "wt": 1, "zv": 2}
 
         def w4_pass(name, a, t):
-            first = J + scale_run[name] * N + P * t
-            return dealt[name][:, a, 2 * P * t : 2 * P * (t + 1)].bitcast(FP4X4), planes[:, a, first : first + P]
+            first = HALF + (scale_run[name] * 2 + t % 2) * P
+            return dealt[name][:, a, 2 * P * t : 2 * P * (t + 1)].bitcast(FP4X4), planes[t // 2][:, a, first : first + P]
 
         def wv_pass(t):
-            return wv_w[t // 2][:, block(t % 2)].bitcast(FP8X4), wv_s[t // 2][:, block(t % 2)]
+            return wv_w[t].bitcast(FP8X4), wv_s[t]
 
-        def v_pass(h):
-            return v_w[h][:].bitcast(FP8X4), v_s[:, half_cols(h)]
+        def v_pass(first, count):
+            cols = slice(first % HALF, first % HALF + count)
+            return v_w[first // HALF][:, cols].bitcast(FP8X4), v_s[first // HALF][:, cols]
 
-        def v2_pass(h, d):
-            return v2_w[h][:, d, :].bitcast(FP4X4), planes[:, d, half_cols(h)]
+        def v2_pass(first, count, d):
+            at = first % HALF
+            return v2_w[first // HALF][:, d, 2 * at : 2 * (at + count)].bitcast(FP4X4), planes[first // HALF][:, d, at : at + count]
 
         def mm(out, left, right, start, stop):
-            nc.tensor.matmul_mx(out=out[:], lhsT=left[0], lhsT_scale=left[1], rhs=right[0], rhs_scale=right[1], start=start, stop=stop)
-
-        taken = [0]
-
-        def mx_bank():
-            taken[0] = taken[0] + 1
-            return bank("mx%d" % (taken[0] % MX_BANKS))
+            nc.tensor.matmul_mx(out=out, lhsT=left[0], lhsT_scale=left[1], rhs=right[0], rhs_scale=right[1], start=start, stop=stop)
 
         last = len(UNITS) - 1
         out_rows = out_0.rearrange("(p t) c -> t p c", t=PACK)
+        text, gate, picture, z = {}, {}, {}, {}
 
-        def unit_tile(name, u):
-            if u == last and name in ("gate", "picture"):
-                return at_byte(name, [P, HALF], F32, LAST_AT + (0 if name == "gate" else 2048 + 8192))
-            if u == VECTOR_UNITS and name == "text":
-                return at_byte("text%d" % u, [P, HALF], F32, WV_AT + 64 + 2048 * u)
-            if u < VECTOR_UNITS and name == "gate":
-                return at_byte("gate%d" % u, [P, HALF], F32, WV_AT + 64 + 2048 * u)
-            return held("%s%d" % (name, u), [P, HALF], F32)
+        def text_passes(u, role, n):
+            t, first, count = UNITS[u]
+            ht = bank(role, n)[:, :count]
+            mm(ht, w4_pass("wt", 0, t), v2_pass(first, count, 0), True, False)
+            mm(ht, w4_pass("wt", 1, t), v2_pass(first, count, 1), False, True)
+            return ht
 
-        text, gate, picture, gated, weighed, result = {}, {}, {}, {}, {}, {}
-
-        def text_sum(u):
-            t, h = UNITS[u]
-            text[u] = unit_tile("text", u)
-            ht = mx_bank()
-            mm(ht, w4_pass("wt", 0, t), v2_pass(h, 0), True, False)
-            mm(ht, w4_pass("wt", 1, t), v2_pass(h, 1), False, True)
-            nc.scalar.activation(text[u][:], ht[:], ACT.Relu)
-
-        def picture_sum(u, hv):
-            t, h = UNITS[u]
-            picture[u] = unit_tile("picture", u)
-            mm(hv, wv_pass(t), v_pass(h), True, True)
-
-        z = {}
+        def text_sum(u, role, n):
+            text[u] = at_byte("text1", [P, HALF], F32, TEXT0_AT) if u == 1 else held("text%d" % u, [P, HALF], F32)
+            nc.scalar.activation(text[u][:], text_passes(u, role, n), ACT.Relu)
 
         def open_gate(u):
-            t, h = UNITS[u]
-            z[u] = mx_bank()
-            mm(z[u], w4_pass("zt", 0, t), v2_pass(h, 0), True, False)
-            mm(z[u], w4_pass("zt", 1, t), v2_pass(h, 1), False, False)
+            t, first, count = UNITS[u]
+            z[u] = bank("gate", u)[:, :count]
+            mm(z[u], w4_pass("zt", 0, t), v2_pass(first, count, 0), True, False)
+            mm(z[u], w4_pass("zt", 1, t), v2_pass(first, count, 1), False, False)
 
-        def gate_sum(u):
-            t, h = UNITS[u]
-            if u not in z:
-                open_gate(u)
-            gate[u] = unit_tile("gate", u)
-            mm(z[u], w4_pass("zv", 0, t), v_pass(h), False, True)
-            nc.scalar.activation(gate[u][:], z[u][:], ACT.Sigmoid, bias=bias[:, t : t + 1])
+        def close_gate(u):
+            t, first, count = UNITS[u]
+            gate[u] = at_byte("gate_last", [P, count], F32, GATE_AT) if u == last else ring.tile([P, count], F32, name="gate")
+            mm(z[u], w4_pass("zv", 0, t), v_pass(first, count), False, True)
+            nc.scalar.activation(gate[u][:], z[u], ACT.Sigmoid, bias=bias[:, t : t + 1])
 
-        def place(u):
-            t, h = UNITS[u]
-            nc.vector.tensor_copy(page[t][:].indirect(list1[:, list_cols(h)]), result[u][:])
-            if h == HALVES - 1:
+        def picture_sum(u):
+            t, first, count = UNITS[u]
+            picture[u] = ring.tile([P, count], F32, name="picture")
+            hv = bank("picture", u)[:, :count]
+            mm(hv, wv_pass(t), v_pass(first, count), True, True)
+            nc.scalar.activation(picture[u][:], hv, ACT.Relu)
+
+        def mix(u):
+            nc.gpsimd.tensor_tensor(picture[u][:], picture[u][:], text[u][:], ALU.subtract)
+            nc.gpsimd.tensor_tensor(picture[u][:], picture[u][:], gate[u][:], ALU.mult)
+
+        def finish(u):
+            t, first, count = UNITS[u]
+            blocks = range(count // P)
+            turned = bank("turned", u)
+            for k in blocks:
+                nc.tensor.matmul(turned[:, block(k)], text[u][:, block(k)], ident[:], start=True, stop=False, is_transpose=True)
+                nc.tensor.matmul(turned[:, block(k)], picture[u][:, block(k)], ident[:], start=False, stop=True, is_transpose=True)
+            weighed = at_byte("weighed_last", [P, count], F32, WEIGHED_AT) if u == last else ring.tile([P, count], F32, name="weighed")
+            for k in blocks:
+                col = first // P + k
+                nc.scalar.activation(weighed[:, block(k)], turned[:, block(k)], ACT.Copy, scale=w_cols[:, col : col + 1])
+            back = bank("back", u)
+            for k in blocks:
+                nc.tensor.transpose(back[:, block(k)], weighed[:, block(k)], ident[:])
+            result = held("result%d" % u, [P, count], F32)
+            nc.scalar.copy(result[:], back[:, :count])
+            nc.vector.tensor_copy(page[t][:].indirect(list1[:, entries(first, count)]), result[:])
+            if first + count == J:
                 nc.sync.dma_start(out_rows[t], page[t][:])
 
-        def vector_units(hv):
-            for u in hv:
-                nc.vector.scalar_tensor_tensor(picture[u][:], hv[u][:], 0.0, text[u][:], ALU.max, ALU.subtract)
-            for u in hv:
-                nc.vector.tensor_tensor(picture[u][:], picture[u][:], gate[u][:], ALU.mult)
-            for u in hv:
-                nc.vector.tensor_tensor(picture[u][:], picture[u][:], text[u][:], ALU.add)
-            for u in hv:
-                result[u] = unit_tile("result", u)
-                nc.vector.tensor_tensor(result[u][:], picture[u][:], w_wide[:], ALU.mult)
-            for u in hv:
-                place(u)
+        def clear_piece(t, c):
+            nc.gpsimd.memset(page[t][:, c * CHUNK : (c + 1) * CHUNK], 0.0)
 
-        def difference(u):
-            hv = mx_bank()
-            picture_sum(u, hv)
-            nc.scalar.activation(picture[u][:], hv[:], ACT.Relu)
-            nc.gpsimd.tensor_tensor(picture[u][:], picture[u][:], text[u][:], ALU.subtract)
-
-        def product(u):
-            gate_sum(u)
-            gated[u] = ring.tile([P, HALF], F32, name="gated")
-            nc.gpsimd.tensor_tensor(gated[u][:], picture[u][:], gate[u][:], ALU.mult)
-
-        turned, back = {}, {}
-
-        def turn(u):
-            turned[u] = bank("turned")
-            for k in range(BLOCKS):
-                nc.tensor.matmul(turned[u][:, block(k)], gated[u][:, block(k)], ident[:], start=True, stop=False, is_transpose=True)
-                nc.tensor.matmul(turned[u][:, block(k)], text[u][:, block(k)], ident[:], start=False, stop=True, is_transpose=True)
-
-        def weigh(u):
-            t, h = UNITS[u]
-            if u == last:
-                weighed[u] = [pairs[k][:, 2 * CHUNK : 2 * CHUNK + 2 * P].bitcast(F32) for k in range(BLOCKS)]
-            else:
-                whole = ring.tile([P, HALF], F32, name="weighed")
-                weighed[u] = [whole[:, block(k)] for k in range(BLOCKS)]
-            for k in range(BLOCKS):
-                col = h * BLOCKS + k
-                nc.scalar.activation(weighed[u][k], turned[u][:, block(k)], ACT.Copy, scale=w_cols[:, col : col + 1])
-            back[u] = bank("back")
-            for k in range(BLOCKS):
-                nc.tensor.transpose(back[u][:, block(k)], weighed[u][k], ident[:])
-
-        def hand_over(u):
-            result[u] = unit_tile("result", u)
-            nc.scalar.copy(result[u][:], back[u][:])
-            place(u)
-
-        pair_at = (LAST_AT + 64 - 4096, LAST_AT + 2048 - 64, LAST_AT + 2048 + 8192 + 64 - 4096, LAST_AT + 4096 + 8192 - 64)
-        pairs = []
-        first = VECTOR_UNITS
-        quantise_wv(0)
-        quantise_wv(1)
-        text_sum(0)
-        text_sum(1)
+        ht0 = text_passes(0, "back", 0)
         open_gate(0)
+        text_sum(1, "turned", 1)
         open_gate(1)
-        for u in range(first):
-            gate_sum(u)
-        text_sum(first)
-        open_gate(first)
-        hv_banks = {0: bank("turned"), 1: mx_bank()}
-        for u in hv_banks:
-            picture_sum(u, hv_banks[u])
-        vector_units(hv_banks)
-        difference(first)
-        product(first)
-        text_sum(first + 1)
-        for u in range(first, last + 3):
-            if u - 2 >= first:
-                weigh(u - 2)
-            if first < u <= last:
-                difference(u)
-                product(u)
-            if u == last:
-                pairs.extend(at_byte("pairs%d" % c, [P, 4 * CHUNK], BF16, pair_at[c]) for c in range(CHUNKS))
+        close_gate(0)
+        minus_bias = held("minus_bias", [P, 1], F32)
+        nc.scalar.activation(minus_bias[:], bias[:, 0:1], ACT.Copy, scale=-1.0)
+        rest = held("rest", [P, HALF], F32)
+        nc.scalar.activation(rest[:], z[0], ACT.Sigmoid, bias=minus_bias[:], scale=-1.0)
+        close_gate(1)
+        text[0] = at_byte("share", [P, HALF], F32, SHARE_AT)
+        nc.vector.scalar_tensor_tensor(text[0][:], ht0, 0.0, rest[:], ALU.max, ALU.mult)
+        hv0 = bank("picture", 0)
+        mm(hv0[:], wv_pass(0), v_pass(0, HALF), True, True)
+        picture[0] = ring.tile([P, HALF], F32, name="picture")
+        nc.vector.scalar_tensor_tensor(picture[0][:], hv0[:], 0.0, gate[0][:], ALU.max, ALU.mult)
+        gather_picture_scales(1)
+        gather_picture(1)
+        picture_sum(1)
+        mix(1)
+        for u, role in ((2, "turned"), (3, "back"), (4, "turned"), (5, "back"), (6, "picture")):
+            text_sum(u, role, min(u - 2, 1))
+        for u in range(last + 1):
+            finish(u)
+            if u == 1:
+                page[3] = at_byte("page3", [P, T], F32, PAGE3_AT)
+            if u == 1:
+                text_sum(last, "back", u)
             if u + 2 <= last:
-                text_sum(u + 2)
-            if u - 2 >= first:
-                hand_over(u - 2)
-            if first <= u - 1 <= last:
-                turn(u - 1)
+                open_gate(u + 2)
+                close_gate(u + 2)
+                picture_sum(u + 2)
+                mix(u + 2)
+            if 1 <= u <= CHUNKS:
+                clear_piece(3, u - 1)
+
+        pairs = [at_byte("pairs%d" % c, [P, 4 * CHUNK], BF16, (PAIR0_AT, PAIR1_AT, PAIR2_AT, PAIR3_AT)[c]) for c in range(CHUNKS)]
 
         def round_page(t, c):
             rows_f32 = page[t][:, c * CHUNK : (c + 1) * CHUNK]
             words = pairs[c][:, t // 2 * 2 * CHUNK : (t // 2 + 1) * 2 * CHUNK].rearrange("p (c i) -> p c i", i=2)
-            twice = rows_f32.unsqueeze(2).to_broadcast([P, CHUNK, 2])
-            if t == 0:
-                nc.gpsimd.tensor_scalar(words, twice, 1.0, -0.0, ALU.mult, ALU.add)
-            elif t == 1 and c >= VECTOR_CHUNKS:
-                nc.gpsimd.tensor_scalar(words[:, :, 1], rows_f32, 1.0, -0.0, ALU.mult, ALU.add)
-            elif c < VECTOR_CHUNKS and t == PACK - 2:
-                nc.scalar.copy(words, twice)
-            elif c < VECTOR_CHUNKS and t == PACK - 1:
-                nc.vector.tensor_copy(words[:, :, 1], rows_f32)
-            else:
+            if c >= VECTOR_CHUNKS:
                 nc.scalar.copy(words[:, :, t % 2], rows_f32)
+            elif t == PACK - 1:
+                nc.vector.tensor_copy(words[:, :, 1], rows_f32)
+            elif t == PACK - 2:
+                nc.gpsimd.tensor_scalar(words, rows_f32.unsqueeze(2).to_broadcast([P, CHUNK, 2]), 1.0, -0.0, ALU.mult, ALU.add)
+            else:
+                nc.gpsimd.tensor_scalar(words[:, :, t], rows_f32, 1.0, -0.0, ALU.mult, ALU.add)
 
-        for c in ROUNDING_ORDER:
-            round_page(0, c)
-            round_page(1, c)
-        for t in (2, 3):
+        for t in range(PACK):
             for c in range(CHUNKS):
                 round_page(t, c)
 
         y_s = held("y_s", [P, T], U8)
         out_words = out_1[0].rearrange("p c i -> p (c i)").bitcast(I32)
-        spare = ("tab2_w", "text0", "text1", "zt_raw", "wt_raw")
+        spare = ("tab2_w", "tab_w", "text2", "zt_raw", "wt_raw")
         grouped = []
         for n, (c, first, width) in enumerate(PIECES):
             grouped.append(held("grouped%d" % n, [P, width, PACK], BF16, tag=spare[n]))

@@ -25,31 +25,26 @@ CHUNK = 512
 CHUNKS = T // CHUNK
 VECTOR_CHUNKS = 2
 PIECES = ((0, 0, 512), (1, 0, 512), (2, 0, 512), (3, 0, 256), (3, 256, 256))
-UNITS = tuple((t, h * HALF, HALF) for t, h in ((0, 0), (1, 0), (2, 0), (0, 1), (1, 1), (3, 0), (2, 1), (3, 1)))
-SWAPPED = {("gate", 3): ("turned", 0), ("turned", 2): ("gate", 1), ("picture", 3): ("back", 0), ("back", 2): ("picture", 1)}
+UNITS = tuple((t, h * HALF, HALF) for t, h in ((0, 0), (1, 0), (2, 0), (0, 1), (1, 1), (2, 1), (3, 0), (3, 1)))
+TEXT_BANK = {2: ("turned", 1), 3: ("picture", 0), 4: ("back", 0), 5: ("back", 1), 6: ("back", 0), 7: ("back", 1)}
+LAST_TURNED = 6
+VECTOR_UNITS = 2
 LAP = 64
 PAGE = 4 * T
 ROW = 4 * HALF
 PAIR = 8 * CHUNK
-PAGE0_AT = 0
-WS_AT = PAGE0_AT + PAGE - LAP
-PAGE1_AT = WS_AT + 3 * N
-V2ROWS_AT = PAGE1_AT + PAGE - LAP
-WV_AT = V2ROWS_AT + J - LAP
-BOTH_AT = WV_AT + PAGE
-VS0_AT = BOTH_AT + HALF
-PAGE2_AT = BOTH_AT + 2 * ROW - LAP
-SHARE_AT = PAGE2_AT + PAGE
-ROUND0_AT = SHARE_AT + ROW - LAP
-ROUND1_AT = ROUND0_AT + ROW // 2
-ROUND2_AT = ROUND1_AT + ROW // 2
-VS1_AT = ROUND2_AT + LAP
-VW1_AT = ROUND2_AT + ROW - LAP
-PAGE3_AT = VW1_AT + ROW
-TEXT0_AT = PAGE3_AT + PAGE - LAP
-PAIR0_AT = TEXT0_AT + ROW
-GATE_AT = PAIR0_AT + PAIR - LAP
-PAIR1_AT = GATE_AT + ROW - LAP
+TAB_AT = 0
+WS_AT = TAB_AT + PAGE - LAP
+WV_AT = WS_AT + 3 * N
+V2ROWS_AT = WV_AT + PAGE - LAP
+BIAS_AT = V2ROWS_AT + LAP
+WROWS_AT = V2ROWS_AT + 2 * LAP
+BOTH_AT = V2ROWS_AT + J
+VS_AT = BOTH_AT + HALF
+WIDE_AT = BOTH_AT + 2 * ROW - LAP
+PAIR0_AT = WIDE_AT + ROW
+TEXT_AT = PAIR0_AT + PAIR - LAP
+PAIR1_AT = TEXT_AT + ROW - LAP
 PAIR2_AT = PAIR1_AT + PAIR
 WEIGHED_AT = PAIR2_AT + PAIR - LAP
 PAIR3_AT = WEIGHED_AT + ROW - LAP
@@ -63,7 +58,7 @@ def tile_list_gmu_relu_scatP_kernel(
     with ExitStack() as ctx:
         keep = ctx.enter_context(tc.tile_pool(name="keep", bufs=1))
         placed = ctx.enter_context(tc.tile_pool(name="placed", bufs=1))
-        ring = ctx.enter_context(tc.tile_pool(name="ring", bufs=3))
+        ring = ctx.enter_context(tc.tile_pool(name="ring", bufs=4))
         psum = ctx.enter_context(tc.psum_pool(name="psum", bufs=1))
 
         def held(name, shape, dtype, tag=""):
@@ -73,51 +68,44 @@ def tile_list_gmu_relu_scatP_kernel(
             return placed.tile(shape, dtype, name=name, tag=name, align_bytes=64, offset=offset)
 
         def bank(role, u):
-            role, n = SWAPPED.get((role, u), (role, u % 2))
-            return psum.tile([P, HALF], F32, name="bank", tag="%s%d" % (role, n))
+            return psum.tile([P, HALF], F32, name="bank", tag="%s%d" % (role, u % 2))
 
         list1 = held("list1", [P, J // 16], U16)
         list2 = held("list2", [P, J // 16], U16)
         tab_s = held("tab_s", [P, T], U8)
         tab2_s = held("tab2_s", [P, T], U8)
         tab2_w = held("tab2_w", [P, T], I32)
-        tab_w = held("tab_w", [P, T], I32)
         ws_raw = at_byte("ws_raw", [P, 3 * N], U8, WS_AT)
         raw = {name: held(name + "_raw", [P, passes, 2 * N], U8) for name, passes in (("wt", 2), ("zt", 2), ("zv", 1))}
-        bias = held("bias", [P, PACK], F32)
-        w_rows = held("w_rows", [P, P], F32)
         ident = held("ident", [P, P], F32)
         warm = held("warm", [P, 8], F32)
 
         nc.vector.memset(warm[:], 0.0)
         nc.vector.memset(ws_raw[:, 2 * N :].bitcast(I32), 0)
+        nc.vector.memset(tab_s[:].bitcast(I32), 0)
         for rows32 in (slice(32, 64), slice(64, 128)):
             nc.vector.memset(ws_raw[rows32, : 2 * N].bitcast(I32), 0)
-        nc.vector.memset(tab_s[:].bitcast(I32), 0)
-        nc.vector.memset(w_rows[:], 0.0)
         for rows32 in (slice(32, 64), slice(64, 128)):
             nc.gpsimd.memset(tab2_s[rows32, :].bitcast(I32), 0)
+        make_identity(nc, ident[:])
 
         words_in = {"zt": zt_words, "wt": wt_words, "zv": zv_words}
 
         def load_words(name):
             nc.sync.dma_start(raw[name][:].bitcast(I32), words_in[name].rearrange("a p n -> p a n").bitcast(I32))
 
-        make_identity(nc, ident[:])
         nc.sync.dma_start(list2[:], offs2)
         nc.sync.dma_start(tab2_s[0:32, :].bitcast(I32), tab2_scales.rearrange("a q t -> q a t").bitcast(I32))
         nc.scalar.dma_start(ws_raw[0:32, 0:N].bitcast(I32), zt_scales.rearrange("a q n -> q a n").bitcast(I32))
         nc.scalar.dma_start(ws_raw[0:32, N : 2 * N].bitcast(I32), wt_scales.rearrange("a q n -> q a n").bitcast(I32))
         nc.scalar.dma_start(ws_raw[0:32:2, 2 * N :].bitcast(I32), zv_scales[0].bitcast(I32))
         nc.sync.dma_start(tab2_w[:], tab2_words[0].rearrange("p t i -> p (t i)").bitcast(I32))
-        load_words("wt")
         load_words("zt")
         nc.sync.dma_start(list1[:], offs)
+        load_words("wt")
+        load_words("zv")
         for r in range(4):
             nc.scalar.dma_start(tab_s[r:P:32, :].bitcast(I32), tab_scales[0, r:16:4, :].bitcast(I32))
-        nc.sync.dma_start(tab_w[:], tab_words[0].rearrange("p t i -> p (t i)").bitcast(I32))
-        load_words("zv")
-        nc.scalar.dma_start(w_rows[0 : J // P, :], wgo[0].rearrange("(c p) -> c p", p=P))
 
         nc.scalar.activation(warm[:, 0:1], warm[:, 1:2], ACT.Sigmoid)
 
@@ -132,42 +120,31 @@ def tile_list_gmu_relu_scatP_kernel(
 
         page = {}
 
-        def clear_page(t, offset, pieces):
-            page[t] = at_byte("page%d" % t, [P, T], F32, offset)
-            for c in range(pieces):
-                nc.gpsimd.memset(page[t][:, c * T // pieces : (c + 1) * T // pieces], 0.0)
+        for t in range(PACK):
+            page[t] = held("page%d" % t, [P, T], F32)
+            for c in range(CHUNKS):
+                nc.gpsimd.memset(page[t][:, c * CHUNK : (c + 1) * CHUNK], 0.0)
 
-        rows, planes = {}, {}
-        width = HALF + 3 * 2 * P
-
-        def deal_scales(g):
-            rows[g] = held("rows%d" % g, [P, width], U8)
-            nc.vector.tensor_copy(
-                rows[g][:, HALF:].rearrange("p (a t o i) -> p o a t i", a=3, t=2, i=16),
-                ws_raw[:].rearrange("p (a o i t) -> p o a t i", a=3, t=PACK, i=16)[:, :, :, 2 * g : 2 * g + 2, :],
-            )
-
-        def join_rows(g):
-            nc.vector.tensor_copy(rows[g][:, :HALF].bitcast(I32), v2_rows[:, half_cols(g)].bitcast(I32))
-
-        def move_rows(g):
-            planes[g] = held("planes%d" % g, [P, 2, width], U8)
-            for q in (0, 2, 1, 3):
-                nc.sync.dma_start(planes[g][32 * q : 32 * q + 4, :, :].bitcast(I32), rows[g][8 * q : 8 * q + 8, :].bitcast(I32))
-
-        deal_scales(0)
-        deal_scales(1)
-        clear_page(0, PAGE0_AT, 1)
+        rows = held("rows", [P, J + 3 * N], U8)
+        nc.vector.tensor_copy(
+            rows[:, J:].rearrange("p (a t o i) -> p o a t i", a=3, t=PACK, i=16),
+            ws_raw[:].rearrange("p (a o i t) -> p o a t i", a=3, t=PACK, i=16),
+        )
+        tab_w = at_byte("tab_w", [P, T], I32, TAB_AT)
+        nc.sync.dma_start(tab_w[:], tab_words[0].rearrange("p t i -> p (t i)").bitcast(I32))
         v2_rows = at_byte("v2_rows", [P, J], U8, V2ROWS_AT)
         nc.vector.tensor_copy(v2_rows[:], tab2_s[:].indirect(list2[:]))
-        join_rows(0)
-        join_rows(1)
-        move_rows(0)
-        nc.scalar.dma_start(bias[:], b.rearrange("(p t) -> p t", t=PACK))
+        nc.vector.tensor_copy(rows[:, :J].bitcast(I32), v2_rows[:].bitcast(I32))
+        planes = held("planes", [P, 2, J + 3 * N], U8)
+        for q in (0, 2, 1, 3):
+            nc.sync.dma_start(planes[32 * q : 32 * q + 4, :, :].bitcast(I32), rows[8 * q : 8 * q + 8, :].bitcast(I32))
         wv_raw = at_byte("wv_raw", [P, PACK, N], F32, WV_AT)
         nc.sync.dma_start(wv_raw[:], wv.rearrange("(p i) n -> p i n", i=PACK))
-        move_rows(1)
-        clear_page(1, PAGE1_AT, 1)
+        bias = at_byte("bias", [P, PACK], F32, BIAS_AT)
+        nc.sync.dma_start(bias[:], b.rearrange("(p t) -> p t", t=PACK))
+        w_rows = at_byte("w_rows", [P, P], F32, WROWS_AT)
+        nc.gpsimd.memset(w_rows[:], 0.0)
+        nc.sync.dma_start(w_rows[0 : J // P, :], wgo[0].rearrange("(c p) -> c p", p=P))
 
         dealt = {}
 
@@ -180,15 +157,11 @@ def tile_list_gmu_relu_scatP_kernel(
                     raw[name][:, a, :].bitcast(U16).rearrange("p (o i t) -> p o t i", t=PACK, i=8),
                 )
 
-        deal("wt")
         deal("zt")
-        w_bank = bank("picture", 1)
-        nc.tensor.transpose(w_bank[:, 0:P], w_rows[:], ident[:])
-        w_cols = held("w_cols", [P, J // P], F32)
-        nc.scalar.copy(w_cols[:], w_bank[:, 0 : J // P])
+        deal("wt")
         deal("zv")
 
-        v2_w, v_w, v_s, wv_w, wv_s = {}, {}, {}, {}, {}
+        v2_w, v_w, wv_w, wv_s = {}, {}, {}, {}
         both = at_byte("both", [P, J], U32, BOTH_AT)
         nc.vector.tensor_copy(both[:], tab2_w[:].bitcast(U32).indirect(list2[:]))
 
@@ -199,58 +172,44 @@ def tile_list_gmu_relu_scatP_kernel(
                 both[:, half_cols(h)].bitcast(U16).rearrange("p (o i d) -> p o d i", d=2, i=8),
             )
 
-        def gather_picture_scales(h):
-            v_s[h] = at_byte("v_s%d" % h, [P, HALF], U8, (VS0_AT, VS1_AT)[h])
-            nc.vector.tensor_copy(v_s[h][:], tab_s[:].indirect(list1[:, entries(h * HALF, HALF)]))
-
-        def gather_picture(h):
-            v_w[h] = at_byte("v_w1", [P, HALF], U32, VW1_AT) if h else held("v_w0", [P, HALF], U32)
+        for h in range(HALVES):
+            part_text(h)
+        v_s = at_byte("v_s", [P, J], U8, VS_AT)
+        nc.vector.tensor_copy(v_s[:], tab_s[:].indirect(list1[:]))
+        for h in range(HALVES):
+            v_w[h] = held("v_w%d" % h, [P, HALF], U32)
             nc.vector.tensor_copy(v_w[h][:], tab_w[:].bitcast(U32).indirect(list1[:, entries(h * HALF, HALF)]))
 
-        rounded = {}
-
-        def round_wv(t, count, offset):
-            rounded[t] = at_byte("wv_bf%d" % t, [P, count * P * PACK], BF16, offset)
-            nc.vector.tensor_copy(
-                rounded[t][:].rearrange("p (t m i) -> p m t i", t=count, i=PACK),
-                wv_raw[:].rearrange("p i (m t) -> p m t i", t=PACK)[:, :, t : t + count, :],
-            )
-
-        def quantise_wv(t, count):
-            words = held("wv_w%d" % t, [P, count * P], U32)
-            scales = held("wv_s%d" % t, [P, count * P], U8)
-            nc.vector.quantize_mx(out=words[:].bitcast(FP8X4), scales=scales[:], in_=rounded[t][:])
-            for n in range(count):
-                wv_w[t + n], wv_s[t + n] = words[:, block(n)], scales[:, block(n)]
-
-        part_text(0)
-        part_text(1)
-        clear_page(2, PAGE2_AT, 1)
-        gather_picture_scales(0)
-        gather_picture(0)
-        round_wv(0, 1, ROUND0_AT)
-        round_wv(1, 1, ROUND1_AT)
-        quantise_wv(0, 1)
-        quantise_wv(1, 1)
-        round_wv(2, 2, ROUND2_AT)
-        quantise_wv(2, 2)
+        for g in range(2):
+            rounded = held("wv_bf%d" % g, [P, 2 * P * PACK], BF16)
+            grouped_wv = rounded[:].rearrange("p (t m i) -> p m t i", t=2, i=PACK)
+            raw_wv = wv_raw[:].rearrange("p i (m t) -> p m t i", t=PACK)[:, :, 2 * g : 2 * g + 2, :]
+            if g == 0:
+                nc.scalar.copy(grouped_wv, raw_wv)
+            else:
+                nc.gpsimd.tensor_scalar(grouped_wv, raw_wv, 1.0, -0.0, ALU.mult, ALU.add)
+            words = held("wv_w%d" % g, [P, 2 * P], U32)
+            scales = held("wv_s%d" % g, [P, 2 * P], U8)
+            nc.vector.quantize_mx(out=words[:].bitcast(FP8X4), scales=scales[:], in_=rounded[:])
+            for n in range(2):
+                wv_w[2 * g + n], wv_s[2 * g + n] = words[:, block(n)], scales[:, block(n)]
 
         scale_run = {"zt": 0, "wt": 1, "zv": 2}
 
         def w4_pass(name, a, t):
-            first = HALF + (scale_run[name] * 2 + t % 2) * P
-            return dealt[name][:, a, 2 * P * t : 2 * P * (t + 1)].bitcast(FP4X4), planes[t // 2][:, a, first : first + P]
+            first = J + scale_run[name] * N + P * t
+            return dealt[name][:, a, 2 * P * t : 2 * P * (t + 1)].bitcast(FP4X4), planes[:, a, first : first + P]
 
         def wv_pass(t):
             return wv_w[t].bitcast(FP8X4), wv_s[t]
 
         def v_pass(first, count):
             cols = slice(first % HALF, first % HALF + count)
-            return v_w[first // HALF][:, cols].bitcast(FP8X4), v_s[first // HALF][:, cols]
+            return v_w[first // HALF][:, cols].bitcast(FP8X4), v_s[:, first : first + count]
 
         def v2_pass(first, count, d):
             at = first % HALF
-            return v2_w[first // HALF][:, d, 2 * at : 2 * (at + count)].bitcast(FP4X4), planes[first // HALF][:, d, at : at + count]
+            return v2_w[first // HALF][:, d, 2 * at : 2 * (at + count)].bitcast(FP4X4), planes[:, d, first : first + count]
 
         def mm(out, left, right, start, stop):
             nc.tensor.matmul_mx(out=out, lhsT=left[0], lhsT_scale=left[1], rhs=right[0], rhs_scale=right[1], start=start, stop=stop)
@@ -267,7 +226,7 @@ def tile_list_gmu_relu_scatP_kernel(
             return ht
 
         def text_sum(u, role, n):
-            text[u] = at_byte("text1", [P, HALF], F32, TEXT0_AT) if u == 1 else held("text%d" % u, [P, HALF], F32)
+            text[u] = at_byte("text_last", [P, HALF], F32, TEXT_AT) if u == last else held("text%d" % u, [P, HALF], F32)
             nc.scalar.activation(text[u][:], text_passes(u, role, n), ACT.Relu)
 
         def open_gate(u):
@@ -278,7 +237,10 @@ def tile_list_gmu_relu_scatP_kernel(
 
         def close_gate(u):
             t, first, count = UNITS[u]
-            gate[u] = at_byte("gate_last", [P, count], F32, GATE_AT) if u == last else ring.tile([P, count], F32, name="gate")
+            if u < VECTOR_UNITS:
+                gate[u] = at_byte("gate%d" % u, [P, count], F32, WV_AT + u * ROW)
+            else:
+                gate[u] = ring.tile([P, count], F32, name="gate")
             mm(z[u], w4_pass("zv", 0, t), v_pass(first, count), False, True)
             nc.scalar.activation(gate[u][:], z[u], ACT.Sigmoid, bias=bias[:, t : t + 1])
 
@@ -293,14 +255,27 @@ def tile_list_gmu_relu_scatP_kernel(
             nc.gpsimd.tensor_tensor(picture[u][:], picture[u][:], text[u][:], ALU.subtract)
             nc.gpsimd.tensor_tensor(picture[u][:], picture[u][:], gate[u][:], ALU.mult)
 
+        def place(u, result):
+            t, first, count = UNITS[u]
+            window = page[t][:].indirect(list1[:, entries(first, count)])
+            if u == last:
+                nc.vector.tensor_tensor(window, result[:], w_wide[:], ALU.mult)
+            else:
+                nc.vector.tensor_copy(window, result[:])
+            if first + count == J:
+                nc.sync.dma_start(out_rows[t], page[t][:])
+
         def finish(u):
             t, first, count = UNITS[u]
+            if u > LAST_TURNED:
+                nc.gpsimd.tensor_tensor(picture[u][:], picture[u][:], text[u][:], ALU.add)
+                return
             blocks = range(count // P)
             turned = bank("turned", u)
             for k in blocks:
                 nc.tensor.matmul(turned[:, block(k)], text[u][:, block(k)], ident[:], start=True, stop=False, is_transpose=True)
                 nc.tensor.matmul(turned[:, block(k)], picture[u][:, block(k)], ident[:], start=False, stop=True, is_transpose=True)
-            weighed = at_byte("weighed_last", [P, count], F32, WEIGHED_AT) if u == last else ring.tile([P, count], F32, name="weighed")
+            weighed = at_byte("weighed_last", [P, count], F32, WEIGHED_AT) if u == LAST_TURNED else ring.tile([P, count], F32, name="weighed")
             for k in blocks:
                 col = first // P + k
                 nc.scalar.activation(weighed[:, block(k)], turned[:, block(k)], ACT.Copy, scale=w_cols[:, col : col + 1])
@@ -309,48 +284,56 @@ def tile_list_gmu_relu_scatP_kernel(
                 nc.tensor.transpose(back[:, block(k)], weighed[:, block(k)], ident[:])
             result = held("result%d" % u, [P, count], F32)
             nc.scalar.copy(result[:], back[:, :count])
-            nc.vector.tensor_copy(page[t][:].indirect(list1[:, entries(first, count)]), result[:])
-            if first + count == J:
-                nc.sync.dma_start(out_rows[t], page[t][:])
+            place(u, result)
 
-        def clear_piece(t, c):
-            nc.gpsimd.memset(page[t][:, c * CHUNK : (c + 1) * CHUNK], 0.0)
+        ht, rest = {}, {}
+        for u in range(VECTOR_UNITS):
+            open_gate(u)
+            close_gate(u)
+            ht[u] = text_passes(u, "back", u)
+            rest[u] = held("rest%d" % u, [P, HALF], F32)
+            nc.gpsimd.tensor_scalar(rest[u][:], gate[u][:], -1.0, 1.0, ALU.mult, ALU.add)
+        w_bank = bank("turned", 1)
+        nc.tensor.transpose(w_bank[:, 0:P], w_rows[:], ident[:])
+        w_cols = held("w_cols", [P, J // P], F32)
+        nc.scalar.copy(w_cols[:], w_bank[:, 0 : J // P])
+        w_first = bank("turned", 0)
+        for k in range(HALF // P):
+            nc.tensor.transpose(w_first[:, block(k)], w_cols[:, k : k + 1].to_broadcast([P, P]), ident[:])
+        for u in range(VECTOR_UNITS):
+            hv = bank("picture", u)
+            mm(hv[:], wv_pass(u), v_pass(0, HALF), True, True)
+            picture[u] = ring.tile([P, HALF], F32, name="picture")
+            nc.vector.scalar_tensor_tensor(picture[u][:], hv[:], 0.0, gate[u][:], ALU.max, ALU.mult)
+        for u in range(VECTOR_UNITS):
+            text[u] = held("share%d" % u, [P, HALF], F32)
+            nc.vector.scalar_tensor_tensor(text[u][:], ht[u], 0.0, rest[u][:], ALU.max, ALU.mult)
+        nc.vector.tensor_tensor(picture[0][:], picture[0][:], text[0][:], ALU.add)
+        first_result = held("result0", [P, HALF], F32)
+        nc.vector.tensor_tensor(first_result[:], picture[0][:], w_first[:], ALU.mult)
+        w_wide = at_byte("w_wide", [P, HALF], F32, WIDE_AT)
+        nc.sync.dma_start(w_wide[:], wgo[:, HALF:])
 
-        ht0 = text_passes(0, "back", 0)
-        open_gate(0)
-        text_sum(1, "turned", 1)
-        open_gate(1)
-        close_gate(0)
-        minus_bias = held("minus_bias", [P, 1], F32)
-        nc.scalar.activation(minus_bias[:], bias[:, 0:1], ACT.Copy, scale=-1.0)
-        rest = held("rest", [P, HALF], F32)
-        nc.scalar.activation(rest[:], z[0], ACT.Sigmoid, bias=minus_bias[:], scale=-1.0)
-        close_gate(1)
-        text[0] = at_byte("share", [P, HALF], F32, SHARE_AT)
-        nc.vector.scalar_tensor_tensor(text[0][:], ht0, 0.0, rest[:], ALU.max, ALU.mult)
-        hv0 = bank("picture", 0)
-        mm(hv0[:], wv_pass(0), v_pass(0, HALF), True, True)
-        picture[0] = ring.tile([P, HALF], F32, name="picture")
-        nc.vector.scalar_tensor_tensor(picture[0][:], hv0[:], 0.0, gate[0][:], ALU.max, ALU.mult)
-        gather_picture_scales(1)
-        gather_picture(1)
-        picture_sum(1)
-        mix(1)
-        for u, role in ((2, "turned"), (3, "back"), (4, "turned"), (5, "back"), (6, "picture")):
-            text_sum(u, role, min(u - 2, 1))
-        for u in range(last + 1):
+
+        def prepare(u):
+            text_sum(u, *TEXT_BANK[u])
+            open_gate(u)
+            close_gate(u)
+            picture_sum(u)
+            mix(u)
+            if u == last:
+                finish(last)
+
+        prepare(2)
+        place(0, first_result)
+        finish(1)
+        prepare(3)
+        prepare(4)
+        for u in range(2, last):
             finish(u)
-            if u == 1:
-                page[3] = at_byte("page3", [P, T], F32, PAGE3_AT)
-            if u == 1:
-                text_sum(last, "back", u)
-            if u + 2 <= last:
-                open_gate(u + 2)
-                close_gate(u + 2)
-                picture_sum(u + 2)
-                mix(u + 2)
-            if 1 <= u <= CHUNKS:
-                clear_piece(3, u - 1)
+            if u + 3 <= last:
+                prepare(u + 3)
+        place(last, picture[last])
 
         pairs = [at_byte("pairs%d" % c, [P, 4 * CHUNK], BF16, (PAIR0_AT, PAIR1_AT, PAIR2_AT, PAIR3_AT)[c]) for c in range(CHUNKS)]
 
@@ -372,7 +355,7 @@ def tile_list_gmu_relu_scatP_kernel(
 
         y_s = held("y_s", [P, T], U8)
         out_words = out_1[0].rearrange("p c i -> p (c i)").bitcast(I32)
-        spare = ("tab2_w", "tab_w", "text2", "zt_raw", "wt_raw")
+        spare = ("tab2_w", "text3", "text2", "zt_raw", "wt_raw")
         grouped = []
         for n, (c, first, width) in enumerate(PIECES):
             grouped.append(held("grouped%d" % n, [P, width, PACK], BF16, tag=spare[n]))

@@ -39,10 +39,13 @@ WV_AT = WS_AT + 3 * N
 V2ROWS_AT = WV_AT + PAGE - LAP
 BIAS_AT = V2ROWS_AT + LAP
 WROWS_AT = V2ROWS_AT + 2 * LAP
-BOTH_AT = V2ROWS_AT + J
+PAGE1_AT = V2ROWS_AT + J - LAP
+PAGE2_AT = PAGE1_AT + PAGE
+BOTH_AT = PAGE2_AT + PAGE - LAP
 VS_AT = BOTH_AT + HALF
-WIDE_AT = BOTH_AT + 2 * ROW - LAP
-PAIR0_AT = WIDE_AT + ROW
+PAGE3_AT = BOTH_AT + 2 * ROW - LAP
+WIDE_AT = BOTH_AT + ROW - LAP
+PAIR0_AT = PAGE3_AT + PAGE
 TEXT_AT = PAIR0_AT + PAIR - LAP
 PAIR1_AT = TEXT_AT + ROW - LAP
 PAIR2_AT = PAIR1_AT + PAIR
@@ -120,20 +123,21 @@ def tile_list_gmu_relu_scatP_kernel(
 
         page = {}
 
-        for t in range(PACK):
-            page[t] = held("page%d" % t, [P, T], F32)
-            for c in range(CHUNKS):
-                nc.gpsimd.memset(page[t][:, c * CHUNK : (c + 1) * CHUNK], 0.0)
+        def clear_page(t, offset):
+            page[t] = at_byte("page%d" % t, [P, T], F32, offset)
+            nc.gpsimd.memset(page[t][:], 0.0)
 
+        page[0] = held("page0", [P, T], F32)
+        nc.gpsimd.memset(page[0][:], 0.0)
         rows = held("rows", [P, J + 3 * N], U8)
+        v2_rows = at_byte("v2_rows", [P, J], U8, V2ROWS_AT)
+        nc.vector.tensor_copy(v2_rows[:], tab2_s[:].indirect(list2[:]))
         nc.vector.tensor_copy(
             rows[:, J:].rearrange("p (a t o i) -> p o a t i", a=3, t=PACK, i=16),
             ws_raw[:].rearrange("p (a o i t) -> p o a t i", a=3, t=PACK, i=16),
         )
         tab_w = at_byte("tab_w", [P, T], I32, TAB_AT)
         nc.sync.dma_start(tab_w[:], tab_words[0].rearrange("p t i -> p (t i)").bitcast(I32))
-        v2_rows = at_byte("v2_rows", [P, J], U8, V2ROWS_AT)
-        nc.vector.tensor_copy(v2_rows[:], tab2_s[:].indirect(list2[:]))
         nc.vector.tensor_copy(rows[:, :J].bitcast(I32), v2_rows[:].bitcast(I32))
         planes = held("planes", [P, 2, J + 3 * N], U8)
         for q in (0, 2, 1, 3):
@@ -146,6 +150,7 @@ def tile_list_gmu_relu_scatP_kernel(
         nc.gpsimd.memset(w_rows[:], 0.0)
         nc.sync.dma_start(w_rows[0 : J // P, :], wgo[0].rearrange("(c p) -> c p", p=P))
 
+        clear_page(1, PAGE1_AT)
         dealt = {}
 
         def deal(name):
@@ -174,9 +179,12 @@ def tile_list_gmu_relu_scatP_kernel(
 
         for h in range(HALVES):
             part_text(h)
-        v_s = at_byte("v_s", [P, J], U8, VS_AT)
-        nc.vector.tensor_copy(v_s[:], tab_s[:].indirect(list1[:]))
+        clear_page(2, PAGE2_AT)
+        clear_page(3, PAGE3_AT)
+        v_s = {}
         for h in range(HALVES):
+            v_s[h] = at_byte("v_s%d" % h, [P, HALF], U8, VS_AT + h * HALF)
+            nc.vector.tensor_copy(v_s[h][:], tab_s[:].indirect(list1[:, entries(h * HALF, HALF)]))
             v_w[h] = held("v_w%d" % h, [P, HALF], U32)
             nc.vector.tensor_copy(v_w[h][:], tab_w[:].bitcast(U32).indirect(list1[:, entries(h * HALF, HALF)]))
 
@@ -184,10 +192,7 @@ def tile_list_gmu_relu_scatP_kernel(
             rounded = held("wv_bf%d" % g, [P, 2 * P * PACK], BF16)
             grouped_wv = rounded[:].rearrange("p (t m i) -> p m t i", t=2, i=PACK)
             raw_wv = wv_raw[:].rearrange("p i (m t) -> p m t i", t=PACK)[:, :, 2 * g : 2 * g + 2, :]
-            if g == 0:
-                nc.scalar.copy(grouped_wv, raw_wv)
-            else:
-                nc.gpsimd.tensor_scalar(grouped_wv, raw_wv, 1.0, -0.0, ALU.mult, ALU.add)
+            nc.scalar.copy(grouped_wv, raw_wv)
             words = held("wv_w%d" % g, [P, 2 * P], U32)
             scales = held("wv_s%d" % g, [P, 2 * P], U8)
             nc.vector.quantize_mx(out=words[:].bitcast(FP8X4), scales=scales[:], in_=rounded[:])
@@ -205,7 +210,7 @@ def tile_list_gmu_relu_scatP_kernel(
 
         def v_pass(first, count):
             cols = slice(first % HALF, first % HALF + count)
-            return v_w[first // HALF][:, cols].bitcast(FP8X4), v_s[:, first : first + count]
+            return v_w[first // HALF][:, cols].bitcast(FP8X4), v_s[first // HALF][:, cols]
 
         def v2_pass(first, count, d):
             at = first % HALF
@@ -237,8 +242,8 @@ def tile_list_gmu_relu_scatP_kernel(
 
         def close_gate(u):
             t, first, count = UNITS[u]
-            if u < VECTOR_UNITS:
-                gate[u] = at_byte("gate%d" % u, [P, count], F32, WV_AT + u * ROW)
+            if u == 1:
+                gate[u] = at_byte("gate1", [P, count], F32, WV_AT)
             else:
                 gate[u] = ring.tile([P, count], F32, name="gate")
             mm(z[u], w4_pass("zv", 0, t), v_pass(first, count), False, True)
@@ -257,11 +262,7 @@ def tile_list_gmu_relu_scatP_kernel(
 
         def place(u, result):
             t, first, count = UNITS[u]
-            window = page[t][:].indirect(list1[:, entries(first, count)])
-            if u == last:
-                nc.vector.tensor_tensor(window, result[:], w_wide[:], ALU.mult)
-            else:
-                nc.vector.tensor_copy(window, result[:])
+            nc.vector.tensor_copy(page[t][:].indirect(list1[:, entries(first, count)]), result[:])
             if first + count == J:
                 nc.sync.dma_start(out_rows[t], page[t][:])
 
@@ -269,6 +270,7 @@ def tile_list_gmu_relu_scatP_kernel(
             t, first, count = UNITS[u]
             if u > LAST_TURNED:
                 nc.gpsimd.tensor_tensor(picture[u][:], picture[u][:], text[u][:], ALU.add)
+                nc.gpsimd.tensor_tensor(picture[u][:], picture[u][:], w_wide[:], ALU.mult)
                 return
             blocks = range(count // P)
             turned = bank("turned", u)
@@ -300,17 +302,23 @@ def tile_list_gmu_relu_scatP_kernel(
         w_first = bank("turned", 0)
         for k in range(HALF // P):
             nc.tensor.transpose(w_first[:, block(k)], w_cols[:, k : k + 1].to_broadcast([P, P]), ident[:])
-        for u in range(VECTOR_UNITS):
+        def share(u):
+            text[u] = held("share%d" % u, [P, HALF], F32)
+            nc.vector.scalar_tensor_tensor(text[u][:], ht[u], 0.0, rest[u][:], ALU.max, ALU.mult)
+
+        def product(u):
             hv = bank("picture", u)
             mm(hv[:], wv_pass(u), v_pass(0, HALF), True, True)
             picture[u] = ring.tile([P, HALF], F32, name="picture")
             nc.vector.scalar_tensor_tensor(picture[u][:], hv[:], 0.0, gate[u][:], ALU.max, ALU.mult)
-        for u in range(VECTOR_UNITS):
-            text[u] = held("share%d" % u, [P, HALF], F32)
-            nc.vector.scalar_tensor_tensor(text[u][:], ht[u], 0.0, rest[u][:], ALU.max, ALU.mult)
+
+        share(0)
+        product(0)
         nc.vector.tensor_tensor(picture[0][:], picture[0][:], text[0][:], ALU.add)
+        product(1)
         first_result = held("result0", [P, HALF], F32)
         nc.vector.tensor_tensor(first_result[:], picture[0][:], w_first[:], ALU.mult)
+        share(1)
         w_wide = at_byte("w_wide", [P, HALF], F32, WIDE_AT)
         nc.sync.dma_start(w_wide[:], wgo[:, HALF:])
 

@@ -35,10 +35,10 @@ ROW = 4 * HALF
 PAIR = 8 * CHUNK
 TAB_AT = 0
 WS_AT = TAB_AT + PAGE - LAP
-WV_AT = WS_AT + 3 * N
+ZV_AT = WS_AT + 3 * N - LAP
+WV_AT = ZV_AT + 2 * N
 V2ROWS_AT = WV_AT + PAGE - LAP
 BIAS_AT = V2ROWS_AT + LAP
-WROWS_AT = V2ROWS_AT + 2 * LAP
 PAGE1_AT = V2ROWS_AT + J - LAP
 PAGE2_AT = PAGE1_AT + PAGE
 BOTH_AT = PAGE2_AT + PAGE - LAP
@@ -79,13 +79,15 @@ def tile_list_gmu_relu_scatP_kernel(
         tab2_s = held("tab2_s", [P, T], U8)
         tab2_w = held("tab2_w", [P, T], I32)
         ws_raw = at_byte("ws_raw", [P, 3 * N], U8, WS_AT)
-        raw = {name: held(name + "_raw", [P, passes, 2 * N], U8) for name, passes in (("wt", 2), ("zt", 2), ("zv", 1))}
+        raw = {name: held(name + "_raw", [P, passes, 2 * N], U8) for name, passes in (("wt", 2), ("zt", 2))}
+        w_rows = held("w_rows", [P, P], F32)
         ident = held("ident", [P, P], F32)
         warm = held("warm", [P, 8], F32)
 
         nc.vector.memset(warm[:], 0.0)
         nc.vector.memset(ws_raw[:, 2 * N :].bitcast(I32), 0)
         nc.vector.memset(tab_s[:].bitcast(I32), 0)
+        nc.vector.memset(w_rows[:], 0.0)
         for rows32 in (slice(32, 64), slice(64, 128)):
             nc.vector.memset(ws_raw[rows32, : 2 * N].bitcast(I32), 0)
         for rows32 in (slice(32, 64), slice(64, 128)):
@@ -106,9 +108,9 @@ def tile_list_gmu_relu_scatP_kernel(
         load_words("zt")
         nc.sync.dma_start(list1[:], offs)
         load_words("wt")
-        load_words("zv")
         for r in range(4):
             nc.scalar.dma_start(tab_s[r:P:32, :].bitcast(I32), tab_scales[0, r:16:4, :].bitcast(I32))
+        nc.scalar.dma_start(w_rows[0 : J // P, :], wgo[0].rearrange("(c p) -> c p", p=P))
 
         nc.scalar.activation(warm[:, 0:1], warm[:, 1:2], ACT.Sigmoid)
 
@@ -138,6 +140,8 @@ def tile_list_gmu_relu_scatP_kernel(
         )
         tab_w = at_byte("tab_w", [P, T], I32, TAB_AT)
         nc.sync.dma_start(tab_w[:], tab_words[0].rearrange("p t i -> p (t i)").bitcast(I32))
+        raw["zv"] = at_byte("zv_raw", [P, 1, 2 * N], U8, ZV_AT)
+        load_words("zv")
         nc.vector.tensor_copy(rows[:, :J].bitcast(I32), v2_rows[:].bitcast(I32))
         planes = held("planes", [P, 2, J + 3 * N], U8)
         for q in (0, 2, 1, 3):
@@ -146,9 +150,6 @@ def tile_list_gmu_relu_scatP_kernel(
         nc.sync.dma_start(wv_raw[:], wv.rearrange("(p i) n -> p i n", i=PACK))
         bias = at_byte("bias", [P, PACK], F32, BIAS_AT)
         nc.sync.dma_start(bias[:], b.rearrange("(p t) -> p t", t=PACK))
-        w_rows = at_byte("w_rows", [P, P], F32, WROWS_AT)
-        nc.gpsimd.memset(w_rows[:], 0.0)
-        nc.sync.dma_start(w_rows[0 : J // P, :], wgo[0].rearrange("(c p) -> c p", p=P))
 
         clear_page(1, PAGE1_AT)
         dealt = {}
@@ -192,7 +193,7 @@ def tile_list_gmu_relu_scatP_kernel(
             rounded = held("wv_bf%d" % g, [P, 2 * P * PACK], BF16)
             grouped_wv = rounded[:].rearrange("p (t m i) -> p m t i", t=2, i=PACK)
             raw_wv = wv_raw[:].rearrange("p i (m t) -> p m t i", t=PACK)[:, :, 2 * g : 2 * g + 2, :]
-            nc.scalar.copy(grouped_wv, raw_wv)
+            (nc.scalar.copy, nc.vector.tensor_copy)[g](grouped_wv, raw_wv)
             words = held("wv_w%d" % g, [P, 2 * P], U32)
             scales = held("wv_s%d" % g, [P, 2 * P], U8)
             nc.vector.quantize_mx(out=words[:].bitcast(FP8X4), scales=scales[:], in_=rounded[:])
@@ -316,9 +317,9 @@ def tile_list_gmu_relu_scatP_kernel(
         product(0)
         nc.vector.tensor_tensor(picture[0][:], picture[0][:], text[0][:], ALU.add)
         product(1)
+        share(1)
         first_result = held("result0", [P, HALF], F32)
         nc.vector.tensor_tensor(first_result[:], picture[0][:], w_first[:], ALU.mult)
-        share(1)
         w_wide = at_byte("w_wide", [P, HALF], F32, WIDE_AT)
         nc.sync.dma_start(w_wide[:], wgo[:, HALF:])
 
@@ -343,41 +344,49 @@ def tile_list_gmu_relu_scatP_kernel(
                 prepare(u + 3)
         place(last, picture[last])
 
-        pairs = [at_byte("pairs%d" % c, [P, 4 * CHUNK], BF16, (PAIR0_AT, PAIR1_AT, PAIR2_AT, PAIR3_AT)[c]) for c in range(CHUNKS)]
+        pairs = [at_byte("pairs%d" % c, [P, 4 * CHUNK], BF16, (PAIR2_AT, PAIR3_AT, PAIR0_AT, PAIR1_AT)[c]) for c in range(CHUNKS)]
 
         def round_page(t, c):
             rows_f32 = page[t][:, c * CHUNK : (c + 1) * CHUNK]
             words = pairs[c][:, t // 2 * 2 * CHUNK : (t // 2 + 1) * 2 * CHUNK].rearrange("p (c i) -> p c i", i=2)
-            if c >= VECTOR_CHUNKS:
-                nc.scalar.copy(words[:, :, t % 2], rows_f32)
-            elif t == PACK - 1:
-                nc.vector.tensor_copy(words[:, :, 1], rows_f32)
-            elif t == PACK - 2:
-                nc.gpsimd.tensor_scalar(words, rows_f32.unsqueeze(2).to_broadcast([P, CHUNK, 2]), 1.0, -0.0, ALU.mult, ALU.add)
+            twice = rows_f32.unsqueeze(2).to_broadcast([P, CHUNK, 2])
+            if t == PACK - 2:
+                out, source = words, twice
             else:
-                nc.gpsimd.tensor_scalar(words[:, :, t], rows_f32, 1.0, -0.0, ALU.mult, ALU.add)
+                out, source = words[:, :, t % 2], rows_f32
+            if c < VECTOR_CHUNKS or t == PACK - 1:
+                nc.scalar.copy(out, source)
+            else:
+                nc.gpsimd.tensor_scalar(out, source, 1.0, -0.0, ALU.mult, ALU.add)
 
-        for t in range(PACK):
+        spare = ("tab2_w", "text3", "text2", "zt_raw", "wt_raw")
+        grouped = {}
+
+        def weave(n):
+            c, first, width = PIECES[n]
+            grouped[n] = held("grouped%d" % n, [P, width, PACK], BF16, tag=spare[n])
+            woven = grouped[n][:].rearrange("p c i -> p (c i)").bitcast(U32).rearrange("p (c a) -> p c a", a=2)
+            nc.scalar.copy(woven, pairs[c][:].bitcast(U32).rearrange("p (a c) -> p c a", a=2)[:, first : first + width, :])
+
+        for t in range(PACK - 1):
             for c in range(CHUNKS):
                 round_page(t, c)
+        for n in range(VECTOR_CHUNKS):
+            weave(n)
+        for c in range(VECTOR_CHUNKS):
+            nc.vector.tensor_copy(grouped[c][:, :, PACK - 1], page[PACK - 1][:, c * CHUNK : (c + 1) * CHUNK])
+        round_page(PACK - 1, 2)
+        weave(2)
+        round_page(PACK - 1, 3)
+        weave(3)
+        weave(4)
 
         y_s = held("y_s", [P, T], U8)
+        y_w = held("y_w", [P, T], I32)
         out_words = out_1[0].rearrange("p c i -> p (c i)").bitcast(I32)
-        spare = ("tab2_w", "text3", "text2", "zt_raw", "wt_raw")
-        grouped = []
-        for n, (c, first, width) in enumerate(PIECES):
-            grouped.append(held("grouped%d" % n, [P, width, PACK], BF16, tag=spare[n]))
-            word = I32 if c < VECTOR_CHUNKS else U32
-            woven = grouped[n][:].rearrange("p c i -> p (c i)").bitcast(word).rearrange("p (c a) -> p c a", a=2)
-            parts = pairs[c][:].bitcast(word).rearrange("p (a c) -> p c a", a=2)[:, first : first + width, :]
-            if c < VECTOR_CHUNKS:
-                nc.vector.tensor_copy(woven, parts)
-            else:
-                nc.scalar.copy(woven, parts)
         for n, (c, first, width) in enumerate(PIECES):
             cols = slice(c * CHUNK + first, c * CHUNK + first + width)
-            y_w = held("y_w%d" % n, [P, width], I32)
-            nc.vector.quantize_mx(out=y_w[:].bitcast(FP8X4), scales=y_s[:, cols], in_=grouped[n][:].rearrange("p c i -> p (c i)"))
-            nc.sync.dma_start(out_words[:, cols], y_w[:])
+            nc.vector.quantize_mx(out=y_w[:, cols].bitcast(FP8X4), scales=y_s[:, cols], in_=grouped[n][:].rearrange("p c i -> p (c i)"))
+            nc.sync.dma_start(out_words[:, cols], y_w[:, cols])
         for r in range(4):
             nc.scalar.dma_start(out_2[0, r:16:4, :].bitcast(I32), y_s[r:P:32, :].bitcast(I32))

@@ -33,12 +33,13 @@ LAP = 64
 PAGE = 4 * T
 ROW = 4 * HALF
 PAIR = 8 * CHUNK
-TAB_AT = 0
-WS_AT = TAB_AT + PAGE - LAP
+TABS_AT = 0
+WS_AT = TABS_AT + T - LAP
 ZV_AT = WS_AT + 3 * N - LAP
 WV_AT = ZV_AT + 2 * N
 V2ROWS_AT = WV_AT + PAGE - LAP
 BIAS_AT = V2ROWS_AT + LAP
+WROWS_AT = V2ROWS_AT + 2 * LAP
 PAGE1_AT = V2ROWS_AT + J - LAP
 PAGE2_AT = PAGE1_AT + PAGE
 BOTH_AT = PAGE2_AT + PAGE - LAP
@@ -75,23 +76,20 @@ def tile_list_gmu_relu_scatP_kernel(
 
         list1 = held("list1", [P, J // 16], U16)
         list2 = held("list2", [P, J // 16], U16)
-        tab_s = held("tab_s", [P, T], U8)
+        tab_w = held("tab_w", [P, T], I32)
         tab2_s = held("tab2_s", [P, T], U8)
         tab2_w = held("tab2_w", [P, T], I32)
         ws_raw = at_byte("ws_raw", [P, 3 * N], U8, WS_AT)
         raw = {name: held(name + "_raw", [P, passes, 2 * N], U8) for name, passes in (("wt", 2), ("zt", 2))}
-        w_rows = held("w_rows", [P, P], F32)
         ident = held("ident", [P, P], F32)
         warm = held("warm", [P, 8], F32)
 
+        nc.gpsimd.memset(ws_raw[:, 2 * N :].bitcast(I32), 0)
         nc.vector.memset(warm[:], 0.0)
-        nc.vector.memset(ws_raw[:, 2 * N :].bitcast(I32), 0)
-        nc.vector.memset(tab_s[:].bitcast(I32), 0)
-        nc.vector.memset(w_rows[:], 0.0)
-        for rows32 in (slice(32, 64), slice(64, 128)):
-            nc.vector.memset(ws_raw[rows32, : 2 * N].bitcast(I32), 0)
         for rows32 in (slice(32, 64), slice(64, 128)):
             nc.gpsimd.memset(tab2_s[rows32, :].bitcast(I32), 0)
+        for rows32 in (slice(32, 64), slice(64, 128)):
+            nc.vector.memset(ws_raw[rows32, : 2 * N].bitcast(I32), 0)
         make_identity(nc, ident[:])
 
         words_in = {"zt": zt_words, "wt": wt_words, "zv": zv_words}
@@ -104,13 +102,11 @@ def tile_list_gmu_relu_scatP_kernel(
         nc.scalar.dma_start(ws_raw[0:32, 0:N].bitcast(I32), zt_scales.rearrange("a q n -> q a n").bitcast(I32))
         nc.scalar.dma_start(ws_raw[0:32, N : 2 * N].bitcast(I32), wt_scales.rearrange("a q n -> q a n").bitcast(I32))
         nc.scalar.dma_start(ws_raw[0:32:2, 2 * N :].bitcast(I32), zv_scales[0].bitcast(I32))
+        nc.sync.dma_start(list1[:], offs)
         nc.sync.dma_start(tab2_w[:], tab2_words[0].rearrange("p t i -> p (t i)").bitcast(I32))
         load_words("zt")
-        nc.sync.dma_start(list1[:], offs)
         load_words("wt")
-        for r in range(4):
-            nc.scalar.dma_start(tab_s[r:P:32, :].bitcast(I32), tab_scales[0, r:16:4, :].bitcast(I32))
-        nc.scalar.dma_start(w_rows[0 : J // P, :], wgo[0].rearrange("(c p) -> c p", p=P))
+        nc.sync.dma_start(tab_w[:], tab_words[0].rearrange("p t i -> p (t i)").bitcast(I32))
 
         nc.scalar.activation(warm[:, 0:1], warm[:, 1:2], ACT.Sigmoid)
 
@@ -138,8 +134,6 @@ def tile_list_gmu_relu_scatP_kernel(
             rows[:, J:].rearrange("p (a t o i) -> p o a t i", a=3, t=PACK, i=16),
             ws_raw[:].rearrange("p (a o i t) -> p o a t i", a=3, t=PACK, i=16),
         )
-        tab_w = at_byte("tab_w", [P, T], I32, TAB_AT)
-        nc.sync.dma_start(tab_w[:], tab_words[0].rearrange("p t i -> p (t i)").bitcast(I32))
         raw["zv"] = at_byte("zv_raw", [P, 1, 2 * N], U8, ZV_AT)
         load_words("zv")
         nc.vector.tensor_copy(rows[:, :J].bitcast(I32), v2_rows[:].bitcast(I32))
@@ -150,6 +144,13 @@ def tile_list_gmu_relu_scatP_kernel(
         nc.sync.dma_start(wv_raw[:], wv.rearrange("(p i) n -> p i n", i=PACK))
         bias = at_byte("bias", [P, PACK], F32, BIAS_AT)
         nc.sync.dma_start(bias[:], b.rearrange("(p t) -> p t", t=PACK))
+        tab_s = at_byte("tab_s", [P, T], U8, TABS_AT)
+        nc.gpsimd.memset(tab_s[:].bitcast(I32), 0)
+        for r in range(4):
+            nc.sync.dma_start(tab_s[r:P:32, :].bitcast(I32), tab_scales[0, r:16:4, :].bitcast(I32))
+        w_rows = at_byte("w_rows", [P, P], F32, WROWS_AT)
+        nc.gpsimd.memset(w_rows[:], 0.0)
+        nc.sync.dma_start(w_rows[0 : J // P, :], wgo[0].rearrange("(c p) -> c p", p=P))
 
         clear_page(1, PAGE1_AT)
         dealt = {}
@@ -169,7 +170,8 @@ def tile_list_gmu_relu_scatP_kernel(
 
         v2_w, v_w, wv_w, wv_s = {}, {}, {}, {}
         both = at_byte("both", [P, J], U32, BOTH_AT)
-        nc.vector.tensor_copy(both[:], tab2_w[:].bitcast(U32).indirect(list2[:]))
+        for h in range(HALVES):
+            nc.vector.tensor_copy(both[:, half_cols(h)], tab2_w[:].bitcast(U32).indirect(list2[:, entries(h * HALF, HALF)]))
 
         def part_text(h):
             v2_w[h] = held("v2_w%d" % h, [P, 2, 2 * HALF], U8)
@@ -184,10 +186,11 @@ def tile_list_gmu_relu_scatP_kernel(
         clear_page(3, PAGE3_AT)
         v_s = {}
         for h in range(HALVES):
-            v_s[h] = at_byte("v_s%d" % h, [P, HALF], U8, VS_AT + h * HALF)
-            nc.vector.tensor_copy(v_s[h][:], tab_s[:].indirect(list1[:, entries(h * HALF, HALF)]))
             v_w[h] = held("v_w%d" % h, [P, HALF], U32)
             nc.vector.tensor_copy(v_w[h][:], tab_w[:].bitcast(U32).indirect(list1[:, entries(h * HALF, HALF)]))
+        for h in range(HALVES):
+            v_s[h] = at_byte("v_s%d" % h, [P, HALF], U8, VS_AT + h * HALF)
+            nc.vector.tensor_copy(v_s[h][:], tab_s[:].indirect(list1[:, entries(h * HALF, HALF)]))
 
         for g in range(2):
             rounded = held("wv_bf%d" % g, [P, 2 * P * PACK], BF16)
@@ -223,6 +226,7 @@ def tile_list_gmu_relu_scatP_kernel(
         last = len(UNITS) - 1
         out_rows = out_0.rearrange("(p t) c -> t p c", t=PACK)
         text, gate, picture, z = {}, {}, {}, {}
+        last_page = held("last_page", [P, J], F32)
 
         def text_passes(u, role, n):
             t, first, count = UNITS[u]
@@ -271,7 +275,7 @@ def tile_list_gmu_relu_scatP_kernel(
             t, first, count = UNITS[u]
             if u > LAST_TURNED:
                 nc.gpsimd.tensor_tensor(picture[u][:], picture[u][:], text[u][:], ALU.add)
-                nc.gpsimd.tensor_tensor(picture[u][:], picture[u][:], w_wide[:], ALU.mult)
+                nc.gpsimd.tensor_tensor(last_page[:, HALF:], picture[u][:], w_wide[:], ALU.mult)
                 return
             blocks = range(count // P)
             turned = bank("turned", u)
@@ -285,6 +289,9 @@ def tile_list_gmu_relu_scatP_kernel(
             back = bank("back", u)
             for k in blocks:
                 nc.tensor.transpose(back[:, block(k)], weighed[:, block(k)], ident[:])
+            if u == last - 1:
+                nc.scalar.copy(last_page[:, :HALF], back[:, :count])
+                return
             result = held("result%d" % u, [P, count], F32)
             nc.scalar.copy(result[:], back[:, :count])
             place(u, result)
@@ -296,7 +303,7 @@ def tile_list_gmu_relu_scatP_kernel(
             ht[u] = text_passes(u, "back", u)
             rest[u] = held("rest%d" % u, [P, HALF], F32)
             nc.gpsimd.tensor_scalar(rest[u][:], gate[u][:], -1.0, 1.0, ALU.mult, ALU.add)
-        w_bank = bank("turned", 1)
+        w_bank = bank("gate", 1)
         nc.tensor.transpose(w_bank[:, 0:P], w_rows[:], ident[:])
         w_cols = held("w_cols", [P, J // P], F32)
         nc.scalar.copy(w_cols[:], w_bank[:, 0 : J // P])
@@ -342,7 +349,8 @@ def tile_list_gmu_relu_scatP_kernel(
             finish(u)
             if u + 3 <= last:
                 prepare(u + 3)
-        place(last, picture[last])
+        nc.vector.tensor_copy(page[PACK - 1][:].indirect(list1[:]), last_page[:])
+        nc.sync.dma_start(out_rows[PACK - 1], page[PACK - 1][:])
 
         pairs = [at_byte("pairs%d" % c, [P, 4 * CHUNK], BF16, (PAIR2_AT, PAIR3_AT, PAIR0_AT, PAIR1_AT)[c]) for c in range(CHUNKS)]
 

@@ -43,8 +43,9 @@ WROWS_AT = V2ROWS_AT + 2 * LAP
 PAGE1_AT = V2ROWS_AT + J - LAP
 PAGE2_AT = PAGE1_AT + PAGE
 BOTH_AT = PAGE2_AT + PAGE - LAP
-VS_AT = BOTH_AT + HALF
-PAGE3_AT = BOTH_AT + 2 * ROW - LAP
+ROUNDED_AT = BOTH_AT + 2 * ROW
+VS_AT = ROUNDED_AT + LAP
+PAGE3_AT = ROUNDED_AT + ROW - LAP
 WIDE_AT = BOTH_AT + ROW - LAP
 PAIR0_AT = PAGE3_AT + PAGE
 TEXT_AT = PAIR0_AT + PAIR - LAP
@@ -183,25 +184,28 @@ def tile_list_gmu_relu_scatP_kernel(
         for h in range(HALVES):
             part_text(h)
         clear_page(2, PAGE2_AT)
-        clear_page(3, PAGE3_AT)
-        v_s = {}
         for h in range(HALVES):
             v_w[h] = held("v_w%d" % h, [P, HALF], U32)
             nc.vector.tensor_copy(v_w[h][:], tab_w[:].bitcast(U32).indirect(list1[:, entries(h * HALF, HALF)]))
-        for h in range(HALVES):
-            v_s[h] = at_byte("v_s%d" % h, [P, HALF], U8, VS_AT + h * HALF)
-            nc.vector.tensor_copy(v_s[h][:], tab_s[:].indirect(list1[:, entries(h * HALF, HALF)]))
 
-        for g in range(2):
-            rounded = held("wv_bf%d" % g, [P, 2 * P * PACK], BF16)
-            grouped_wv = rounded[:].rearrange("p (t m i) -> p m t i", t=2, i=PACK)
-            raw_wv = wv_raw[:].rearrange("p i (m t) -> p m t i", t=PACK)[:, :, 2 * g : 2 * g + 2, :]
-            (nc.scalar.copy, nc.vector.tensor_copy)[g](grouped_wv, raw_wv)
+        def quantise_wv(g, rounded, copy):
+            copy(
+                rounded[:].rearrange("p (t m i) -> p m t i", t=2, i=PACK),
+                wv_raw[:].rearrange("p i (m t) -> p m t i", t=PACK)[:, :, 2 * g : 2 * g + 2, :],
+            )
             words = held("wv_w%d" % g, [P, 2 * P], U32)
             scales = held("wv_s%d" % g, [P, 2 * P], U8)
             nc.vector.quantize_mx(out=words[:].bitcast(FP8X4), scales=scales[:], in_=rounded[:])
             for n in range(2):
                 wv_w[2 * g + n], wv_s[2 * g + n] = words[:, block(n)], scales[:, block(n)]
+
+        quantise_wv(0, held("wv_bf0", [P, 2 * P * PACK], BF16), nc.vector.tensor_copy)
+        quantise_wv(1, at_byte("wv_bf1", [P, 2 * P * PACK], BF16, ROUNDED_AT), nc.scalar.copy)
+        clear_page(3, PAGE3_AT)
+        v_s = {}
+        for h in range(HALVES):
+            v_s[h] = at_byte("v_s%d" % h, [P, HALF], U8, VS_AT + h * HALF)
+            nc.vector.tensor_copy(v_s[h][:], tab_s[:].indirect(list1[:, entries(h * HALF, HALF)]))
 
         scale_run = {"zt": 0, "wt": 1, "zv": 2}
 
@@ -247,10 +251,7 @@ def tile_list_gmu_relu_scatP_kernel(
 
         def close_gate(u):
             t, first, count = UNITS[u]
-            if u == 1:
-                gate[u] = at_byte("gate1", [P, count], F32, WV_AT)
-            else:
-                gate[u] = ring.tile([P, count], F32, name="gate")
+            gate[u] = ring.tile([P, count], F32, name="gate")
             mm(z[u], w4_pass("zv", 0, t), v_pass(first, count), False, True)
             nc.scalar.activation(gate[u][:], z[u], ACT.Sigmoid, bias=bias[:, t : t + 1])
 
@@ -302,7 +303,10 @@ def tile_list_gmu_relu_scatP_kernel(
             close_gate(u)
             ht[u] = text_passes(u, "back", u)
             rest[u] = held("rest%d" % u, [P, HALF], F32)
-            nc.gpsimd.tensor_scalar(rest[u][:], gate[u][:], -1.0, 1.0, ALU.mult, ALU.add)
+            if u == 0:
+                nc.scalar.activation(rest[u][:], gate[u][:], ACT.Copy, bias=1.0, scale=-1.0)
+            else:
+                nc.gpsimd.tensor_scalar(rest[u][:], gate[u][:], -1.0, 1.0, ALU.mult, ALU.add)
         w_bank = bank("gate", 1)
         nc.tensor.transpose(w_bank[:, 0:P], w_rows[:], ident[:])
         w_cols = held("w_cols", [P, J // P], F32)

@@ -26,7 +26,8 @@ CHUNKS = T // CHUNK
 VECTOR_CHUNKS = 2
 PIECES = ((0, 0, 512), (1, 0, 512), (2, 0, 512), (3, 0, 256), (3, 256, 256))
 UNITS = tuple((t, h * HALF, HALF) for t, h in ((0, 0), (1, 0), (2, 0), (0, 1), (1, 1), (2, 1), (3, 0), (3, 1)))
-TEXT_BANK = {2: ("turned", 1), 3: ("picture", 0), 4: ("back", 0), 5: ("back", 1), 6: ("back", 0), 7: ("back", 1)}
+TEXT_BANK = {3: ("picture", 0), 4: ("back", 0), 5: ("back", 1), 6: ("back", 0), 7: ("back", 1)}
+EARLY_BANK = {("gate", 2): ("turned", 1), ("picture", 2): ("gate", 0)}
 LAST_TURNED = 6
 VECTOR_UNITS = 2
 LAP = 64
@@ -73,7 +74,8 @@ def tile_list_gmu_relu_scatP_kernel(
             return placed.tile(shape, dtype, name=name, tag=name, align_bytes=64, offset=offset)
 
         def bank(role, u):
-            return psum.tile([P, HALF], F32, name="bank", tag="%s%d" % (role, u % 2))
+            role, n = EARLY_BANK.get((role, u), (role, u % 2))
+            return psum.tile([P, HALF], F32, name="bank", tag="%s%d" % (role, n))
 
         list1 = held("list1", [P, J // 16], U16)
         list2 = held("list2", [P, J // 16], U16)
@@ -146,7 +148,7 @@ def tile_list_gmu_relu_scatP_kernel(
         bias = at_byte("bias", [P, PACK], F32, BIAS_AT)
         nc.sync.dma_start(bias[:], b.rearrange("(p t) -> p t", t=PACK))
         tab_s = at_byte("tab_s", [P, T], U8, TABS_AT)
-        nc.gpsimd.memset(tab_s[:].bitcast(I32), 0)
+        nc.vector.memset(tab_s[:].bitcast(I32), 0)
         for r in range(4):
             nc.sync.dma_start(tab_s[r:P:32, :].bitcast(I32), tab_scales[0, r:16:4, :].bitcast(I32))
         w_rows = at_byte("w_rows", [P, P], F32, WROWS_AT)
@@ -258,13 +260,14 @@ def tile_list_gmu_relu_scatP_kernel(
         def picture_sum(u):
             t, first, count = UNITS[u]
             picture[u] = ring.tile([P, count], F32, name="picture")
-            hv = bank("picture", u)[:, :count]
-            mm(hv, wv_pass(t), v_pass(first, count), True, True)
-            nc.scalar.activation(picture[u][:], hv, ACT.Relu)
+            total = bank("picture", u)[:, :count]
+            mm(total, wv_pass(t), v_pass(first, count), True, True)
+            nc.scalar.activation(picture[u][:], total, ACT.Relu)
 
         def mix(u):
-            nc.gpsimd.tensor_tensor(picture[u][:], picture[u][:], text[u][:], ALU.subtract)
-            nc.gpsimd.tensor_tensor(picture[u][:], picture[u][:], gate[u][:], ALU.mult)
+            difference = held("difference", [P, HALF], F32, tag="share0") if u == VECTOR_UNITS else picture[u]
+            nc.gpsimd.tensor_tensor(difference[:], picture[u][:], text[u][:], ALU.subtract)
+            nc.gpsimd.tensor_tensor(picture[u][:], difference[:], gate[u][:], ALU.mult)
 
         def place(u, result):
             t, first, count = UNITS[u]
@@ -297,17 +300,21 @@ def tile_list_gmu_relu_scatP_kernel(
             nc.scalar.copy(result[:], back[:, :count])
             place(u, result)
 
-        ht, rest = {}, {}
+        ht, hv, rest = {}, {}, {}
         for u in range(VECTOR_UNITS):
             open_gate(u)
-            close_gate(u)
             ht[u] = text_passes(u, "back", u)
+        for u in range(VECTOR_UNITS):
+            close_gate(u)
+            hv[u] = bank("picture", u)
+            mm(hv[u][:], wv_pass(u), v_pass(0, HALF), True, True)
             rest[u] = held("rest%d" % u, [P, HALF], F32)
             if u == 0:
                 nc.scalar.activation(rest[u][:], gate[u][:], ACT.Copy, bias=1.0, scale=-1.0)
             else:
                 nc.gpsimd.tensor_scalar(rest[u][:], gate[u][:], -1.0, 1.0, ALU.mult, ALU.add)
-        w_bank = bank("gate", 1)
+        text_sum(VECTOR_UNITS, "turned", 1)
+        w_bank = bank("turned", 1)
         nc.tensor.transpose(w_bank[:, 0:P], w_rows[:], ident[:])
         w_cols = held("w_cols", [P, J // P], F32)
         nc.scalar.copy(w_cols[:], w_bank[:, 0 : J // P])
@@ -319,15 +326,13 @@ def tile_list_gmu_relu_scatP_kernel(
             nc.vector.scalar_tensor_tensor(text[u][:], ht[u], 0.0, rest[u][:], ALU.max, ALU.mult)
 
         def product(u):
-            hv = bank("picture", u)
-            mm(hv[:], wv_pass(u), v_pass(0, HALF), True, True)
             picture[u] = ring.tile([P, HALF], F32, name="picture")
-            nc.vector.scalar_tensor_tensor(picture[u][:], hv[:], 0.0, gate[u][:], ALU.max, ALU.mult)
+            nc.vector.scalar_tensor_tensor(picture[u][:], hv[u][:], 0.0, gate[u][:], ALU.max, ALU.mult)
 
-        share(0)
         product(0)
-        nc.vector.tensor_tensor(picture[0][:], picture[0][:], text[0][:], ALU.add)
+        share(0)
         product(1)
+        nc.vector.tensor_tensor(picture[0][:], picture[0][:], text[0][:], ALU.add)
         share(1)
         first_result = held("result0", [P, HALF], F32)
         nc.vector.tensor_tensor(first_result[:], picture[0][:], w_first[:], ALU.mult)
@@ -336,10 +341,11 @@ def tile_list_gmu_relu_scatP_kernel(
 
 
         def prepare(u):
-            text_sum(u, *TEXT_BANK[u])
+            if u in TEXT_BANK:
+                text_sum(u, *TEXT_BANK[u])
             open_gate(u)
-            close_gate(u)
             picture_sum(u)
+            close_gate(u)
             mix(u)
             if u == last:
                 finish(last)

from contextlib import ExitStack

import concourse.mybir as mybir
from concourse.masks import make_identity

K, L, N, T, J = 512, 1024, 512, 2048, 1024
FLOPS = 2 * J * N * (2 * K + 2 * L)

F32 = mybir.dt.float32
BF16 = mybir.dt.bfloat16
I32 = mybir.dt.int32
U32 = mybir.dt.uint32
U16 = mybir.dt.uint16
U8 = mybir.dt.uint8
FP8X4 = mybir.dt.float8_e4m3fn_x4
FP4X4 = mybir.dt.float4_e2m1fn_x4
ALU = mybir.AluOpType
ACT = mybir.ActivationFunctionType

P = 128
PACK = 4
HALF = 512
HALVES = J // HALF
CHUNK = 512
CHUNKS = T // CHUNK
VECTOR_CHUNKS = 2
PIECES = ((0, 0, 512), (1, 0, 512), (2, 0, 512), (3, 0, 256), (3, 256, 256))
UNITS = tuple((t, h * HALF, HALF) for t, h in ((0, 0), (1, 0), (2, 0), (0, 1), (1, 1), (2, 1), (3, 0), (3, 1)))
TEXT_BANK = {3: ("picture", 0), 4: ("back", 0), 5: ("back", 1), 6: ("back", 0), 7: ("back", 1)}
EARLY_BANK = {("gate", 2): ("turned", 1), ("picture", 2): ("gate", 0)}
LAST_TURNED = 6
VECTOR_UNITS = 2
LAP = 64
PAGE = 4 * T
ROW = 4 * HALF
PAIR = 8 * CHUNK
TABS_AT = 0
WS_AT = TABS_AT + T - LAP
ZV_AT = WS_AT + 3 * N - LAP
WV_AT = ZV_AT + 2 * N
V2ROWS_AT = WV_AT + PAGE - LAP
BIAS_AT = V2ROWS_AT + LAP
WROWS_AT = V2ROWS_AT + 2 * LAP
PAGE1_AT = V2ROWS_AT + J - LAP
PAGE2_AT = PAGE1_AT + PAGE
BOTH_AT = PAGE2_AT + PAGE - LAP
ROUNDED_AT = BOTH_AT + 2 * ROW
VS_AT = ROUNDED_AT + LAP
PAGE3_AT = ROUNDED_AT + ROW - LAP
WIDE_AT = BOTH_AT + ROW - LAP
PAIR0_AT = PAGE3_AT + PAGE
TEXT_AT = PAIR0_AT + PAIR - LAP
PAIR1_AT = TEXT_AT + ROW - LAP
PAIR2_AT = PAIR1_AT + PAIR
WEIGHED_AT = PAIR2_AT + PAIR - LAP
PAIR3_AT = WEIGHED_AT + ROW - LAP


def tile_list_gmu_relu_scatP_kernel(
    tc, tab_words, tab_scales, tab2_words, tab2_scales, zv_words, zv_scales, zt_words, zt_scales,
    b, wv, wt_words, wt_scales, wgo, offs, offs2, out_0, out_1, out_2,
):
    nc = tc.nc
    with ExitStack() as ctx:
        keep = ctx.enter_context(tc.tile_pool(name="keep", bufs=1))
        placed = ctx.enter_context(tc.tile_pool(name="placed", bufs=1))
        ring = ctx.enter_context(tc.tile_pool(name="ring", bufs=4))
        psum = ctx.enter_context(tc.psum_pool(name="psum", bufs=1))

        def held(name, shape, dtype, tag=""):
            return keep.tile(shape, dtype, name=name, tag=tag or name, align_bytes=64)

        def at_byte(name, shape, dtype, offset):
            return placed.tile(shape, dtype, name=name, tag=name, align_bytes=64, offset=offset)

        def bank(role, u):
            role, n = EARLY_BANK.get((role, u), (role, u % 2))
            return psum.tile([P, HALF], F32, name="bank", tag="%s%d" % (role, n))

        list1 = held("list1", [P, J // 16], U16)
        list2 = held("list2", [P, J // 16], U16)
        tab_w = held("tab_w", [P, T], I32)
        tab2_s = held("tab2_s", [P, T], U8)
        tab2_w = held("tab2_w", [P, T], I32)
        ws_raw = at_byte("ws_raw", [P, 3 * N], U8, WS_AT)
        raw = {name: held(name + "_raw", [P, passes, 2 * N], U8) for name, passes in (("wt", 2), ("zt", 2))}
        ident = held("ident", [P, P], F32)
        warm = held("warm", [P, 8], F32)

        nc.gpsimd.memset(ws_raw[:, 2 * N :].bitcast(I32), 0)
        nc.vector.memset(warm[:], 0.0)
        for rows32 in (slice(32, 64), slice(64, 128)):
            nc.gpsimd.memset(tab2_s[rows32, :].bitcast(I32), 0)
        for rows32 in (slice(32, 64), slice(64, 128)):
            nc.vector.memset(ws_raw[rows32, : 2 * N].bitcast(I32), 0)
        make_identity(nc, ident[:])

        words_in = {"zt": zt_words, "wt": wt_words, "zv": zv_words}

        def load_words(name):
            nc.sync.dma_start(raw[name][:].bitcast(I32), words_in[name].rearrange("a p n -> p a n").bitcast(I32))

        nc.sync.dma_start(list2[:], offs2)
        nc.sync.dma_start(tab2_s[0:32, :].bitcast(I32), tab2_scales.rearrange("a q t -> q a t").bitcast(I32))
        nc.scalar.dma_start(ws_raw[0:32, 0:N].bitcast(I32), zt_scales.rearrange("a q n -> q a n").bitcast(I32))
        nc.scalar.dma_start(ws_raw[0:32, N : 2 * N].bitcast(I32), wt_scales.rearrange("a q n -> q a n").bitcast(I32))
        nc.scalar.dma_start(ws_raw[0:32:2, 2 * N :].bitcast(I32), zv_scales[0].bitcast(I32))
        nc.sync.dma_start(list1[:], offs)
        nc.sync.dma_start(tab2_w[:], tab2_words[0].rearrange("p t i -> p (t i)").bitcast(I32))
        load_words("zt")
        load_words("wt")
        nc.sync.dma_start(tab_w[:], tab_words[0].rearrange("p t i -> p (t i)").bitcast(I32))

        nc.scalar.activation(warm[:, 0:1], warm[:, 1:2], ACT.Sigmoid)

        def entries(first, count):
            return slice(first // 16, (first + count) // 16)

        def half_cols(h):
            return slice(h * HALF, (h + 1) * HALF)

        def block(k):
            return slice(k * P, (k + 1) * P)

        page = {}

        def clear_page(t, offset):
            page[t] = at_byte("page%d" % t, [P, T], F32, offset)
            nc.gpsimd.memset(page[t][:], 0.0)

        page[0] = held("page0", [P, T], F32)
        nc.gpsimd.memset(page[0][:], 0.0)
        rows = held("rows", [P, J + 3 * N], U8)
        v2_rows = at_byte("v2_rows", [P, J], U8, V2ROWS_AT)
        nc.vector.tensor_copy(v2_rows[:], tab2_s[:].indirect(list2[:]))
        nc.vector.tensor_copy(
            rows[:, J:].rearrange("p (a t o i) -> p o a t i", a=3, t=PACK, i=16),
            ws_raw[:].rearrange("p (a o i t) -> p o a t i", a=3, t=PACK, i=16),
        )
        raw["zv"] = at_byte("zv_raw", [P, 1, 2 * N], U8, ZV_AT)
        load_words("zv")
        nc.vector.tensor_copy(rows[:, :J].bitcast(I32), v2_rows[:].bitcast(I32))
        planes = held("planes", [P, 2, J + 3 * N], U8)
        for q in (0, 2, 1, 3):
            nc.sync.dma_start(planes[32 * q : 32 * q + 4, :, :].bitcast(I32), rows[8 * q : 8 * q + 8, :].bitcast(I32))
        wv_raw = at_byte("wv_raw", [P, PACK, N], F32, WV_AT)
        nc.sync.dma_start(wv_raw[:], wv.rearrange("(p i) n -> p i n", i=PACK))
        bias = at_byte("bias", [P, PACK], F32, BIAS_AT)
        nc.sync.dma_start(bias[:], b.rearrange("(p t) -> p t", t=PACK))
        tab_s = at_byte("tab_s", [P, T], U8, TABS_AT)
        nc.vector.memset(tab_s[:].bitcast(I32), 0)
        for r in range(4):
            nc.sync.dma_start(tab_s[r:P:32, :].bitcast(I32), tab_scales[0, r:16:4, :].bitcast(I32))
        w_rows = at_byte("w_rows", [P, P], F32, WROWS_AT)
        nc.gpsimd.memset(w_rows[:], 0.0)
        nc.sync.dma_start(w_rows[0 : J // P, :], wgo[0].rearrange("(c p) -> c p", p=P))

        clear_page(1, PAGE1_AT)
        dealt = {}

        def deal(name):
            passes = raw[name].shape[1]
            dealt[name] = held(name + "_dealt", [P, passes, 2 * N], U8)
            for a in range(passes):
                nc.scalar.copy(
                    dealt[name][:, a, :].bitcast(U16).rearrange("p (t o i) -> p o t i", t=PACK, i=8),
                    raw[name][:, a, :].bitcast(U16).rearrange("p (o i t) -> p o t i", t=PACK, i=8),
                )

        deal("zt")
        deal("wt")
        deal("zv")

        v2_w, v_w, wv_w, wv_s = {}, {}, {}, {}
        both = at_byte("both", [P, J], U32, BOTH_AT)
        for h in range(HALVES):
            nc.vector.tensor_copy(both[:, half_cols(h)], tab2_w[:].bitcast(U32).indirect(list2[:, entries(h * HALF, HALF)]))

        def part_text(h):
            v2_w[h] = held("v2_w%d" % h, [P, 2, 2 * HALF], U8)
            nc.vector.tensor_copy(
                v2_w[h][:].bitcast(U16).rearrange("p d (o i) -> p o d i", i=8),
                both[:, half_cols(h)].bitcast(U16).rearrange("p (o i d) -> p o d i", d=2, i=8),
            )

        for h in range(HALVES):
            part_text(h)
        clear_page(2, PAGE2_AT)
        for h in range(HALVES):
            v_w[h] = held("v_w%d" % h, [P, HALF], U32)
            nc.vector.tensor_copy(v_w[h][:], tab_w[:].bitcast(U32).indirect(list1[:, entries(h * HALF, HALF)]))

        def quantise_wv(g, rounded, copy):
            copy(
                rounded[:].rearrange("p (t m i) -> p m t i", t=2, i=PACK),
                wv_raw[:].rearrange("p i (m t) -> p m t i", t=PACK)[:, :, 2 * g : 2 * g + 2, :],
            )
            words = held("wv_w%d" % g, [P, 2 * P], U32)
            scales = held("wv_s%d" % g, [P, 2 * P], U8)
            nc.vector.quantize_mx(out=words[:].bitcast(FP8X4), scales=scales[:], in_=rounded[:])
            for n in range(2):
                wv_w[2 * g + n], wv_s[2 * g + n] = words[:, block(n)], scales[:, block(n)]

        quantise_wv(0, held("wv_bf0", [P, 2 * P * PACK], BF16), nc.vector.tensor_copy)
        quantise_wv(1, at_byte("wv_bf1", [P, 2 * P * PACK], BF16, ROUNDED_AT), nc.scalar.copy)
        clear_page(3, PAGE3_AT)
        v_s = {}
        for h in range(HALVES):
            v_s[h] = at_byte("v_s%d" % h, [P, HALF], U8, VS_AT + h * HALF)
            nc.vector.tensor_copy(v_s[h][:], tab_s[:].indirect(list1[:, entries(h * HALF, HALF)]))

        scale_run = {"zt": 0, "wt": 1, "zv": 2}

        def w4_pass(name, a, t):
            first = J + scale_run[name] * N + P * t
            return dealt[name][:, a, 2 * P * t : 2 * P * (t + 1)].bitcast(FP4X4), planes[:, a, first : first + P]

        def wv_pass(t):
            return wv_w[t].bitcast(FP8X4), wv_s[t]

        def v_pass(first, count):
            cols = slice(first % HALF, first % HALF + count)
            return v_w[first // HALF][:, cols].bitcast(FP8X4), v_s[first // HALF][:, cols]

        def v2_pass(first, count, d):
            at = first % HALF
            return v2_w[first // HALF][:, d, 2 * at : 2 * (at + count)].bitcast(FP4X4), planes[:, d, first : first + count]

        def mm(out, left, right, start, stop):
            nc.tensor.matmul_mx(out=out, lhsT=left[0], lhsT_scale=left[1], rhs=right[0], rhs_scale=right[1], start=start, stop=stop)

        last = len(UNITS) - 1
        out_rows = out_0.rearrange("(p t) c -> t p c", t=PACK)
        text, gate, picture, z = {}, {}, {}, {}
        last_page = held("last_page", [P, J], F32)

        def text_passes(u, role, n):
            t, first, count = UNITS[u]
            ht = bank(role, n)[:, :count]
            mm(ht, w4_pass("wt", 0, t), v2_pass(first, count, 0), True, False)
            mm(ht, w4_pass("wt", 1, t), v2_pass(first, count, 1), False, True)
            return ht

        def text_sum(u, role, n):
            text[u] = at_byte("text_last", [P, HALF], F32, TEXT_AT) if u == last else held("text%d" % u, [P, HALF], F32)
            nc.scalar.activation(text[u][:], text_passes(u, role, n), ACT.Relu)

        def open_gate(u):
            t, first, count = UNITS[u]
            z[u] = bank("gate", u)[:, :count]
            mm(z[u], w4_pass("zt", 0, t), v2_pass(first, count, 0), True, False)
            mm(z[u], w4_pass("zt", 1, t), v2_pass(first, count, 1), False, False)

        def close_gate(u):
            t, first, count = UNITS[u]
            gate[u] = ring.tile([P, count], F32, name="gate")
            mm(z[u], w4_pass("zv", 0, t), v_pass(first, count), False, True)
            nc.scalar.activation(gate[u][:], z[u], ACT.Sigmoid, bias=bias[:, t : t + 1])

        def picture_sum(u):
            t, first, count = UNITS[u]
            picture[u] = ring.tile([P, count], F32, name="picture")
            total = bank("picture", u)[:, :count]
            mm(total, wv_pass(t), v_pass(first, count), True, True)
            nc.scalar.activation(picture[u][:], total, ACT.Relu)

        def mix(u):
            difference = held("difference", [P, HALF], F32, tag="share0") if u == VECTOR_UNITS else picture[u]
            nc.gpsimd.tensor_tensor(difference[:], picture[u][:], text[u][:], ALU.subtract)
            nc.gpsimd.tensor_tensor(picture[u][:], difference[:], gate[u][:], ALU.mult)

        def place(u, result):
            t, first, count = UNITS[u]
            nc.vector.tensor_copy(page[t][:].indirect(list1[:, entries(first, count)]), result[:])
            if first + count == J:
                nc.sync.dma_start(out_rows[t], page[t][:])

        def finish(u):
            t, first, count = UNITS[u]
            if u > LAST_TURNED:
                nc.gpsimd.tensor_tensor(picture[u][:], picture[u][:], text[u][:], ALU.add)
                nc.gpsimd.tensor_tensor(last_page[:, HALF:], picture[u][:], w_wide[:], ALU.mult)
                return
            blocks = range(count // P)
            turned = bank("turned", u)
            for k in blocks:
                nc.tensor.matmul(turned[:, block(k)], text[u][:, block(k)], ident[:], start=True, stop=False, is_transpose=True)
                nc.tensor.matmul(turned[:, block(k)], picture[u][:, block(k)], ident[:], start=False, stop=True, is_transpose=True)
            weighed = at_byte("weighed_last", [P, count], F32, WEIGHED_AT) if u == LAST_TURNED else ring.tile([P, count], F32, name="weighed")
            for k in blocks:
                col = first // P + k
                nc.scalar.activation(weighed[:, block(k)], turned[:, block(k)], ACT.Copy, scale=w_cols[:, col : col + 1])
            back = bank("back", u)
            for k in blocks:
                nc.tensor.transpose(back[:, block(k)], weighed[:, block(k)], ident[:])
            if u == last - 1:
                nc.scalar.copy(last_page[:, :HALF], back[:, :count])
                return
            result = held("result%d" % u, [P, count], F32)
            nc.scalar.copy(result[:], back[:, :count])
            place(u, result)

        ht, hv, rest = {}, {}, {}
        for u in range(VECTOR_UNITS):
            open_gate(u)
            ht[u] = text_passes(u, "back", u)
        for u in range(VECTOR_UNITS):
            close_gate(u)
            hv[u] = bank("picture", u)
            mm(hv[u][:], wv_pass(u), v_pass(0, HALF), True, True)
            rest[u] = held("rest%d" % u, [P, HALF], F32)
            if u == 0:
                nc.scalar.activation(rest[u][:], gate[u][:], ACT.Copy, bias=1.0, scale=-1.0)
            else:
                nc.gpsimd.tensor_scalar(rest[u][:], gate[u][:], -1.0, 1.0, ALU.mult, ALU.add)
        text_sum(VECTOR_UNITS, "turned", 1)
        w_bank = bank("turned", 1)
        nc.tensor.transpose(w_bank[:, 0:P], w_rows[:], ident[:])
        w_cols = held("w_cols", [P, J // P], F32)
        nc.scalar.copy(w_cols[:], w_bank[:, 0 : J // P])
        w_first = bank("turned", 0)
        for k in range(HALF // P):
            nc.tensor.transpose(w_first[:, block(k)], w_cols[:, k : k + 1].to_broadcast([P, P]), ident[:])
        def share(u):
            text[u] = held("share%d" % u, [P, HALF], F32)
            nc.vector.scalar_tensor_tensor(text[u][:], ht[u], 0.0, rest[u][:], ALU.max, ALU.mult)

        def product(u):
            picture[u] = ring.tile([P, HALF], F32, name="picture")
            nc.vector.scalar_tensor_tensor(picture[u][:], hv[u][:], 0.0, gate[u][:], ALU.max, ALU.mult)

        product(0)
        share(0)
        product(1)
        nc.vector.tensor_tensor(picture[0][:], picture[0][:], text[0][:], ALU.add)
        share(1)
        first_result = held("result0", [P, HALF], F32)
        nc.vector.tensor_tensor(first_result[:], picture[0][:], w_first[:], ALU.mult)
        w_wide = at_byte("w_wide", [P, HALF], F32, WIDE_AT)
        nc.sync.dma_start(w_wide[:], wgo[:, HALF:])


        def prepare(u):
            if u in TEXT_BANK:
                text_sum(u, *TEXT_BANK[u])
            open_gate(u)
            picture_sum(u)
            close_gate(u)
            mix(u)
            if u == last:
                finish(last)

        prepare(2)
        place(0, first_result)
        finish(1)
        prepare(3)
        prepare(4)
        for u in range(2, last):
            finish(u)
            if u + 3 <= last:
                prepare(u + 3)
        nc.vector.tensor_copy(page[PACK - 1][:].indirect(list1[:]), last_page[:])
        nc.sync.dma_start(out_rows[PACK - 1], page[PACK - 1][:])

        pairs = [at_byte("pairs%d" % c, [P, 4 * CHUNK], BF16, (PAIR2_AT, PAIR3_AT, PAIR0_AT, PAIR1_AT)[c]) for c in range(CHUNKS)]

        def round_page(t, c):
            rows_f32 = page[t][:, c * CHUNK : (c + 1) * CHUNK]
            words = pairs[c][:, t // 2 * 2 * CHUNK : (t // 2 + 1) * 2 * CHUNK].rearrange("p (c i) -> p c i", i=2)
            twice = rows_f32.unsqueeze(2).to_broadcast([P, CHUNK, 2])
            if t == PACK - 2:
                out, source = words, twice
            else:
                out, source = words[:, :, t % 2], rows_f32
            if c < VECTOR_CHUNKS or t == PACK - 1:
                nc.scalar.copy(out, source)
            else:
                nc.gpsimd.tensor_scalar(out, source, 1.0, -0.0, ALU.mult, ALU.add)

        spare = ("tab2_w", "text3", "text2", "zt_raw", "wt_raw")
        grouped = {}

        def weave(n):
            c, first, width = PIECES[n]
            grouped[n] = held("grouped%d" % n, [P, width, PACK], BF16, tag=spare[n])
            woven = grouped[n][:].rearrange("p c i -> p (c i)").bitcast(U32).rearrange("p (c a) -> p c a", a=2)
            nc.scalar.copy(woven, pairs[c][:].bitcast(U32).rearrange("p (a c) -> p c a", a=2)[:, first : first + width, :])

        for t in range(PACK - 1):
            for c in range(CHUNKS):
                round_page(t, c)
        for n in range(VECTOR_CHUNKS):
            weave(n)
        for c in range(VECTOR_CHUNKS):
            nc.vector.tensor_copy(grouped[c][:, :, PACK - 1], page[PACK - 1][:, c * CHUNK : (c + 1) * CHUNK])
        round_page(PACK - 1, 2)
        weave(2)
        round_page(PACK - 1, 3)
        weave(3)
        weave(4)

        y_s = held("y_s", [P, T], U8)
        y_w = held("y_w", [P, T], I32)
        out_words = out_1[0].rearrange("p c i -> p (c i)").bitcast(I32)
        for n, (c, first, width) in enumerate(PIECES):
            cols = slice(c * CHUNK + first, c * CHUNK + first + width)
            nc.vector.quantize_mx(out=y_w[:, cols].bitcast(FP8X4), scales=y_s[:, cols], in_=grouped[n][:].rearrange("p c i -> p (c i)"))
            nc.sync.dma_start(out_words[:, cols], y_w[:, cols])
        for r in range(4):
            nc.scalar.dma_start(out_2[0, r:16:4, :].bitcast(I32), y_s[r:P:32, :].bitcast(I32))
